import numpy as np
import ml_dtypes


def mxq(x, axis, fmt="e4m3"):
    dtype, down = {"e4m3": (ml_dtypes.float8_e4m3fn, 7), "e5m2": (ml_dtypes.float8_e5m2, 14)}[fmt]
    v = np.moveaxis(np.asarray(x, np.float32).astype(ml_dtypes.bfloat16).astype(np.float64), axis, -1)
    blocks = v.reshape(v.shape[:-1] + (-1, 32))
    amax = np.abs(blocks).max(-1, keepdims=True)
    byte = np.maximum(np.where(amax > 0, np.frexp(amax)[1] - 1 + 127, 0) - down, 1)
    scale = np.exp2(byte - 127.0)
    codes = (blocks / scale).astype(np.float32).astype(dtype).astype(np.float64)
    return np.moveaxis((codes * scale).reshape(v.shape), -1, axis)


WIDE = False


def mx_kscale(k):
    if not WIDE:
        return np.ones(k)
    levels = np.array([18, -18])
    if k % 512:
        return np.exp2(np.random.permutation(np.resize(levels, k // 32))).repeat(32)
    a = np.empty((k // 512, 16))
    for p in range(k // 512):
        a[p, :8] = np.random.permutation(np.resize(levels, 8))
        for g in range(8):
            far = levels[np.abs(levels - a[p, g]) >= 10]
            a[p, g + 8] = far[np.random.randint(len(far))]
    return np.exp2(a.ravel()).repeat(32)


def f64(x):
    return np.asarray(x).astype(np.float64)


def striped(idx):
    return np.tile(np.asarray(idx).reshape(-1, 16).T, (8, 1)).astype(np.uint16)


def unstriped(offs):
    return offs[:16].T.reshape(-1).astype(np.int64)


B, N, T, D, DV = 2, 512, 2048, 512, 1024


def setup_inputs():
    n = np.random.standard_normal
    idx = np.random.permutation(T)[:B * N]
    v = mx_kscale(DV)[:, None]
    coarse = lambda x: x.astype(np.float32).astype(ml_dtypes.bfloat16).astype(np.float64)
    r = np.random.randint(8, 33, T) / 16.0
    return {
        "dyT": (coarse(n((DV, T))) * v).astype(np.float32),
        "hT": (np.random.randint(-15, 16, (DV, T)) / 16.0).astype(np.float32),
        "ts": np.tile(r, (128, 1)).astype(np.float32),
        "wm": (n((B, DV, D)) / np.sqrt(DV) / v).astype(np.float32),
        "offs": striped(idx),
    }


def reference(dyT, hT, ts, wm, offs):
    idx = unstriped(offs)
    pick = lambda x: x[:, idx].reshape(x.shape[0], B, N).transpose(1, 0, 2)
    h = pick(f64(hT))
    dz = pick(f64(ts))[:, :1, :] * pick(f64(dyT)) * (1.0 - h * h)
    dx = mxq(f64(wm), 1, "e4m3").transpose(0, 2, 1) @ mxq(dz, 1, "e5m2")
    gx = np.zeros((D, T))
    gx[:, idx] = dx.transpose(1, 0, 2).reshape(D, B * N)
    return gx

@@ -1,0 +1,209 @@
+from contextlib import ExitStack
+
+import concourse.mybir as mybir
+
+EXPERTS, SLOTS, TOKENS, D_IN, D_OUT = 2, 512, 2048, 512, 1024
+FLOPS = 2 * EXPERTS * SLOTS * D_IN * D_OUT
+
+F32 = mybir.dt.float32
+BF16 = mybir.dt.bfloat16
+U32 = mybir.dt.uint32
+U16 = mybir.dt.uint16
+U8 = mybir.dt.uint8
+E4M3 = mybir.dt.float8_e4m3fn_x4
+E5M2 = mybir.dt.float8_e5m2_x4
+MULT = mybir.AluOpType.mult
+SUB = mybir.AluOpType.subtract
+COPY = mybir.ActivationFunctionType.Copy
+SQUARE = mybir.ActivationFunctionType.Square
+
+P = 128
+PACK = 4
+K_PASS = P * PACK
+PASSES = D_OUT // K_PASS
+PLANES = PASSES * PACK
+LISTED = EXPERTS * SLOTS
+LIST_COLS = SLOTS // 16
+W_COLS = 256
+RUN = 4
+
+
+def tile_attend_gex_tnh_x_kernel(tc, dyT, hT, ts, wm, offs, out):
+    nc = tc.nc
+
+    with ExitStack() as ctx:
+        keep = ctx.enter_context(tc.tile_pool(name="keep", bufs=1))
+        ring = ctx.enter_context(tc.tile_pool(name="ring", bufs=2))
+        psum = ctx.enter_context(tc.psum_pool(name="psum", bufs=1))
+
+        offsets = keep.tile([P, LISTED // 16], U16, name="offsets")
+        nc.sync.dma_start(offsets[:], offs)
+
+        def slots_of(e):
+            return offsets[:, e * LIST_COLS : (e + 1) * LIST_COLS]
+
+        def plane_rows(x, j):
+            g, t = divmod(j, PACK)
+            return x[g * K_PASS : (g + 1) * K_PASS, :].rearrange("(p t) c -> p t c", t=PACK)[:, t, :]
+
+        windows = [keep.tile([P, TOKENS], F32, name="out%d" % m) for m in range(D_IN // P)]
+        for window in windows:
+            nc.gpsimd.memset(window[:], 0.0)
+
+        factor = {}
+        dy = {}
+        ts_listed = keep.tile([P, LISTED], F32, name="ts_listed")
+
+        def gather_h(j):
+            h = ring.tile([P, TOKENS], F32, name="h", bufs=4)
+            nc.sync.dma_start(h[:], plane_rows(hT, j))
+            hh = ring.tile([P, LISTED], F32, name="hh", bufs=3)
+            nc.vector.tensor_copy(hh[:], h[:].indirect(offsets[:]))
+            nc.scalar.activation(hh[:], hh[:], SQUARE)
+            factor[j] = hh
+
+        def gather_ts():
+            t = keep.tile([P, TOKENS], F32, name="ts_all")
+            nc.sync.dma_start(t[:], ts)
+            nc.vector.tensor_copy(ts_listed[:], t[:].indirect(offsets[:]))
+
+        def weigh(j):
+            w = ring.tile([P, LISTED], F32, name="w", bufs=4)
+            nc.vector.scalar_tensor_tensor(w[:], factor[j][:], 1.0, ts_listed[:], SUB, MULT)
+            factor[j] = w
+
+        def load_dy(j):
+            dy[j] = ring.tile([P, TOKENS], F32, name="dy", bufs=4)
+            nc.sync.dma_start(dy[j][:], plane_rows(dyT, j))
+
+        dz0 = keep.tile([P, PACK, LISTED], F32, name="dz0")
+        dz1 = [keep.tile([P, PACK, SLOTS], F32, name="dz1_%d" % e) for e in range(EXPERTS)]
+
+        def gather_dy_both(j):
+            nc.vector.tensor_tensor(dz0[:, j, :], dy[j][:].indirect(offsets[:]), factor[j][:], MULT)
+
+        def gather_dy(j, e):
+            nc.vector.tensor_tensor(
+                dz1[e][:, j - PACK, :],
+                dy[j][:].indirect(slots_of(e)),
+                factor[j][:, e * SLOTS : (e + 1) * SLOTS],
+                MULT,
+            )
+
+        dz_bf = {}
+        dz_codes = {}
+        dz_scales = {}
+
+        def interleave_dz(g, e):
+            src = dz0[:, :, e * SLOTS : (e + 1) * SLOTS] if g == 0 else dz1[e][:]
+            dz_bf[g, e] = ring.tile([P, SLOTS, PACK], BF16, name="dz_bf", align_bytes=64)
+            nc.scalar.activation(
+                dz_bf[g, e][:].rearrange("p (c i) t -> p c t i", i=RUN),
+                src.rearrange("p t (c i) -> p c t i", i=RUN),
+                COPY,
+                scale=-1.0,
+            )
+
+        def quantize_dz(g, e):
+            dz_codes[g, e] = keep.tile([P, SLOTS], U32, name="dz_codes%d%d" % (g, e), align_bytes=64)
+            dz_scales[g, e] = keep.tile([P, SLOTS], U8, name="dz_scales%d%d" % (g, e), align_bytes=64)
+            nc.vector.quantize_mx(
+                out=dz_codes[g, e][:].bitcast(E5M2),
+                scales=dz_scales[g, e][:],
+                in_=dz_bf[g, e][:].rearrange("p c t -> p (c t)"),
+            )
+
+        w_raw = {}
+        w_bf = {}
+        w_codes = {}
+        w_scales = {}
+
+        def load_w(e, half):
+            w_raw[e, half] = ring.tile([P, PASSES, PACK, W_COLS], F32, name="w_raw")
+            rows = wm[e].rearrange("(g p t) d -> p g t d", g=PASSES, t=PACK)
+            for g in range(PASSES):
+                nc.sync.dma_start(w_raw[e, half][:, g, :, :], rows[:, g, :, half * W_COLS : (half + 1) * W_COLS])
+
+        def interleave_w(e, half):
+            w_bf[e, half] = ring.tile([P, PASSES, W_COLS, PACK], BF16, name="w_bf", align_bytes=64)
+            for g in range(PASSES):
+                nc.scalar.copy(
+                    w_bf[e, half][:, g, :, :].rearrange("p (c i) t -> p c t i", i=RUN),
+                    w_raw[e, half][:, g, :, :].rearrange("p t (c i) -> p c t i", i=RUN),
+                )
+
+        def quantize_w(e, half):
+            w_codes[e, half] = keep.tile([P, PASSES * W_COLS], U32, name="w_codes%d%d" % (e, half), align_bytes=64)
+            w_scales[e, half] = keep.tile([P, PASSES * W_COLS], U8, name="w_scales%d%d" % (e, half), align_bytes=64)
+            nc.vector.quantize_mx(
+                out=w_codes[e, half][:].bitcast(E4M3),
+                scales=w_scales[e, half][:],
+                in_=w_bf[e, half][:].rearrange("p g c t -> p (g c t)"),
+            )
+
+        def multiply_and_scatter(e, m):
+            half, q = divmod(m * P, W_COLS)
+            acc = psum.tile([P, SLOTS], F32, name="acc%d%d" % (e, m))
+            for g in range(PASSES):
+                cols = slice(g * W_COLS + q, g * W_COLS + q + P)
+                nc.tensor.matmul_mx(
+                    out=acc[:],
+                    lhsT=w_codes[e, half][:, cols].bitcast(E4M3),
+                    lhsT_scale=w_scales[e, half][:, cols],
+                    rhs=dz_codes[g, e][:].bitcast(E5M2),
+                    rhs_scale=dz_scales[g, e][:],
+                    start=(g == 0),
+                    stop=(g == PASSES - 1),
+                )
+            dx = ring.tile([P, SLOTS], F32, name="dx", bufs=4)
+            nc.scalar.copy(dx[:], acc[:])
+            nc.vector.tensor_copy(windows[m][:].indirect(slots_of(e)), dx[:])
+
+        def store(m):
+            nc.sync.dma_start(out[m * P : (m + 1) * P, :], windows[m][:])
+
+        gather_h(0)
+        gather_h(1)
+        gather_ts()
+        for j in range(PLANES):
+            if j + 2 < PLANES:
+                gather_h(j + 2)
+            weigh(j)
+            if j == PLANES - 2:
+                load_w(0, 0)
+                interleave_w(0, 0)
+                quantize_w(0, 0)
+            load_dy(j)
+            if j < PACK:
+                gather_dy_both(j)
+            else:
+                gather_dy(j, 0)
+            if j == PACK:
+                gather_dy(j, 1)
+                for e in range(EXPERTS):
+                    interleave_dz(0, e)
+                    quantize_dz(0, e)
+        interleave_dz(1, 0)
+        quantize_dz(1, 0)
+        for j in range(PACK + 1, PLANES):
+            gather_dy(j, 1)
+        interleave_dz(1, 1)
+        load_w(1, 0)
+        interleave_w(1, 0)
+        multiply_and_scatter(0, 0)
+        quantize_dz(1, 1)
+        quantize_w(1, 0)
+        multiply_and_scatter(0, 1)
+        load_w(0, 1)
+        load_w(1, 1)
+        multiply_and_scatter(1, 0)
+        store(0)
+        for e in range(EXPERTS):
+            interleave_w(e, 1)
+            quantize_w(e, 1)
+        multiply_and_scatter(1, 1)
+        store(1)
+        for m in (2, 3):
+            for e in range(EXPERTS):
+                multiply_and_scatter(e, m)
+            store(m)

@@ -26,6 +26,9 @@ LISTED = EXPERTS * SLOTS
 LIST_COLS = SLOTS // 16
 W_COLS = 256
 RUN = 4
+LOAD_BUFS = 9
+WBF = 2
+ON_GPSIMD = 6
 
 
 def tile_attend_gex_tnh_x_kernel(tc, dyT, hT, ts, wm, offs, out):
@@ -34,6 +37,8 @@ def tile_attend_gex_tnh_x_kernel(tc, dyT, hT, ts, wm, offs, out):
     with ExitStack() as ctx:
         keep = ctx.enter_context(tc.tile_pool(name="keep", bufs=1))
         ring = ctx.enter_context(tc.tile_pool(name="ring", bufs=2))
+        early = ctx.enter_context(tc.tile_pool(name="early", bufs=1))
+        later = ctx.enter_context(tc.tile_pool(name="later", bufs=1))
         psum = ctx.enter_context(tc.psum_pool(name="psum", bufs=1))
 
         offsets = keep.tile([P, LISTED // 16], U16, name="offsets")
@@ -54,30 +59,50 @@ def tile_attend_gex_tnh_x_kernel(tc, dyT, hT, ts, wm, offs, out):
         dy = {}
         ts_listed = keep.tile([P, LISTED], F32, name="ts_listed")
 
+        ts_negated = keep.tile([P, LISTED], F32, name="ts_negated")
+
         def gather_h(j):
-            h = ring.tile([P, TOKENS], F32, name="h", bufs=4)
+            h = ring.tile([P, TOKENS], F32, name="h", tag="load", bufs=LOAD_BUFS)
             nc.sync.dma_start(h[:], plane_rows(hT, j))
-            hh = ring.tile([P, LISTED], F32, name="hh", bufs=3)
+            hh = ring.tile([P, LISTED], F32, name="hh", bufs=4)
             nc.vector.tensor_copy(hh[:], h[:].indirect(offsets[:]))
             nc.scalar.activation(hh[:], hh[:], SQUARE)
+            if j < ON_GPSIMD:
+                nc.scalar.activation(hh[:], hh[:], COPY, bias=1.0, scale=-1.0)
             factor[j] = hh
 
         def gather_ts():
-            t = keep.tile([P, TOKENS], F32, name="ts_all")
+            t = ring.tile([P, TOKENS], F32, name="ts_all", tag="load", bufs=LOAD_BUFS)
             nc.sync.dma_start(t[:], ts)
             nc.vector.tensor_copy(ts_listed[:], t[:].indirect(offsets[:]))
+            nc.scalar.activation(ts_negated[:], ts_listed[:], COPY, scale=-1.0)
 
         def weigh(j):
-            w = ring.tile([P, LISTED], F32, name="w", bufs=4)
-            nc.vector.scalar_tensor_tensor(w[:], factor[j][:], 1.0, ts_listed[:], SUB, MULT)
+            w = ring.tile([P, LISTED], F32, name="w", bufs=3)
+            nc.gpsimd.tensor_tensor(w[:], factor[j][:], ts_listed[:], MULT)
             factor[j] = w
 
+        late = {}
+        dz1 = {}
+
+        def weigh_late(j, e):
+            if e == 0:
+                tile = early.tile([P, SLOTS], F32, name="late%d" % j, offset=(j - 6) * 11776)
+                late[j, e] = tile[:]
+            else:
+                late[j, e] = dz1[e][:, j - 2, :]
+            cols = slice(e * SLOTS, (e + 1) * SLOTS)
+            nc.vector.scalar_tensor_tensor(late[j, e], factor[j][:, cols], 1.0, ts_negated[:, cols], SUB, MULT)
+
         def load_dy(j):
-            dy[j] = ring.tile([P, TOKENS], F32, name="dy", bufs=4)
+            if j in (2, 3):
+                dy[j] = early.tile([P, TOKENS], F32, name="dy%d" % j, offset=(j - 2) * 8192)
+            else:
+                dy[j] = ring.tile([P, TOKENS], F32, name="dy", tag="load", bufs=LOAD_BUFS)
             nc.sync.dma_start(dy[j][:], plane_rows(dyT, j))
 
         dz0 = keep.tile([P, PACK, LISTED], F32, name="dz0")
-        dz1 = [keep.tile([P, PACK, SLOTS], F32, name="dz1_%d" % e) for e in range(EXPERTS)]
+        dz1[0] = keep.tile([P, PACK, SLOTS], F32, name="dz1_first")
 
         def gather_dy_both(j):
             nc.vector.tensor_tensor(dz0[:, j, :], dy[j][:].indirect(offsets[:]), factor[j][:], MULT)
@@ -86,7 +111,7 @@ def tile_attend_gex_tnh_x_kernel(tc, dyT, hT, ts, wm, offs, out):
             nc.vector.tensor_tensor(
                 dz1[e][:, j - PACK, :],
                 dy[j][:].indirect(slots_of(e)),
-                factor[j][:, e * SLOTS : (e + 1) * SLOTS],
+                late[j, e] if (j, e) in late else factor[j][:, e * SLOTS : (e + 1) * SLOTS],
                 MULT,
             )
 
@@ -95,18 +120,23 @@ def tile_attend_gex_tnh_x_kernel(tc, dyT, hT, ts, wm, offs, out):
         dz_scales = {}
 
         def interleave_dz(g, e):
-            src = dz0[:, :, e * SLOTS : (e + 1) * SLOTS] if g == 0 else dz1[e][:]
-            dz_bf[g, e] = ring.tile([P, SLOTS, PACK], BF16, name="dz_bf", align_bytes=64)
+            src = dz0[:, :, e * SLOTS : (e + 1) * SLOTS] if g == 0 else dz1[e][:, 0:PACK, :]
+            if e == 0:
+                dz_bf[g, e] = keep.tile([P, SLOTS, PACK], BF16, name="dz_bf%d%d" % (g, e), align_bytes=64)
+            else:
+                dz_bf[g, e] = later.tile([P, SLOTS, PACK], BF16, name="dz_bf%d%d" % (g, e), align_bytes=64, offset=g * 4096)
             nc.scalar.activation(
                 dz_bf[g, e][:].rearrange("p (c i) t -> p c t i", i=RUN),
                 src.rearrange("p t (c i) -> p c t i", i=RUN),
                 COPY,
-                scale=-1.0,
             )
 
         def quantize_dz(g, e):
             dz_codes[g, e] = keep.tile([P, SLOTS], U32, name="dz_codes%d%d" % (g, e), align_bytes=64)
-            dz_scales[g, e] = keep.tile([P, SLOTS], U8, name="dz_scales%d%d" % (g, e), align_bytes=64)
+            if (g, e) == (0, 0):
+                dz_scales[g, e] = early.tile([P, SLOTS], U8, name="dz_scales00", align_bytes=64, offset=12288)
+            else:
+                dz_scales[g, e] = keep.tile([P, SLOTS], U8, name="dz_scales%d%d" % (g, e), align_bytes=64)
             nc.vector.quantize_mx(
                 out=dz_codes[g, e][:].bitcast(E5M2),
                 scales=dz_scales[g, e][:],
@@ -119,13 +149,13 @@ def tile_attend_gex_tnh_x_kernel(tc, dyT, hT, ts, wm, offs, out):
         w_scales = {}
 
         def load_w(e, half):
-            w_raw[e, half] = ring.tile([P, PASSES, PACK, W_COLS], F32, name="w_raw")
+            w_raw[e, half] = ring.tile([P, PASSES, PACK, W_COLS], F32, name="w_raw", tag="load", bufs=LOAD_BUFS)
             rows = wm[e].rearrange("(g p t) d -> p g t d", g=PASSES, t=PACK)
             for g in range(PASSES):
                 nc.sync.dma_start(w_raw[e, half][:, g, :, :], rows[:, g, :, half * W_COLS : (half + 1) * W_COLS])
 
         def interleave_w(e, half):
-            w_bf[e, half] = ring.tile([P, PASSES, W_COLS, PACK], BF16, name="w_bf", align_bytes=64)
+            w_bf[e, half] = ring.tile([P, PASSES, W_COLS, PACK], BF16, name="w_bf%d%d" % (e, half), tag="w_bf", bufs=WBF, align_bytes=64)
             for g in range(PASSES):
                 nc.scalar.copy(
                     w_bf[e, half][:, g, :, :].rearrange("p (c i) t -> p c t i", i=RUN),
@@ -133,15 +163,19 @@ def tile_attend_gex_tnh_x_kernel(tc, dyT, hT, ts, wm, offs, out):
                 )
 
         def quantize_w(e, half):
-            w_codes[e, half] = keep.tile([P, PASSES * W_COLS], U32, name="w_codes%d%d" % (e, half), align_bytes=64)
-            w_scales[e, half] = keep.tile([P, PASSES * W_COLS], U8, name="w_scales%d%d" % (e, half), align_bytes=64)
+            if (e, half) == (0, 0):
+                w_codes[e, half] = later.tile([P, PASSES * W_COLS], U32, name="w_codes00", align_bytes=64, offset=3072)
+                w_scales[e, half] = early.tile([P, PASSES * W_COLS], U8, name="w_scales00", align_bytes=64, offset=12800)
+            else:
+                w_codes[e, half] = keep.tile([P, PASSES * W_COLS], U32, name="w_codes%d%d" % (e, half), align_bytes=64)
+                w_scales[e, half] = keep.tile([P, PASSES * W_COLS], U8, name="w_scales%d%d" % (e, half), align_bytes=64)
             nc.vector.quantize_mx(
                 out=w_codes[e, half][:].bitcast(E4M3),
                 scales=w_scales[e, half][:],
                 in_=w_bf[e, half][:].rearrange("p g c t -> p (g c t)"),
             )
 
-        def multiply_and_scatter(e, m):
+        def multiply(e, m, dx):
             half, q = divmod(m * P, W_COLS)
             acc = psum.tile([P, SLOTS], F32, name="acc%d%d" % (e, m))
             for g in range(PASSES):
@@ -155,9 +189,16 @@ def tile_attend_gex_tnh_x_kernel(tc, dyT, hT, ts, wm, offs, out):
                     start=(g == 0),
                     stop=(g == PASSES - 1),
                 )
-            dx = ring.tile([P, SLOTS], F32, name="dx", bufs=4)
-            nc.scalar.copy(dx[:], acc[:])
-            nc.vector.tensor_copy(windows[m][:].indirect(slots_of(e)), dx[:])
+            nc.scalar.copy(dx, acc[:])
+
+        dx_one = {}
+
+        def multiply_one(e, m):
+            dx_one[e, m] = ring.tile([P, SLOTS], F32, name="dx", bufs=4)
+            multiply(e, m, dx_one[e, m][:])
+
+        def scatter_one(e, m):
+            nc.vector.tensor_copy(windows[m][:].indirect(slots_of(e)), dx_one[e, m][:])
 
         def store(m):
             nc.sync.dma_start(out[m * P : (m + 1) * P, :], windows[m][:])
@@ -165,45 +206,56 @@ def tile_attend_gex_tnh_x_kernel(tc, dyT, hT, ts, wm, offs, out):
         gather_h(0)
         gather_h(1)
         gather_ts()
-        for j in range(PLANES):
-            if j + 2 < PLANES:
-                gather_h(j + 2)
+        for j in range(3):
+            gather_h(j + 2)
             weigh(j)
-            if j == PLANES - 2:
-                load_w(0, 0)
-                interleave_w(0, 0)
-                quantize_w(0, 0)
+        for j in range(3):
             load_dy(j)
-            if j < PACK:
-                gather_dy_both(j)
-            else:
-                gather_dy(j, 0)
-            if j == PACK:
-                gather_dy(j, 1)
-                for e in range(EXPERTS):
-                    interleave_dz(0, e)
-                    quantize_dz(0, e)
+            gather_dy_both(j)
+            if j == 1:
+                load_w(0, 0)
+            gather_h(j + 5)
+            weigh(j + 3)
+        weigh_late(6, 0)
+        interleave_w(0, 0)
+        load_dy(3)
+        gather_dy_both(3)
+        weigh_late(7, 0)
+        interleave_dz(0, 0)
+        for j in range(PACK, PLANES):
+            load_dy(j)
+            gather_dy(j, 0)
         interleave_dz(1, 0)
-        quantize_dz(1, 0)
-        for j in range(PACK + 1, PLANES):
-            gather_dy(j, 1)
-        interleave_dz(1, 1)
-        load_w(1, 0)
-        interleave_w(1, 0)
-        multiply_and_scatter(0, 0)
-        quantize_dz(1, 1)
-        quantize_w(1, 0)
-        multiply_and_scatter(0, 1)
         load_w(0, 1)
+        load_w(1, 0)
         load_w(1, 1)
-        multiply_and_scatter(1, 0)
-        store(0)
-        for e in range(EXPERTS):
-            interleave_w(e, 1)
-            quantize_w(e, 1)
-        multiply_and_scatter(1, 1)
-        store(1)
-        for m in (2, 3):
-            for e in range(EXPERTS):
-                multiply_and_scatter(e, m)
+        quantize_dz(1, 0)
+        quantize_dz(0, 0)
+        quantize_w(0, 0)
+        multiply_one(0, 0)
+        multiply_one(0, 1)
+        interleave_w(0, 1)
+        dz1[1] = early.tile([P, PACK + 2, SLOTS], F32, name="second", offset=0)
+        gather_dy(4, 1)
+        gather_dy(5, 1)
+        weigh_late(6, 1)
+        weigh_late(7, 1)
+        gather_dy(6, 1)
+        gather_dy(7, 1)
+        quantize_w(0, 1)
+        interleave_dz(0, 1)
+        interleave_dz(1, 1)
+        quantize_dz(0, 1)
+        quantize_dz(1, 1)
+        multiply_one(0, 2)
+        interleave_w(1, 0)
+        quantize_w(1, 0)
+        multiply_one(0, 3)
+        interleave_w(1, 1)
+        quantize_w(1, 1)
+        for m in range(4):
+            scatter_one(0, m)
+        for m in range(4):
+            multiply_one(1, m)
+            scatter_one(1, m)
             store(m)

@@ -24,10 +24,10 @@ PASSES = D_OUT // K_PASS
 PLANES = PASSES * PACK
 LISTED = EXPERTS * SLOTS
 LIST_COLS = SLOTS // 16
-W_COLS = 256
+PIECES = {(0, 0): 1, (0, 1): 1, (0, 2): 2, (1, 0): 2, (1, 2): 2}
 RUN = 4
+W_PLACE = (0, 1, 0, 1, 2, 0)
 LOAD_BUFS = 9
-WBF = 2
 ON_GPSIMD = 6
 
 
@@ -39,6 +39,7 @@ def tile_attend_gex_tnh_x_kernel(tc, dyT, hT, ts, wm, offs, out):
         ring = ctx.enter_context(tc.tile_pool(name="ring", bufs=2))
         early = ctx.enter_context(tc.tile_pool(name="early", bufs=1))
         later = ctx.enter_context(tc.tile_pool(name="later", bufs=1))
+        places = ctx.enter_context(tc.tile_pool(name="places", bufs=1))
         psum = ctx.enter_context(tc.psum_pool(name="psum", bufs=1))
 
         offsets = keep.tile([P, LISTED // 16], U16, name="offsets")
@@ -78,7 +79,7 @@ def tile_attend_gex_tnh_x_kernel(tc, dyT, hT, ts, wm, offs, out):
             nc.scalar.activation(ts_negated[:], ts_listed[:], COPY, scale=-1.0)
 
         def weigh(j):
-            w = ring.tile([P, LISTED], F32, name="w", bufs=3)
+            w = places.tile([P, LISTED], F32, name="w%d" % j, offset=W_PLACE[j] * 4096)
             nc.gpsimd.tensor_tensor(w[:], factor[j][:], ts_listed[:], MULT)
             factor[j] = w
 
@@ -121,10 +122,10 @@ def tile_attend_gex_tnh_x_kernel(tc, dyT, hT, ts, wm, offs, out):
 
         def interleave_dz(g, e):
             src = dz0[:, :, e * SLOTS : (e + 1) * SLOTS] if g == 0 else dz1[e][:, 0:PACK, :]
-            if e == 0:
+            if (g, e) != (1, 1):
                 dz_bf[g, e] = keep.tile([P, SLOTS, PACK], BF16, name="dz_bf%d%d" % (g, e), align_bytes=64)
             else:
-                dz_bf[g, e] = later.tile([P, SLOTS, PACK], BF16, name="dz_bf%d%d" % (g, e), align_bytes=64, offset=g * 4096)
+                dz_bf[g, e] = later.tile([P, SLOTS, PACK], BF16, name="dz_bf%d%d" % (g, e), align_bytes=64, offset=0)
             nc.scalar.activation(
                 dz_bf[g, e][:].rearrange("p (c i) t -> p c t i", i=RUN),
                 src.rearrange("p t (c i) -> p c t i", i=RUN),
@@ -133,8 +134,8 @@ def tile_attend_gex_tnh_x_kernel(tc, dyT, hT, ts, wm, offs, out):
 
         def quantize_dz(g, e):
             dz_codes[g, e] = keep.tile([P, SLOTS], U32, name="dz_codes%d%d" % (g, e), align_bytes=64)
-            if (g, e) == (0, 0):
-                dz_scales[g, e] = early.tile([P, SLOTS], U8, name="dz_scales00", align_bytes=64, offset=12288)
+            if g == 0:
+                dz_scales[g, e] = early.tile([P, SLOTS], U8, name="dz_scales0%d" % e, align_bytes=64, offset=12288 + 512 * e)
             else:
                 dz_scales[g, e] = keep.tile([P, SLOTS], U8, name="dz_scales%d%d" % (g, e), align_bytes=64)
             nc.vector.quantize_mx(
@@ -148,42 +149,45 @@ def tile_attend_gex_tnh_x_kernel(tc, dyT, hT, ts, wm, offs, out):
         w_codes = {}
         w_scales = {}
 
-        def load_w(e, half):
-            w_raw[e, half] = ring.tile([P, PASSES, PACK, W_COLS], F32, name="w_raw", tag="load", bufs=LOAD_BUFS)
+        def load_w(e, m):
+            width = PIECES[e, m] * P
+            w_raw[e, m] = ring.tile([P, PASSES, PACK, width], F32, name="w_raw", tag="load", bufs=LOAD_BUFS)
             rows = wm[e].rearrange("(g p t) d -> p g t d", g=PASSES, t=PACK)
             for g in range(PASSES):
-                nc.sync.dma_start(w_raw[e, half][:, g, :, :], rows[:, g, :, half * W_COLS : (half + 1) * W_COLS])
+                nc.sync.dma_start(w_raw[e, m][:, g, :, :], rows[:, g, :, m * P : m * P + width])
 
-        def interleave_w(e, half):
-            w_bf[e, half] = ring.tile([P, PASSES, W_COLS, PACK], BF16, name="w_bf%d%d" % (e, half), tag="w_bf", bufs=WBF, align_bytes=64)
+        def interleave_w(e, m):
+            width = PIECES[e, m] * P
+            w_bf[e, m] = ring.tile([P, PASSES, width, PACK], BF16, name="w_bf%d%d" % (e, m), tag="w_bf", align_bytes=64)
             for g in range(PASSES):
                 nc.scalar.copy(
-                    w_bf[e, half][:, g, :, :].rearrange("p (c i) t -> p c t i", i=RUN),
-                    w_raw[e, half][:, g, :, :].rearrange("p t (c i) -> p c t i", i=RUN),
+                    w_bf[e, m][:, g, :, :].rearrange("p (c i) t -> p c t i", i=RUN),
+                    w_raw[e, m][:, g, :, :].rearrange("p t (c i) -> p c t i", i=RUN),
                 )
 
-        def quantize_w(e, half):
-            if (e, half) == (0, 0):
-                w_codes[e, half] = later.tile([P, PASSES * W_COLS], U32, name="w_codes00", align_bytes=64, offset=3072)
-                w_scales[e, half] = early.tile([P, PASSES * W_COLS], U8, name="w_scales00", align_bytes=64, offset=12800)
+        def quantize_w(e, m):
+            words = PASSES * PIECES[e, m] * P
+            if (e, m) == (0, 1):
+                w_codes[e, m] = later.tile([P, words], U32, name="w_codes01", align_bytes=64, offset=0)
             else:
-                w_codes[e, half] = keep.tile([P, PASSES * W_COLS], U32, name="w_codes%d%d" % (e, half), align_bytes=64)
-                w_scales[e, half] = keep.tile([P, PASSES * W_COLS], U8, name="w_scales%d%d" % (e, half), align_bytes=64)
+                w_codes[e, m] = keep.tile([P, words], U32, name="w_codes%d%d" % (e, m), align_bytes=64)
+            w_scales[e, m] = keep.tile([P, words], U8, name="w_scales%d%d" % (e, m), align_bytes=64)
             nc.vector.quantize_mx(
-                out=w_codes[e, half][:].bitcast(E4M3),
-                scales=w_scales[e, half][:],
-                in_=w_bf[e, half][:].rearrange("p g c t -> p (g c t)"),
+                out=w_codes[e, m][:].bitcast(E4M3),
+                scales=w_scales[e, m][:],
+                in_=w_bf[e, m][:].rearrange("p g c t -> p (g c t)"),
             )
 
         def multiply(e, m, dx):
-            half, q = divmod(m * P, W_COLS)
+            first = m if (e, m) in PIECES else m - 1
+            width = PIECES[e, first] * P
             acc = psum.tile([P, SLOTS], F32, name="acc%d%d" % (e, m))
             for g in range(PASSES):
-                cols = slice(g * W_COLS + q, g * W_COLS + q + P)
+                cols = slice(g * width + (m - first) * P, g * width + (m - first + 1) * P)
                 nc.tensor.matmul_mx(
                     out=acc[:],
-                    lhsT=w_codes[e, half][:, cols].bitcast(E4M3),
-                    lhsT_scale=w_scales[e, half][:, cols],
+                    lhsT=w_codes[e, first][:, cols].bitcast(E4M3),
+                    lhsT_scale=w_scales[e, first][:, cols],
                     rhs=dz_codes[g, e][:].bitcast(E5M2),
                     rhs_scale=dz_scales[g, e][:],
                     start=(g == 0),
@@ -206,35 +210,45 @@ def tile_attend_gex_tnh_x_kernel(tc, dyT, hT, ts, wm, offs, out):
         gather_h(0)
         gather_h(1)
         gather_ts()
-        for j in range(3):
-            gather_h(j + 2)
-            weigh(j)
-        for j in range(3):
-            load_dy(j)
-            gather_dy_both(j)
-            if j == 1:
-                load_w(0, 0)
-            gather_h(j + 5)
-            weigh(j + 3)
+        gather_h(2)
+        weigh(0)
+        gather_h(3)
+        weigh(1)
+        load_dy(0)
+        gather_dy_both(0)
+        gather_h(4)
+        weigh(2)
+        load_dy(1)
+        gather_dy_both(1)
+        gather_h(5)
+        weigh(3)
+        gather_h(6)
+        weigh(4)
+        load_dy(2)
+        gather_dy_both(2)
+        gather_h(7)
+        weigh(5)
         weigh_late(6, 0)
-        interleave_w(0, 0)
         load_dy(3)
         gather_dy_both(3)
         weigh_late(7, 0)
         interleave_dz(0, 0)
+        interleave_dz(0, 1)
         for j in range(PACK, PLANES):
             load_dy(j)
             gather_dy(j, 0)
         interleave_dz(1, 0)
-        load_w(0, 1)
-        load_w(1, 0)
-        load_w(1, 1)
+        for e, m in PIECES:
+            load_w(e, m)
+        interleave_w(0, 0)
         quantize_dz(1, 0)
         quantize_dz(0, 0)
         quantize_w(0, 0)
         multiply_one(0, 0)
-        multiply_one(0, 1)
         interleave_w(0, 1)
+        quantize_w(0, 1)
+        interleave_w(0, 2)
+        multiply_one(0, 1)
         dz1[1] = early.tile([P, PACK + 2, SLOTS], F32, name="second", offset=0)
         gather_dy(4, 1)
         gather_dy(5, 1)
@@ -242,17 +256,16 @@ def tile_attend_gex_tnh_x_kernel(tc, dyT, hT, ts, wm, offs, out):
         weigh_late(7, 1)
         gather_dy(6, 1)
         gather_dy(7, 1)
-        quantize_w(0, 1)
-        interleave_dz(0, 1)
-        interleave_dz(1, 1)
+        quantize_w(0, 2)
         quantize_dz(0, 1)
+        interleave_dz(1, 1)
         quantize_dz(1, 1)
         multiply_one(0, 2)
         interleave_w(1, 0)
         quantize_w(1, 0)
         multiply_one(0, 3)
-        interleave_w(1, 1)
-        quantize_w(1, 1)
+        interleave_w(1, 2)
+        quantize_w(1, 2)
         for m in range(4):
             scatter_one(0, m)
         for m in range(4):

@@ -88,7 +88,7 @@ def tile_attend_gex_tnh_x_kernel(tc, dyT, hT, ts, wm, offs, out):
 
         def weigh_late(j, e):
             if e == 0:
-                tile = early.tile([P, SLOTS], F32, name="late%d" % j, offset=(j - 6) * 11776)
+                tile = early.tile([P, SLOTS], F32, name="late%d" % j, offset=(j - 6) * 13824)
                 late[j, e] = tile[:]
             else:
                 late[j, e] = dz1[e][:, j - 2, :]
@@ -135,7 +135,7 @@ def tile_attend_gex_tnh_x_kernel(tc, dyT, hT, ts, wm, offs, out):
         def quantize_dz(g, e):
             dz_codes[g, e] = keep.tile([P, SLOTS], U32, name="dz_codes%d%d" % (g, e), align_bytes=64)
             if g == 0:
-                dz_scales[g, e] = early.tile([P, SLOTS], U8, name="dz_scales0%d" % e, align_bytes=64, offset=12288 + 512 * e)
+                dz_scales[g, e] = early.tile([P, SLOTS], U8, name="dz_scales0%d" % e, align_bytes=64, offset=14336 * e)
             else:
                 dz_scales[g, e] = keep.tile([P, SLOTS], U8, name="dz_scales%d%d" % (g, e), align_bytes=64)
             nc.vector.quantize_mx(
@@ -171,7 +171,10 @@ def tile_attend_gex_tnh_x_kernel(tc, dyT, hT, ts, wm, offs, out):
                 w_codes[e, m] = later.tile([P, words], U32, name="w_codes01", align_bytes=64, offset=0)
             else:
                 w_codes[e, m] = keep.tile([P, words], U32, name="w_codes%d%d" % (e, m), align_bytes=64)
-            w_scales[e, m] = keep.tile([P, words], U8, name="w_scales%d%d" % (e, m), align_bytes=64)
+            if (e, m) == (0, 0):
+                w_scales[e, m] = early.tile([P, words], U8, name="w_scales00", align_bytes=64, offset=512)
+            else:
+                w_scales[e, m] = keep.tile([P, words], U8, name="w_scales%d%d" % (e, m), align_bytes=64)
             nc.vector.quantize_mx(
                 out=w_codes[e, m][:].bitcast(E4M3),
                 scales=w_scales[e, m][:],
@@ -226,9 +229,11 @@ def tile_attend_gex_tnh_x_kernel(tc, dyT, hT, ts, wm, offs, out):
         weigh(4)
         load_dy(2)
         gather_dy_both(2)
+        load_w(0, 0)
         gather_h(7)
         weigh(5)
         weigh_late(6, 0)
+        interleave_w(0, 0)
         load_dy(3)
         gather_dy_both(3)
         weigh_late(7, 0)
@@ -237,38 +242,42 @@ def tile_attend_gex_tnh_x_kernel(tc, dyT, hT, ts, wm, offs, out):
         for j in range(PACK, PLANES):
             load_dy(j)
             gather_dy(j, 0)
+            if j == 6:
+                quantize_dz(0, 0)
+                quantize_w(0, 0)
         interleave_dz(1, 0)
-        for e, m in PIECES:
-            load_w(e, m)
-        interleave_w(0, 0)
+        load_w(0, 1)
+        load_w(0, 2)
+        load_w(1, 0)
+        load_w(1, 2)
         quantize_dz(1, 0)
-        quantize_dz(0, 0)
-        quantize_w(0, 0)
         multiply_one(0, 0)
         interleave_w(0, 1)
-        quantize_w(0, 1)
         interleave_w(0, 2)
-        multiply_one(0, 1)
-        dz1[1] = early.tile([P, PACK + 2, SLOTS], F32, name="second", offset=0)
+        dz1[1] = early.tile([P, PACK + 2, SLOTS], F32, name="second", offset=2048)
         gather_dy(4, 1)
         gather_dy(5, 1)
         weigh_late(6, 1)
         weigh_late(7, 1)
         gather_dy(6, 1)
         gather_dy(7, 1)
-        quantize_w(0, 2)
+        quantize_w(0, 1)
+        multiply_one(0, 1)
         quantize_dz(0, 1)
+        quantize_w(0, 2)
         interleave_dz(1, 1)
         quantize_dz(1, 1)
         multiply_one(0, 2)
         interleave_w(1, 0)
         quantize_w(1, 0)
         multiply_one(0, 3)
+        for m in range(4):
+            scatter_one(0, m)
+        multiply_one(1, 0)
         interleave_w(1, 2)
         quantize_w(1, 2)
         for m in range(4):
-            scatter_one(0, m)
-        for m in range(4):
-            multiply_one(1, m)
+            if m > 0:
+                multiply_one(1, m)
             scatter_one(1, m)
             store(m)

@@ -26,7 +26,8 @@ LISTED = EXPERTS * SLOTS
 LIST_COLS = SLOTS // 16
 PIECES = {(0, 0): 1, (0, 1): 1, (0, 2): 2, (1, 0): 2, (1, 2): 2}
 RUN = 4
-W_PLACE = (0, 1, 0, 1, 2, 0)
+H_PLACE = (0, 1, 2, 3, 2, 0, 1, 3)
+W_PLACE = (0, 1, 3, 2, 0, 1)
 LOAD_BUFS = 9
 ON_GPSIMD = 6
 
@@ -63,11 +64,15 @@ def tile_attend_gex_tnh_x_kernel(tc, dyT, hT, ts, wm, offs, out):
         ts_negated = keep.tile([P, LISTED], F32, name="ts_negated")
 
         def gather_h(j):
-            h = ring.tile([P, TOKENS], F32, name="h", tag="load", bufs=LOAD_BUFS)
+            if j == 7:
+                h = early.tile([P, TOKENS], F32, name="h7", offset=0)
+            else:
+                h = ring.tile([P, TOKENS], F32, name="h", tag="load", bufs=LOAD_BUFS)
             nc.sync.dma_start(h[:], plane_rows(hT, j))
+            listed = places.tile([P, LISTED], F32, name="listed%d" % j, align_bytes=64, offset=H_PLACE[j] * 4096)
             hh = ring.tile([P, LISTED], F32, name="hh", bufs=4)
-            nc.vector.tensor_copy(hh[:], h[:].indirect(offsets[:]))
-            nc.scalar.activation(hh[:], hh[:], SQUARE)
+            nc.vector.tensor_copy(listed[:], h[:].indirect(offsets[:]))
+            nc.scalar.activation(hh[:], listed[:], SQUARE)
             if j < ON_GPSIMD:
                 nc.scalar.activation(hh[:], hh[:], COPY, bias=1.0, scale=-1.0)
             factor[j] = hh
@@ -79,7 +84,7 @@ def tile_attend_gex_tnh_x_kernel(tc, dyT, hT, ts, wm, offs, out):
             nc.scalar.activation(ts_negated[:], ts_listed[:], COPY, scale=-1.0)
 
         def weigh(j):
-            w = places.tile([P, LISTED], F32, name="w%d" % j, offset=W_PLACE[j] * 4096)
+            w = places.tile([P, LISTED], F32, name="w%d" % j, align_bytes=64, offset=W_PLACE[j] * 4096)
             nc.gpsimd.tensor_tensor(w[:], factor[j][:], ts_listed[:], MULT)
             factor[j] = w
 
@@ -88,7 +93,7 @@ def tile_attend_gex_tnh_x_kernel(tc, dyT, hT, ts, wm, offs, out):
 
         def weigh_late(j, e):
             if e == 0:
-                tile = early.tile([P, SLOTS], F32, name="late%d" % j, offset=(j - 6) * 13824)
+                tile = early.tile([P, SLOTS], F32, name="late%d" % j, offset=(j - 6) * 1024)
                 late[j, e] = tile[:]
             else:
                 late[j, e] = dz1[e][:, j - 2, :]
@@ -96,10 +101,7 @@ def tile_attend_gex_tnh_x_kernel(tc, dyT, hT, ts, wm, offs, out):
             nc.vector.scalar_tensor_tensor(late[j, e], factor[j][:, cols], 1.0, ts_negated[:, cols], SUB, MULT)
 
         def load_dy(j):
-            if j in (2, 3):
-                dy[j] = early.tile([P, TOKENS], F32, name="dy%d" % j, offset=(j - 2) * 8192)
-            else:
-                dy[j] = ring.tile([P, TOKENS], F32, name="dy", tag="load", bufs=LOAD_BUFS)
+            dy[j] = ring.tile([P, TOKENS], F32, name="dy", tag="load", bufs=LOAD_BUFS)
             nc.sync.dma_start(dy[j][:], plane_rows(dyT, j))
 
         dz0 = keep.tile([P, PACK, LISTED], F32, name="dz0")
@@ -122,7 +124,9 @@ def tile_attend_gex_tnh_x_kernel(tc, dyT, hT, ts, wm, offs, out):
 
         def interleave_dz(g, e):
             src = dz0[:, :, e * SLOTS : (e + 1) * SLOTS] if g == 0 else dz1[e][:, 0:PACK, :]
-            if (g, e) != (1, 1):
+            if (g, e) == (0, 1):
+                dz_bf[g, e] = places.tile([P, SLOTS, PACK], BF16, name="dz_bf01", align_bytes=64, offset=3 * 4096)
+            elif e == 0:
                 dz_bf[g, e] = keep.tile([P, SLOTS, PACK], BF16, name="dz_bf%d%d" % (g, e), align_bytes=64)
             else:
                 dz_bf[g, e] = later.tile([P, SLOTS, PACK], BF16, name="dz_bf%d%d" % (g, e), align_bytes=64, offset=0)
@@ -135,7 +139,7 @@ def tile_attend_gex_tnh_x_kernel(tc, dyT, hT, ts, wm, offs, out):
         def quantize_dz(g, e):
             dz_codes[g, e] = keep.tile([P, SLOTS], U32, name="dz_codes%d%d" % (g, e), align_bytes=64)
             if g == 0:
-                dz_scales[g, e] = early.tile([P, SLOTS], U8, name="dz_scales0%d" % e, align_bytes=64, offset=14336 * e)
+                dz_scales[g, e] = early.tile([P, SLOTS], U8, name="dz_scales0%d" % e, align_bytes=64, offset=1024 * e)
             else:
                 dz_scales[g, e] = keep.tile([P, SLOTS], U8, name="dz_scales%d%d" % (g, e), align_bytes=64)
             nc.vector.quantize_mx(
@@ -217,32 +221,24 @@ def tile_attend_gex_tnh_x_kernel(tc, dyT, hT, ts, wm, offs, out):
         weigh(0)
         gather_h(3)
         weigh(1)
-        load_dy(0)
-        gather_dy_both(0)
-        gather_h(4)
         weigh(2)
-        load_dy(1)
-        gather_dy_both(1)
-        gather_h(5)
-        weigh(3)
-        gather_h(6)
-        weigh(4)
-        load_dy(2)
-        gather_dy_both(2)
-        load_w(0, 0)
-        gather_h(7)
-        weigh(5)
+        for j in range(PACK):
+            load_dy(j)
+            gather_dy_both(j)
+            if j == 2:
+                load_w(0, 0)
+                interleave_w(0, 0)
+            gather_h(j + 4)
+            if j < 3:
+                weigh(j + 3)
         weigh_late(6, 0)
-        interleave_w(0, 0)
-        load_dy(3)
-        gather_dy_both(3)
-        weigh_late(7, 0)
         interleave_dz(0, 0)
         interleave_dz(0, 1)
         for j in range(PACK, PLANES):
             load_dy(j)
             gather_dy(j, 0)
             if j == 6:
+                weigh_late(7, 0)
                 quantize_dz(0, 0)
                 quantize_w(0, 0)
         interleave_dz(1, 0)
@@ -254,7 +250,7 @@ def tile_attend_gex_tnh_x_kernel(tc, dyT, hT, ts, wm, offs, out):
         multiply_one(0, 0)
         interleave_w(0, 1)
         interleave_w(0, 2)
-        dz1[1] = early.tile([P, PACK + 2, SLOTS], F32, name="second", offset=2048)
+        dz1[1] = early.tile([P, PACK + 2, SLOTS], F32, name="second", offset=2560)
         gather_dy(4, 1)
         gather_dy(5, 1)
         weigh_late(6, 1)

@@ -1,6 +1,7 @@
 from contextlib import ExitStack
 
 import concourse.mybir as mybir
+from concourse.masks import make_identity
 
 EXPERTS, SLOTS, TOKENS, D_IN, D_OUT = 2, 512, 2048, 512, 1024
 FLOPS = 2 * EXPERTS * SLOTS * D_IN * D_OUT
@@ -13,8 +14,8 @@ U8 = mybir.dt.uint8
 E4M3 = mybir.dt.float8_e4m3fn_x4
 E5M2 = mybir.dt.float8_e5m2_x4
 MULT = mybir.AluOpType.mult
-SUB = mybir.AluOpType.subtract
 COPY = mybir.ActivationFunctionType.Copy
+IDENTITY = mybir.ActivationFunctionType.Identity
 SQUARE = mybir.ActivationFunctionType.Square
 
 P = 128
@@ -24,12 +25,13 @@ PASSES = D_OUT // K_PASS
 PLANES = PASSES * PACK
 LISTED = EXPERTS * SLOTS
 LIST_COLS = SLOTS // 16
-PIECES = {(0, 0): 1, (0, 1): 1, (0, 2): 2, (1, 0): 2, (1, 2): 2}
+BLOCKS = SLOTS // P
+D_TILES = D_IN // P
 RUN = 4
-H_PLACE = (0, 1, 2, 3, 2, 0, 1, 3)
-W_PLACE = (0, 1, 3, 2, 0, 1)
-LOAD_BUFS = 9
-ON_GPSIMD = 6
+KIB = 1024
+ON_GPSIMD = 5
+TS_ROW = P - 1
+PIECES = ((0, 0, 1), (0, 1, 1), (0, 2, 1), (0, 3, 1), (1, 0, 2), (1, 2, 2))
 
 
 def tile_attend_gex_tnh_x_kernel(tc, dyT, hT, ts, wm, offs, out):
@@ -38,10 +40,9 @@ def tile_attend_gex_tnh_x_kernel(tc, dyT, hT, ts, wm, offs, out):
     with ExitStack() as ctx:
         keep = ctx.enter_context(tc.tile_pool(name="keep", bufs=1))
         ring = ctx.enter_context(tc.tile_pool(name="ring", bufs=2))
-        early = ctx.enter_context(tc.tile_pool(name="early", bufs=1))
-        later = ctx.enter_context(tc.tile_pool(name="later", bufs=1))
-        places = ctx.enter_context(tc.tile_pool(name="places", bufs=1))
-        psum = ctx.enter_context(tc.psum_pool(name="psum", bufs=1))
+        big = ctx.enter_context(tc.tile_pool(name="big", bufs=1))
+        shared = ctx.enter_context(tc.tile_pool(name="shared", bufs=1))
+        psum = ctx.enter_context(tc.psum_pool(name="psum", bufs=4))
 
         offsets = keep.tile([P, LISTED // 16], U16, name="offsets")
         nc.sync.dma_start(offsets[:], offs)
@@ -53,83 +54,123 @@ def tile_attend_gex_tnh_x_kernel(tc, dyT, hT, ts, wm, offs, out):
             g, t = divmod(j, PACK)
             return x[g * K_PASS : (g + 1) * K_PASS, :].rearrange("(p t) c -> p t c", t=PACK)[:, t, :]
 
-        windows = [keep.tile([P, TOKENS], F32, name="out%d" % m) for m in range(D_IN // P)]
-        for window in windows:
-            nc.gpsimd.memset(window[:], 0.0)
+        def half(e):
+            return slice(e * SLOTS, (e + 1) * SLOTS)
 
+        ts_all = big.tile([P, TOKENS], F32, name="ts_all", offset=64 * KIB)
+        nc.sync.dma_start(ts_all[TS_ROW : TS_ROW + 1, :], ts[TS_ROW : TS_ROW + 1, :])
+        nc.vector.memset(ts_all[0:TS_ROW, :], 0.0)
+        identity = keep.tile([P, P], F32, name="identity")
+        nc.vector.memset(identity[:], 0.0)
+        make_identity(nc, identity[:], nomemset=True)
+        ts_listed = big.tile([P, LISTED], F32, name="ts_listed", offset=84 * KIB)
+        nc.vector.tensor_copy(ts_listed[:], ts_all[:].indirect(offsets[:]))
+
+        ts_col = keep.tile([P, EXPERTS * BLOCKS], F32, name="ts_col")
+        ts_col_neg = keep.tile([P, EXPERTS * BLOCKS], F32, name="ts_col_neg")
+        ts_spread = big.tile([P, LISTED], F32, name="ts_spread", offset=88 * KIB)
+
+        def spread_ts():
+            for e in range(EXPERTS):
+                bank = psum.tile([P, BLOCKS, P], F32, name="turned", tag="turn", bufs=5)
+                for b in range(BLOCKS):
+                    c = e * SLOTS + b * P
+                    nc.tensor.transpose(bank[:, b, :], ts_listed[:, c : c + P], identity[:])
+                nc.scalar.copy(ts_col[:, e * BLOCKS : (e + 1) * BLOCKS], bank[:, :, TS_ROW])
+            for e in range(EXPERTS):
+                bank = psum.tile([P, BLOCKS, P], F32, name="turned", tag="turn", bufs=5)
+                for b in range(BLOCKS):
+                    c = e * BLOCKS + b
+                    nc.tensor.transpose(bank[:, b, :], ts_col[:, c : c + 1].to_broadcast([P, P]), identity[:])
+                nc.scalar.copy(ts_spread[:, half(e)], bank[:].rearrange("p b s -> p (b s)"))
+            nc.scalar.activation(ts_col_neg[:], ts_col[:], COPY, scale=-1.0)
+
+        dz_first = big.tile([P, PACK, LISTED], F32, name="dz_first", offset=112 * KIB)
+        dz_second = [keep.tile([P, PACK, SLOTS], F32, name="dz_second%d" % e) for e in range(EXPERTS)]
         factor = {}
-        dy = {}
-        ts_listed = keep.tile([P, LISTED], F32, name="ts_listed")
-
-        ts_negated = keep.tile([P, LISTED], F32, name="ts_negated")
+        listed = {}
 
         def gather_h(j):
-            if j == 7:
-                h = early.tile([P, TOKENS], F32, name="h7", offset=0)
-            else:
-                h = ring.tile([P, TOKENS], F32, name="h", tag="load", bufs=LOAD_BUFS)
+            h = big.tile([P, TOKENS], F32, name="h%d" % j, offset=j * 8 * KIB)
             nc.sync.dma_start(h[:], plane_rows(hT, j))
-            listed = places.tile([P, LISTED], F32, name="listed%d" % j, align_bytes=64, offset=H_PLACE[j] * 4096)
-            hh = ring.tile([P, LISTED], F32, name="hh", bufs=4)
-            nc.vector.tensor_copy(listed[:], h[:].indirect(offsets[:]))
-            nc.scalar.activation(hh[:], listed[:], SQUARE)
-            if j < ON_GPSIMD:
-                nc.scalar.activation(hh[:], hh[:], COPY, bias=1.0, scale=-1.0)
-            factor[j] = hh
+            listed[j] = big.tile([P, LISTED], F32, name="listed%d" % j, offset=(72 + 4 * (j % 3)) * KIB)
+            nc.vector.tensor_copy(listed[j][:], h[:].indirect(offsets[:]))
 
-        def gather_ts():
-            t = ring.tile([P, TOKENS], F32, name="ts_all", tag="load", bufs=LOAD_BUFS)
-            nc.sync.dma_start(t[:], ts)
-            nc.vector.tensor_copy(ts_listed[:], t[:].indirect(offsets[:]))
-            nc.scalar.activation(ts_negated[:], ts_listed[:], COPY, scale=-1.0)
+        def weigh_on_gpsimd(j):
+            f = big.tile([P, LISTED], F32, name="factor%d" % j, offset=(92 + 4 * j) * KIB)
+            nc.scalar.activation(f[:], listed[j][:], SQUARE)
+            nc.scalar.activation(f[:], f[:], COPY, bias=1.0, scale=-1.0)
+            nc.gpsimd.tensor_tensor(f[:], f[:], ts_spread[:], MULT)
+            factor[j] = f[:]
+            for e in range(EXPERTS):
+                factor[j, e] = f[:, half(e)]
 
-        def weigh(j):
-            w = places.tile([P, LISTED], F32, name="w%d" % j, align_bytes=64, offset=W_PLACE[j] * 4096)
-            nc.gpsimd.tensor_tensor(w[:], factor[j][:], ts_listed[:], MULT)
-            factor[j] = w
+        squares = {}
 
-        late = {}
-        dz1 = {}
+        def square(j):
+            squares[j] = ring.tile([P, LISTED], F32, name="squares", bufs=3)
+            nc.scalar.activation(squares[j][:], listed[j][:], SQUARE)
 
-        def weigh_late(j, e):
-            if e == 0:
-                tile = early.tile([P, SLOTS], F32, name="late%d" % j, offset=(j - 6) * 1024)
-                late[j, e] = tile[:]
-            else:
-                late[j, e] = dz1[e][:, j - 2, :]
-            cols = slice(e * SLOTS, (e + 1) * SLOTS)
-            nc.vector.scalar_tensor_tensor(late[j, e], factor[j][:, cols], 1.0, ts_negated[:, cols], SUB, MULT)
+        turned_planes = range(ON_GPSIMD, PLANES)
+
+        def factor_place(j, e):
+            if (j, e) == (PLANES - 1, 0):
+                flat = dz_second[1][:].rearrange("p t s -> p (t s)")
+                return flat[:, SLOTS + SLOTS // 2 : 2 * SLOTS + SLOTS // 2]
+            if (j, e) == (PACK + 1, 0):
+                tile = shared.tile([P, SLOTS], F32, name="factor50", align_bytes=64, offset=0)
+                return tile[:]
+            tile = keep.tile([P, SLOTS], F32, name="factor%d%d" % (j, e))
+            return tile[:]
+
+        def weigh_turned(e):
+            weighed = ring.tile([P, BLOCKS, len(turned_planes), P], F32, name="weighed")
+            for b in range(BLOCKS):
+                there = psum.tile([P, len(turned_planes), P], F32, name="there", tag="turn", bufs=5)
+                c = e * SLOTS + b * P
+                for k, j in enumerate(turned_planes):
+                    nc.tensor.transpose(there[:, k, :], squares[j][:, c : c + P], identity[:])
+                c = e * BLOCKS + b
+                nc.scalar.activation(
+                    weighed[:, b, :, :], there[:], IDENTITY, bias=ts_col[:, c : c + 1], scale=ts_col_neg[:, c : c + 1]
+                )
+            for k, j in enumerate(turned_planes):
+                back = psum.tile([P, BLOCKS, P], F32, name="back", tag="turn", bufs=5)
+                for b in range(BLOCKS):
+                    nc.tensor.transpose(back[:, b, :], weighed[:, b, k, :], identity[:])
+                factor[j, e] = factor_place(j, e)
+                nc.scalar.copy(factor[j, e], back[:].rearrange("p b s -> p (b s)"))
+
+        dy = {}
 
         def load_dy(j):
-            dy[j] = ring.tile([P, TOKENS], F32, name="dy", tag="load", bufs=LOAD_BUFS)
+            dy[j] = big.tile([P, TOKENS], F32, name="dy%d" % j, offset=j * 8 * KIB)
             nc.sync.dma_start(dy[j][:], plane_rows(dyT, j))
 
-        dz0 = keep.tile([P, PACK, LISTED], F32, name="dz0")
-        dz1[0] = keep.tile([P, PACK, SLOTS], F32, name="dz1_first")
-
         def gather_dy_both(j):
-            nc.vector.tensor_tensor(dz0[:, j, :], dy[j][:].indirect(offsets[:]), factor[j][:], MULT)
+            nc.vector.tensor_tensor(dz_first[:, j, :], dy[j][:].indirect(offsets[:]), factor[j], MULT)
 
         def gather_dy(j, e):
-            nc.vector.tensor_tensor(
-                dz1[e][:, j - PACK, :],
-                dy[j][:].indirect(slots_of(e)),
-                late[j, e] if (j, e) in late else factor[j][:, e * SLOTS : (e + 1) * SLOTS],
-                MULT,
-            )
+            nc.vector.tensor_tensor(dz_second[e][:, j - PACK, :], dy[j][:].indirect(slots_of(e)), factor[j, e], MULT)
+
+        windows = {}
+
+        def clear_window(m):
+            windows[m] = big.tile([P, TOKENS], F32, name="out%d" % m, offset=m * 8 * KIB)
+            nc.gpsimd.memset(windows[m][:], 0.0)
 
         dz_bf = {}
         dz_codes = {}
         dz_scales = {}
 
         def interleave_dz(g, e):
-            src = dz0[:, :, e * SLOTS : (e + 1) * SLOTS] if g == 0 else dz1[e][:, 0:PACK, :]
-            if (g, e) == (0, 1):
-                dz_bf[g, e] = places.tile([P, SLOTS, PACK], BF16, name="dz_bf01", align_bytes=64, offset=3 * 4096)
-            elif e == 0:
+            src = dz_first[:, :, half(e)] if g == 0 else dz_second[e][:]
+            if (g, e) != (1, 1):
                 dz_bf[g, e] = keep.tile([P, SLOTS, PACK], BF16, name="dz_bf%d%d" % (g, e), align_bytes=64)
             else:
-                dz_bf[g, e] = later.tile([P, SLOTS, PACK], BF16, name="dz_bf%d%d" % (g, e), align_bytes=64, offset=0)
+                dz_bf[g, e] = shared.tile(
+                    [P, SLOTS, PACK], BF16, name="dz_bf%d%d" % (g, e), align_bytes=64, offset=4 * KIB
+                )
             nc.scalar.activation(
                 dz_bf[g, e][:].rearrange("p (c i) t -> p c t i", i=RUN),
                 src.rearrange("p t (c i) -> p c t i", i=RUN),
@@ -137,143 +178,152 @@ def tile_attend_gex_tnh_x_kernel(tc, dyT, hT, ts, wm, offs, out):
             )
 
         def quantize_dz(g, e):
-            dz_codes[g, e] = keep.tile([P, SLOTS], U32, name="dz_codes%d%d" % (g, e), align_bytes=64)
             if g == 0:
-                dz_scales[g, e] = early.tile([P, SLOTS], U8, name="dz_scales0%d" % e, align_bytes=64, offset=1024 * e)
+                dz_codes[g, e] = shared.tile(
+                    [P, SLOTS], U32, name="dz_codes%d%d" % (g, e), align_bytes=64, offset=2 * e * KIB
+                )
             else:
-                dz_scales[g, e] = keep.tile([P, SLOTS], U8, name="dz_scales%d%d" % (g, e), align_bytes=64)
+                dz_codes[g, e] = keep.tile([P, SLOTS], U32, name="dz_codes%d%d" % (g, e), align_bytes=64)
+            dz_scales[g, e] = keep.tile([P, SLOTS], U8, name="dz_scales%d%d" % (g, e), align_bytes=64)
             nc.vector.quantize_mx(
                 out=dz_codes[g, e][:].bitcast(E5M2),
                 scales=dz_scales[g, e][:],
                 in_=dz_bf[g, e][:].rearrange("p c t -> p (c t)"),
             )
 
-        w_raw = {}
+        stage = {}
         w_bf = {}
         w_codes = {}
         w_scales = {}
 
-        def load_w(e, m):
-            width = PIECES[e, m] * P
-            w_raw[e, m] = ring.tile([P, PASSES, PACK, width], F32, name="w_raw", tag="load", bufs=LOAD_BUFS)
+        def raw(i):
+            return stage[i][:].rearrange("p (g t d) -> p g t d", g=PASSES, t=PACK)
+
+        def load_w(i):
+            e, m, tiles = PIECES[i]
+            place = (92, 96, 100, 104, 32, 112)[i]
+            stage[i] = big.tile([P, tiles * PLANES * P], F32, name="stage%d" % i, offset=place * KIB)
             rows = wm[e].rearrange("(g p t) d -> p g t d", g=PASSES, t=PACK)
             for g in range(PASSES):
-                nc.sync.dma_start(w_raw[e, m][:, g, :, :], rows[:, g, :, m * P : m * P + width])
+                nc.sync.dma_start(raw(i)[:, g, :, :], rows[:, g, :, m * P : (m + tiles) * P])
 
-        def interleave_w(e, m):
-            width = PIECES[e, m] * P
-            w_bf[e, m] = ring.tile([P, PASSES, width, PACK], BF16, name="w_bf%d%d" % (e, m), tag="w_bf", align_bytes=64)
-            for g in range(PASSES):
-                nc.scalar.copy(
-                    w_bf[e, m][:, g, :, :].rearrange("p (c i) t -> p c t i", i=RUN),
-                    w_raw[e, m][:, g, :, :].rearrange("p t (c i) -> p c t i", i=RUN),
-                )
-
-        def quantize_w(e, m):
-            words = PASSES * PIECES[e, m] * P
-            if (e, m) == (0, 1):
-                w_codes[e, m] = later.tile([P, words], U32, name="w_codes01", align_bytes=64, offset=0)
+        def interleave_w(i):
+            width = PIECES[i][2] * P
+            if i == 0:
+                w_bf[i] = shared.tile([P, PASSES, width, PACK], BF16, name="w_bf0", align_bytes=64, offset=2 * KIB)
             else:
-                w_codes[e, m] = keep.tile([P, words], U32, name="w_codes%d%d" % (e, m), align_bytes=64)
-            if (e, m) == (0, 0):
-                w_scales[e, m] = early.tile([P, words], U8, name="w_scales00", align_bytes=64, offset=512)
-            else:
-                w_scales[e, m] = keep.tile([P, words], U8, name="w_scales%d%d" % (e, m), align_bytes=64)
-            nc.vector.quantize_mx(
-                out=w_codes[e, m][:].bitcast(E4M3),
-                scales=w_scales[e, m][:],
-                in_=w_bf[e, m][:].rearrange("p g c t -> p (g c t)"),
+                w_bf[i] = ring.tile([P, PASSES, width, PACK], BF16, name="w_bf%d" % i, tag="w_bf", align_bytes=64)
+            nc.scalar.copy(
+                w_bf[i][:].rearrange("p g (c i) t -> p g c t i", i=RUN),
+                raw(i).rearrange("p g t (c i) -> p g c t i", i=RUN),
             )
 
-        def multiply(e, m, dx):
-            first = m if (e, m) in PIECES else m - 1
-            width = PIECES[e, first] * P
-            acc = psum.tile([P, SLOTS], F32, name="acc%d%d" % (e, m))
+        def quantize_w(i):
+            words = PASSES * PIECES[i][2] * P
+            if i == 0:
+                w_codes[i] = shared.tile([P, words], U32, name="w_codes0", align_bytes=64, offset=4 * KIB)
+            else:
+                w_codes[i] = keep.tile([P, words], U32, name="w_codes%d" % i, align_bytes=64)
+            w_scales[i] = keep.tile([P, words], U8, name="w_scales%d" % i, align_bytes=64)
+            nc.vector.quantize_mx(
+                out=w_codes[i][:].bitcast(E4M3),
+                scales=w_scales[i][:],
+                in_=w_bf[i][:].rearrange("p g c t -> p (g c t)"),
+            )
+
+        acc = {}
+        dx = {}
+
+        def multiply(e, m):
+            i = [k for k, (pe, pm, tiles) in enumerate(PIECES) if pe == e and pm <= m < pm + tiles][0]
+            first, width = PIECES[i][1], PIECES[i][2] * P
+            acc[e, m] = psum.tile([P, SLOTS], F32, name="acc", tag="acc", bufs=3)
             for g in range(PASSES):
                 cols = slice(g * width + (m - first) * P, g * width + (m - first + 1) * P)
                 nc.tensor.matmul_mx(
-                    out=acc[:],
-                    lhsT=w_codes[e, first][:, cols].bitcast(E4M3),
-                    lhsT_scale=w_scales[e, first][:, cols],
+                    out=acc[e, m][:],
+                    lhsT=w_codes[i][:, cols].bitcast(E4M3),
+                    lhsT_scale=w_scales[i][:, cols],
                     rhs=dz_codes[g, e][:].bitcast(E5M2),
                     rhs_scale=dz_scales[g, e][:],
                     start=(g == 0),
                     stop=(g == PASSES - 1),
                 )
-            nc.scalar.copy(dx, acc[:])
 
-        dx_one = {}
+        def drain(e, m, i, start=0):
+            dx[e, m] = stage[i][:, start : start + SLOTS]
+            nc.scalar.copy(dx[e, m], acc[e, m][:])
 
-        def multiply_one(e, m):
-            dx_one[e, m] = ring.tile([P, SLOTS], F32, name="dx", bufs=4)
-            multiply(e, m, dx_one[e, m][:])
-
-        def scatter_one(e, m):
-            nc.vector.tensor_copy(windows[m][:].indirect(slots_of(e)), dx_one[e, m][:])
+        def scatter(e, m):
+            nc.vector.tensor_copy(windows[m][:].indirect(slots_of(e)), dx[e, m])
 
         def store(m):
             nc.sync.dma_start(out[m * P : (m + 1) * P, :], windows[m][:])
 
         gather_h(0)
-        gather_h(1)
-        gather_ts()
-        gather_h(2)
-        weigh(0)
-        gather_h(3)
-        weigh(1)
-        weigh(2)
-        for j in range(PACK):
+        spread_ts()
+        for j in range(PLANES):
+            if j + 1 < PLANES:
+                gather_h(j + 1)
+            if j < ON_GPSIMD:
+                weigh_on_gpsimd(j)
+            else:
+                square(j)
+        for e in range(EXPERTS):
+            weigh_turned(e)
+        for j in range(PLANES):
             load_dy(j)
+        for j in range(PACK):
             gather_dy_both(j)
-            if j == 2:
-                load_w(0, 0)
-                interleave_w(0, 0)
-            gather_h(j + 4)
-            if j < 3:
-                weigh(j + 3)
-        weigh_late(6, 0)
+            clear_window(j)
+            load_w(j)
         interleave_dz(0, 0)
         interleave_dz(0, 1)
-        for j in range(PACK, PLANES):
-            load_dy(j)
-            gather_dy(j, 0)
-            if j == 6:
-                weigh_late(7, 0)
-                quantize_dz(0, 0)
-                quantize_w(0, 0)
-        interleave_dz(1, 0)
-        load_w(0, 1)
-        load_w(0, 2)
-        load_w(1, 0)
-        load_w(1, 2)
-        quantize_dz(1, 0)
-        multiply_one(0, 0)
-        interleave_w(0, 1)
-        interleave_w(0, 2)
-        dz1[1] = early.tile([P, PACK + 2, SLOTS], F32, name="second", offset=2560)
+        gather_dy(4, 0)
         gather_dy(4, 1)
+        load_w(4)
+        load_w(5)
+        gather_dy(5, 0)
+        quantize_dz(0, 0)
+        gather_dy(6, 0)
+        gather_dy(7, 0)
+        interleave_dz(1, 0)
         gather_dy(5, 1)
-        weigh_late(6, 1)
-        weigh_late(7, 1)
         gather_dy(6, 1)
         gather_dy(7, 1)
-        quantize_w(0, 1)
-        multiply_one(0, 1)
+        interleave_w(0)
+        quantize_dz(1, 0)
+        quantize_w(0)
+        multiply(0, 0)
         quantize_dz(0, 1)
-        quantize_w(0, 2)
+        interleave_w(1)
+        quantize_w(1)
+        multiply(0, 1)
+        drain(0, 0, 1)
+        scatter(0, 0)
+        interleave_w(2)
+        quantize_w(2)
+        multiply(0, 2)
+        drain(0, 1, 2)
+        scatter(0, 1)
+        interleave_w(3)
+        quantize_w(3)
+        multiply(0, 3)
+        drain(0, 2, 3)
+        scatter(0, 2)
         interleave_dz(1, 1)
         quantize_dz(1, 1)
-        multiply_one(0, 2)
-        interleave_w(1, 0)
-        quantize_w(1, 0)
-        multiply_one(0, 3)
-        for m in range(4):
-            scatter_one(0, m)
-        multiply_one(1, 0)
-        interleave_w(1, 2)
-        quantize_w(1, 2)
-        for m in range(4):
-            if m > 0:
-                multiply_one(1, m)
-            scatter_one(1, m)
+        interleave_w(4)
+        quantize_w(4)
+        multiply(1, 0)
+        multiply(1, 1)
+        drain(0, 3, 4)
+        scatter(0, 3)
+        interleave_w(5)
+        quantize_w(5)
+        multiply(1, 2)
+        multiply(1, 3)
+        for m in range(D_TILES):
+            drain(1, m, 5, m * SLOTS)
+            scatter(1, m)
             store(m)

@@ -1,7 +1,6 @@
 from contextlib import ExitStack
 
 import concourse.mybir as mybir
-from concourse.masks import make_identity
 
 EXPERTS, SLOTS, TOKENS, D_IN, D_OUT = 2, 512, 2048, 512, 1024
 FLOPS = 2 * EXPERTS * SLOTS * D_IN * D_OUT
@@ -16,6 +15,7 @@ E5M2 = mybir.dt.float8_e5m2_x4
 MULT = mybir.AluOpType.mult
 COPY = mybir.ActivationFunctionType.Copy
 IDENTITY = mybir.ActivationFunctionType.Identity
+RELU = mybir.ActivationFunctionType.Relu
 SQUARE = mybir.ActivationFunctionType.Square
 
 P = 128
@@ -59,16 +59,24 @@ def tile_attend_gex_tnh_x_kernel(tc, dyT, hT, ts, wm, offs, out):
 
         ts_all = big.tile([P, TOKENS], F32, name="ts_all", offset=64 * KIB)
         nc.sync.dma_start(ts_all[TS_ROW : TS_ROW + 1, :], ts[TS_ROW : TS_ROW + 1, :])
-        nc.vector.memset(ts_all[0:TS_ROW, :], 0.0)
+        nc.vector.memset(ts_all[0:TS_ROW, 0 : TOKENS // 2 - 1], 0.0)
+        nc.vector.memset(ts_all[0:TS_ROW, TOKENS // 2 - 1 : TOKENS], 0.0)
         identity = keep.tile([P, P], F32, name="identity")
-        nc.vector.memset(identity[:], 0.0)
-        make_identity(nc, identity[:], nomemset=True)
-        ts_listed = big.tile([P, LISTED], F32, name="ts_listed", offset=84 * KIB)
-        nc.vector.tensor_copy(ts_listed[:], ts_all[:].indirect(offsets[:]))
+        distance = keep.tile([P, P], F32, name="distance")
+        nc.gpsimd.iota(distance[:], [[-1, P]], base=0, channel_multiplier=1, allow_small_or_imprecise_dtypes=True)
+        nc.scalar.activation(distance[:], distance[:], SQUARE)
+        nc.scalar.activation(identity[:], distance[:], RELU, bias=1.0, scale=-1.0)
+        windows = [keep.tile([P, TOKENS], F32, name="out%d" % m) for m in range(D_TILES)]
+        for window in windows:
+            nc.gpsimd.memset(window[:], 0.0)
+        ts_listed = big.tile([P, LISTED], F32, name="ts_listed", offset=72 * KIB)
+        for e in range(EXPERTS):
+            nc.vector.tensor_copy(ts_listed[:, half(e)], ts_all[:].indirect(slots_of(e)))
 
+        ts_wide = big.tile([P, EXPERTS * BLOCKS + 2, P], F32, name="ts_wide", offset=95 * KIB + KIB // 2)
         ts_col = keep.tile([P, EXPERTS * BLOCKS], F32, name="ts_col")
         ts_col_neg = keep.tile([P, EXPERTS * BLOCKS], F32, name="ts_col_neg")
-        ts_spread = big.tile([P, LISTED], F32, name="ts_spread", offset=88 * KIB)
+        ts_spread = big.tile([P, LISTED], F32, name="ts_spread", offset=76 * KIB)
 
         def spread_ts():
             for e in range(EXPERTS):
@@ -76,16 +84,19 @@ def tile_attend_gex_tnh_x_kernel(tc, dyT, hT, ts, wm, offs, out):
                 for b in range(BLOCKS):
                     c = e * SLOTS + b * P
                     nc.tensor.transpose(bank[:, b, :], ts_listed[:, c : c + P], identity[:])
-                nc.scalar.copy(ts_col[:, e * BLOCKS : (e + 1) * BLOCKS], bank[:, :, TS_ROW])
+                nc.scalar.copy(
+                    ts_wide[:, e * BLOCKS : (e + 1) * BLOCKS, :],
+                    bank[:, :, TS_ROW : TS_ROW + 1].to_broadcast([P, BLOCKS, P]),
+                )
             for e in range(EXPERTS):
                 bank = psum.tile([P, BLOCKS, P], F32, name="turned", tag="turn", bufs=5)
                 for b in range(BLOCKS):
-                    c = e * BLOCKS + b
-                    nc.tensor.transpose(bank[:, b, :], ts_col[:, c : c + 1].to_broadcast([P, P]), identity[:])
+                    nc.tensor.transpose(bank[:, b, :], ts_wide[:, e * BLOCKS + b, :], identity[:])
                 nc.scalar.copy(ts_spread[:, half(e)], bank[:].rearrange("p b s -> p (b s)"))
-            nc.scalar.activation(ts_col_neg[:], ts_col[:], COPY, scale=-1.0)
+            nc.scalar.copy(ts_col[:], ts_wide[:, 0 : EXPERTS * BLOCKS, 0])
+            nc.scalar.activation(ts_col_neg[:], ts_wide[:, 0 : EXPERTS * BLOCKS, 0], COPY, scale=-1.0)
 
-        dz_first = big.tile([P, PACK, LISTED], F32, name="dz_first", offset=112 * KIB)
+        dz_first = big.tile([P, PACK, LISTED], F32, name="dz_first", offset=64 * KIB)
         dz_second = [keep.tile([P, PACK, SLOTS], F32, name="dz_second%d" % e) for e in range(EXPERTS)]
         factor = {}
         listed = {}
@@ -93,7 +104,7 @@ def tile_attend_gex_tnh_x_kernel(tc, dyT, hT, ts, wm, offs, out):
         def gather_h(j):
             h = big.tile([P, TOKENS], F32, name="h%d" % j, offset=j * 8 * KIB)
             nc.sync.dma_start(h[:], plane_rows(hT, j))
-            listed[j] = big.tile([P, LISTED], F32, name="listed%d" % j, offset=(72 + 4 * (j % 3)) * KIB)
+            listed[j] = big.tile([P, LISTED], F32, name="listed%d" % j, offset=(80 + 4 * (j % 3)) * KIB)
             nc.vector.tensor_copy(listed[j][:], h[:].indirect(offsets[:]))
 
         def weigh_on_gpsimd(j):
@@ -153,12 +164,6 @@ def tile_attend_gex_tnh_x_kernel(tc, dyT, hT, ts, wm, offs, out):
         def gather_dy(j, e):
             nc.vector.tensor_tensor(dz_second[e][:, j - PACK, :], dy[j][:].indirect(slots_of(e)), factor[j, e], MULT)
 
-        windows = {}
-
-        def clear_window(m):
-            windows[m] = big.tile([P, TOKENS], F32, name="out%d" % m, offset=m * 8 * KIB)
-            nc.gpsimd.memset(windows[m][:], 0.0)
-
         dz_bf = {}
         dz_codes = {}
         dz_scales = {}
@@ -201,7 +206,7 @@ def tile_attend_gex_tnh_x_kernel(tc, dyT, hT, ts, wm, offs, out):
 
         def load_w(i):
             e, m, tiles = PIECES[i]
-            place = (92, 96, 100, 104, 32, 112)[i]
+            place = (92, 96, 100, 104, 32, 64)[i]
             stage[i] = big.tile([P, tiles * PLANES * P], F32, name="stage%d" % i, offset=place * KIB)
             rows = wm[e].rearrange("(g p t) d -> p g t d", g=PASSES, t=PACK)
             for g in range(PASSES):
@@ -260,8 +265,8 @@ def tile_attend_gex_tnh_x_kernel(tc, dyT, hT, ts, wm, offs, out):
         def store(m):
             nc.sync.dma_start(out[m * P : (m + 1) * P, :], windows[m][:])
 
-        gather_h(0)
         spread_ts()
+        gather_h(0)
         for j in range(PLANES):
             if j + 1 < PLANES:
                 gather_h(j + 1)
@@ -275,7 +280,6 @@ def tile_attend_gex_tnh_x_kernel(tc, dyT, hT, ts, wm, offs, out):
             load_dy(j)
         for j in range(PACK):
             gather_dy_both(j)
-            clear_window(j)
             load_w(j)
         interleave_dz(0, 0)
         interleave_dz(0, 1)

@@ -69,11 +69,11 @@ def tile_attend_gex_tnh_x_kernel(tc, dyT, hT, ts, wm, offs, out):
         windows = [keep.tile([P, TOKENS], F32, name="out%d" % m) for m in range(D_TILES)]
         for window in windows:
             nc.gpsimd.memset(window[:], 0.0)
-        ts_listed = big.tile([P, LISTED], F32, name="ts_listed", offset=72 * KIB)
+        ts_listed = big.tile([P, LISTED], F32, name="ts_listed", offset=112 * KIB)
         for e in range(EXPERTS):
             nc.vector.tensor_copy(ts_listed[:, half(e)], ts_all[:].indirect(slots_of(e)))
 
-        ts_wide = big.tile([P, EXPERTS * BLOCKS + 2, P], F32, name="ts_wide", offset=95 * KIB + KIB // 2)
+        ts_turned = big.tile([P, LISTED + 2 * P], F32, name="ts_turned", offset=99 * KIB + KIB // 2)
         ts_col = keep.tile([P, EXPERTS * BLOCKS], F32, name="ts_col")
         ts_col_neg = keep.tile([P, EXPERTS * BLOCKS], F32, name="ts_col_neg")
         ts_spread = big.tile([P, LISTED], F32, name="ts_spread", offset=76 * KIB)
@@ -84,20 +84,20 @@ def tile_attend_gex_tnh_x_kernel(tc, dyT, hT, ts, wm, offs, out):
                 for b in range(BLOCKS):
                     c = e * SLOTS + b * P
                     nc.tensor.transpose(bank[:, b, :], ts_listed[:, c : c + P], identity[:])
-                nc.scalar.copy(
-                    ts_wide[:, e * BLOCKS : (e + 1) * BLOCKS, :],
-                    bank[:, :, TS_ROW : TS_ROW + 1].to_broadcast([P, BLOCKS, P]),
-                )
+                nc.scalar.copy(ts_turned[:, e * BLOCKS : (e + 1) * BLOCKS], bank[:, :, TS_ROW])
+            nc.scalar.copy(ts_col[:], ts_turned[:, 0 : EXPERTS * BLOCKS])
+            nc.scalar.activation(ts_col_neg[:], ts_turned[:, 0 : EXPERTS * BLOCKS], COPY, scale=-1.0)
             for e in range(EXPERTS):
                 bank = psum.tile([P, BLOCKS, P], F32, name="turned", tag="turn", bufs=5)
                 for b in range(BLOCKS):
-                    nc.tensor.transpose(bank[:, b, :], ts_wide[:, e * BLOCKS + b, :], identity[:])
+                    c = e * BLOCKS + b
+                    nc.tensor.transpose(bank[:, b, :], ts_turned[:, c : c + 1].to_broadcast([P, P]), identity[:])
                 nc.scalar.copy(ts_spread[:, half(e)], bank[:].rearrange("p b s -> p (b s)"))
-            nc.scalar.copy(ts_col[:], ts_wide[:, 0 : EXPERTS * BLOCKS, 0])
-            nc.scalar.activation(ts_col_neg[:], ts_wide[:, 0 : EXPERTS * BLOCKS, 0], COPY, scale=-1.0)
 
         dz_first = big.tile([P, PACK, LISTED], F32, name="dz_first", offset=64 * KIB)
-        dz_second = [keep.tile([P, PACK, SLOTS], F32, name="dz_second%d" % e) for e in range(EXPERTS)]
+        second_first = keep.tile([P, PACK * SLOTS], F32, name="second_first")
+        second_other = keep.tile([P, (PACK + 1) * SLOTS], F32, name="second_other", align_bytes=64)
+        dz_second = [second_first[:], second_other[:, 0 : PACK * SLOTS]]
         factor = {}
         listed = {}
 
@@ -107,10 +107,14 @@ def tile_attend_gex_tnh_x_kernel(tc, dyT, hT, ts, wm, offs, out):
             listed[j] = big.tile([P, LISTED], F32, name="listed%d" % j, offset=(80 + 4 * (j % 3)) * KIB)
             nc.vector.tensor_copy(listed[j][:], h[:].indirect(offsets[:]))
 
+        squared = big.tile([P, LISTED], F32, name="squared", offset=112 * KIB)
+
         def weigh_on_gpsimd(j):
             f = big.tile([P, LISTED], F32, name="factor%d" % j, offset=(92 + 4 * j) * KIB)
-            nc.scalar.activation(f[:], listed[j][:], SQUARE)
-            nc.scalar.activation(f[:], f[:], COPY, bias=1.0, scale=-1.0)
+            for e in range(EXPERTS):
+                nc.scalar.activation(squared[:, half(e)], listed[j][:, half(e)], SQUARE)
+            for e in range(EXPERTS):
+                nc.scalar.activation(f[:, half(e)], squared[:, half(e)], COPY, bias=1.0, scale=-1.0)
             nc.gpsimd.tensor_tensor(f[:], f[:], ts_spread[:], MULT)
             factor[j] = f[:]
             for e in range(EXPERTS):
@@ -119,17 +123,22 @@ def tile_attend_gex_tnh_x_kernel(tc, dyT, hT, ts, wm, offs, out):
         squares = {}
 
         def square(j):
-            squares[j] = ring.tile([P, LISTED], F32, name="squares", bufs=3)
-            nc.scalar.activation(squares[j][:], listed[j][:], SQUARE)
+            if j == ON_GPSIMD:
+                kept = big.tile([P, PLANES - ON_GPSIMD, LISTED], F32, name="squares", offset=112 * KIB)
+                for k in range(ON_GPSIMD, PLANES):
+                    squares[k] = kept[:, k - ON_GPSIMD, :]
+            nc.scalar.activation(squares[j], listed[j][:], SQUARE)
 
         turned_planes = range(ON_GPSIMD, PLANES)
 
         def factor_place(j, e):
             if (j, e) == (PLANES - 1, 0):
-                flat = dz_second[1][:].rearrange("p t s -> p (t s)")
-                return flat[:, SLOTS + SLOTS // 2 : 2 * SLOTS + SLOTS // 2]
+                return second_other[:, SLOTS + SLOTS // 2 : 2 * SLOTS + SLOTS // 2]
             if (j, e) == (PACK + 1, 0):
                 tile = shared.tile([P, SLOTS], F32, name="factor50", align_bytes=64, offset=0)
+                return tile[:]
+            if j == PACK + 2:
+                tile = shared.tile([P, SLOTS], F32, name="factor6%d" % e, align_bytes=64, offset=(2 + 4 * e) * KIB)
                 return tile[:]
             tile = keep.tile([P, SLOTS], F32, name="factor%d%d" % (j, e))
             return tile[:]
@@ -162,38 +171,43 @@ def tile_attend_gex_tnh_x_kernel(tc, dyT, hT, ts, wm, offs, out):
             nc.vector.tensor_tensor(dz_first[:, j, :], dy[j][:].indirect(offsets[:]), factor[j], MULT)
 
         def gather_dy(j, e):
-            nc.vector.tensor_tensor(dz_second[e][:, j - PACK, :], dy[j][:].indirect(slots_of(e)), factor[j, e], MULT)
+            nc.vector.tensor_tensor(dz_second[e][:, (j - PACK) * SLOTS : (j - PACK + 1) * SLOTS], dy[j][:].indirect(slots_of(e)), factor[j, e], MULT)
 
         dz_bf = {}
         dz_codes = {}
         dz_scales = {}
 
         def interleave_dz(g, e):
-            src = dz_first[:, :, half(e)] if g == 0 else dz_second[e][:]
-            if (g, e) != (1, 1):
-                dz_bf[g, e] = keep.tile([P, SLOTS, PACK], BF16, name="dz_bf%d%d" % (g, e), align_bytes=64)
+            src = dz_first[:, :, half(e)] if g == 0 else dz_second[e].rearrange("p (t s) -> p t s", t=PACK)
+            if (g, e) == (1, 0):
+                dz_bf[g, e] = second_other[:, (PACK - 1) * SLOTS : (PACK + 1) * SLOTS].bitcast(BF16)
+            elif (g, e) == (1, 1):
+                tile = shared.tile([P, SLOTS * PACK], BF16, name="dz_bf11", align_bytes=64, offset=2 * KIB)
+                dz_bf[g, e] = tile[:]
             else:
-                dz_bf[g, e] = shared.tile(
-                    [P, SLOTS, PACK], BF16, name="dz_bf%d%d" % (g, e), align_bytes=64, offset=4 * KIB
-                )
+                tile = keep.tile([P, SLOTS * PACK], BF16, name="dz_bf%d%d" % (g, e), align_bytes=64)
+                dz_bf[g, e] = tile[:]
             nc.scalar.activation(
-                dz_bf[g, e][:].rearrange("p (c i) t -> p c t i", i=RUN),
+                dz_bf[g, e].rearrange("p (c i t) -> p c t i", i=RUN, t=PACK),
                 src.rearrange("p t (c i) -> p c t i", i=RUN),
                 COPY,
             )
 
         def quantize_dz(g, e):
-            if g == 0:
-                dz_codes[g, e] = shared.tile(
-                    [P, SLOTS], U32, name="dz_codes%d%d" % (g, e), align_bytes=64, offset=2 * e * KIB
-                )
+            if (g, e) == (0, 0):
+                tile = shared.tile([P, SLOTS], U32, name="dz_codes00", align_bytes=64, offset=0)
+                dz_codes[g, e] = tile[:]
+            elif (g, e) == (0, 1):
+                tile = shared.tile([P, SLOTS], U32, name="dz_codes01", align_bytes=64, offset=6 * KIB)
+                dz_codes[g, e] = tile[:]
             else:
-                dz_codes[g, e] = keep.tile([P, SLOTS], U32, name="dz_codes%d%d" % (g, e), align_bytes=64)
+                tile = keep.tile([P, SLOTS], U32, name="dz_codes%d%d" % (g, e), align_bytes=64)
+                dz_codes[g, e] = tile[:]
             dz_scales[g, e] = keep.tile([P, SLOTS], U8, name="dz_scales%d%d" % (g, e), align_bytes=64)
             nc.vector.quantize_mx(
-                out=dz_codes[g, e][:].bitcast(E5M2),
+                out=dz_codes[g, e].bitcast(E5M2),
                 scales=dz_scales[g, e][:],
-                in_=dz_bf[g, e][:].rearrange("p c t -> p (c t)"),
+                in_=dz_bf[g, e],
             )
 
         stage = {}
@@ -206,7 +220,7 @@ def tile_attend_gex_tnh_x_kernel(tc, dyT, hT, ts, wm, offs, out):
 
         def load_w(i):
             e, m, tiles = PIECES[i]
-            place = (92, 96, 100, 104, 32, 64)[i]
+            place = (88, 92, 96, 100, 32, 64)[i]
             stage[i] = big.tile([P, tiles * PLANES * P], F32, name="stage%d" % i, offset=place * KIB)
             rows = wm[e].rearrange("(g p t) d -> p g t d", g=PASSES, t=PACK)
             for g in range(PASSES):
@@ -214,26 +228,24 @@ def tile_attend_gex_tnh_x_kernel(tc, dyT, hT, ts, wm, offs, out):
 
         def interleave_w(i):
             width = PIECES[i][2] * P
-            if i == 0:
-                w_bf[i] = shared.tile([P, PASSES, width, PACK], BF16, name="w_bf0", align_bytes=64, offset=2 * KIB)
-            else:
-                w_bf[i] = ring.tile([P, PASSES, width, PACK], BF16, name="w_bf%d" % i, tag="w_bf", align_bytes=64)
+            tile = ring.tile([P, PASSES, width, PACK], BF16, name="w_bf%d" % i, tag="w_bf", align_bytes=64)
+            w_bf[i] = tile[:]
             nc.scalar.copy(
-                w_bf[i][:].rearrange("p g (c i) t -> p g c t i", i=RUN),
+                w_bf[i].rearrange("p g (c i) t -> p g c t i", i=RUN),
                 raw(i).rearrange("p g t (c i) -> p g c t i", i=RUN),
             )
 
         def quantize_w(i):
             words = PASSES * PIECES[i][2] * P
             if i == 0:
-                w_codes[i] = shared.tile([P, words], U32, name="w_codes0", align_bytes=64, offset=4 * KIB)
+                w_codes[i] = shared.tile([P, words], U32, name="w_codes0", align_bytes=64, offset=2 * KIB)
             else:
                 w_codes[i] = keep.tile([P, words], U32, name="w_codes%d" % i, align_bytes=64)
             w_scales[i] = keep.tile([P, words], U8, name="w_scales%d" % i, align_bytes=64)
             nc.vector.quantize_mx(
                 out=w_codes[i][:].bitcast(E4M3),
                 scales=w_scales[i][:],
-                in_=w_bf[i][:].rearrange("p g c t -> p (g c t)"),
+                in_=w_bf[i].rearrange("p g c t -> p (g c t)"),
             )
 
         acc = {}
@@ -249,7 +261,7 @@ def tile_attend_gex_tnh_x_kernel(tc, dyT, hT, ts, wm, offs, out):
                     out=acc[e, m][:],
                     lhsT=w_codes[i][:, cols].bitcast(E4M3),
                     lhsT_scale=w_scales[i][:, cols],
-                    rhs=dz_codes[g, e][:].bitcast(E5M2),
+                    rhs=dz_codes[g, e].bitcast(E5M2),
                     rhs_scale=dz_scales[g, e][:],
                     start=(g == 0),
                     stop=(g == PASSES - 1),
@@ -278,9 +290,12 @@ def tile_attend_gex_tnh_x_kernel(tc, dyT, hT, ts, wm, offs, out):
             weigh_turned(e)
         for j in range(PLANES):
             load_dy(j)
+            if j == PACK + 1:
+                load_w(0)
         for j in range(PACK):
             gather_dy_both(j)
-            load_w(j)
+            if j < PACK - 1:
+                load_w(j + 1)
         interleave_dz(0, 0)
         interleave_dz(0, 1)
         gather_dy(4, 0)
@@ -289,17 +304,17 @@ def tile_attend_gex_tnh_x_kernel(tc, dyT, hT, ts, wm, offs, out):
         load_w(5)
         gather_dy(5, 0)
         quantize_dz(0, 0)
+        interleave_w(0)
         gather_dy(6, 0)
+        quantize_w(0)
         gather_dy(7, 0)
         interleave_dz(1, 0)
         gather_dy(5, 1)
         gather_dy(6, 1)
-        gather_dy(7, 1)
-        interleave_w(0)
-        quantize_dz(1, 0)
-        quantize_w(0)
-        multiply(0, 0)
         quantize_dz(0, 1)
+        quantize_dz(1, 0)
+        multiply(0, 0)
+        gather_dy(7, 1)
         interleave_w(1)
         quantize_w(1)
         multiply(0, 1)

@@ -31,6 +31,7 @@ RUN = 4
 KIB = 1024
 ON_GPSIMD = 5
 TS_ROW = P - 1
+VECTOR_ZEROS = 768
 PIECES = ((0, 0, 1), (0, 1, 1), (0, 2, 1), (0, 3, 1), (1, 0, 2), (1, 2, 2))
 
 
@@ -59,8 +60,9 @@ def tile_attend_gex_tnh_x_kernel(tc, dyT, hT, ts, wm, offs, out):
 
         ts_all = big.tile([P, TOKENS], F32, name="ts_all", offset=64 * KIB)
         nc.sync.dma_start(ts_all[TS_ROW : TS_ROW + 1, :], ts[TS_ROW : TS_ROW + 1, :])
-        nc.vector.memset(ts_all[0:TS_ROW, 0 : TOKENS // 2 - 1], 0.0)
-        nc.vector.memset(ts_all[0:TS_ROW, TOKENS // 2 - 1 : TOKENS], 0.0)
+        nc.gpsimd.memset(ts_all[0:TS_ROW, VECTOR_ZEROS:TOKENS], 0.0)
+        nc.vector.memset(ts_all[0:TS_ROW, 0 : VECTOR_ZEROS - 1], 0.0)
+        nc.vector.memset(ts_all[0:TS_ROW, VECTOR_ZEROS - 1 : VECTOR_ZEROS], 0.0)
         identity = keep.tile([P, P], F32, name="identity")
         distance = keep.tile([P, P], F32, name="distance")
         nc.gpsimd.iota(distance[:], [[-1, P]], base=0, channel_multiplier=1, allow_small_or_imprecise_dtypes=True)
@@ -184,6 +186,9 @@ def tile_attend_gex_tnh_x_kernel(tc, dyT, hT, ts, wm, offs, out):
             elif (g, e) == (1, 1):
                 tile = shared.tile([P, SLOTS * PACK], BF16, name="dz_bf11", align_bytes=64, offset=2 * KIB)
                 dz_bf[g, e] = tile[:]
+            elif (g, e) == (0, 1):
+                tile = big.tile([P, SLOTS * PACK], BF16, name="dz_bf01", align_bytes=64, offset=88 * KIB)
+                dz_bf[g, e] = tile[:]
             else:
                 tile = keep.tile([P, SLOTS * PACK], BF16, name="dz_bf%d%d" % (g, e), align_bytes=64)
                 dz_bf[g, e] = tile[:]
@@ -297,6 +302,7 @@ def tile_attend_gex_tnh_x_kernel(tc, dyT, hT, ts, wm, offs, out):
             if j < PACK - 1:
                 load_w(j + 1)
         interleave_dz(0, 0)
+        interleave_w(0)
         interleave_dz(0, 1)
         gather_dy(4, 0)
         gather_dy(4, 1)
@@ -304,7 +310,6 @@ def tile_attend_gex_tnh_x_kernel(tc, dyT, hT, ts, wm, offs, out):
         load_w(5)
         gather_dy(5, 0)
         quantize_dz(0, 0)
-        interleave_w(0)
         gather_dy(6, 0)
         quantize_w(0)
         gather_dy(7, 0)

@@ -27,12 +27,14 @@ LISTED = EXPERTS * SLOTS
 LIST_COLS = SLOTS // 16
 BLOCKS = SLOTS // P
 D_TILES = D_IN // P
+HALF = SLOTS // 2
 RUN = 4
 KIB = 1024
 ON_GPSIMD = 5
 TS_ROW = P - 1
 VECTOR_ZEROS = 768
-PIECES = ((0, 0, 1), (0, 1, 1), (0, 2, 1), (0, 3, 1), (1, 0, 2), (1, 2, 2))
+PIECES = ((0, 0, 1), (0, 1, 1), (0, 2, 2), (1, 0, 1), (1, 1, 1), (1, 2, 2))
+ORDER = (0, 1, 2, 3, 4, 5, 7, 6)
 
 
 def tile_attend_gex_tnh_x_kernel(tc, dyT, hT, ts, wm, offs, out):
@@ -71,11 +73,11 @@ def tile_attend_gex_tnh_x_kernel(tc, dyT, hT, ts, wm, offs, out):
         windows = [keep.tile([P, TOKENS], F32, name="out%d" % m) for m in range(D_TILES)]
         for window in windows:
             nc.gpsimd.memset(window[:], 0.0)
-        ts_listed = big.tile([P, LISTED], F32, name="ts_listed", offset=112 * KIB)
+        ts_listed = big.tile([P, LISTED], F32, name="ts_listed", offset=108 * KIB)
         for e in range(EXPERTS):
             nc.vector.tensor_copy(ts_listed[:, half(e)], ts_all[:].indirect(slots_of(e)))
 
-        ts_turned = big.tile([P, LISTED + 2 * P], F32, name="ts_turned", offset=99 * KIB + KIB // 2)
+        ts_turned = big.tile([P, LISTED + 2 * P], F32, name="ts_turned", offset=95 * KIB + KIB // 2)
         ts_col = keep.tile([P, EXPERTS * BLOCKS], F32, name="ts_col")
         ts_col_neg = keep.tile([P, EXPERTS * BLOCKS], F32, name="ts_col_neg")
         ts_spread = big.tile([P, LISTED], F32, name="ts_spread", offset=76 * KIB)
@@ -96,54 +98,49 @@ def tile_attend_gex_tnh_x_kernel(tc, dyT, hT, ts, wm, offs, out):
                     nc.tensor.transpose(bank[:, b, :], ts_turned[:, c : c + 1].to_broadcast([P, P]), identity[:])
                 nc.scalar.copy(ts_spread[:, half(e)], bank[:].rearrange("p b s -> p (b s)"))
 
-        dz_first = big.tile([P, PACK, LISTED], F32, name="dz_first", offset=64 * KIB)
-        second_first = keep.tile([P, PACK * SLOTS], F32, name="second_first")
-        second_other = keep.tile([P, (PACK + 1) * SLOTS], F32, name="second_other", align_bytes=64)
-        dz_second = [second_first[:], second_other[:, 0 : PACK * SLOTS]]
+        dz_first = big.tile([P, PACK, LISTED], F32, name="dz_first", align_bytes=64, offset=64 * KIB)
+        dz_second = big.tile([P, PACK * LISTED + SLOTS], F32, name="dz_second", align_bytes=64, offset=120 * KIB)
+        late = dz_second[:, PACK * LISTED - SLOTS : PACK * LISTED + SLOTS]
         factor = {}
         listed = {}
 
         def gather_h(j):
             h = big.tile([P, TOKENS], F32, name="h%d" % j, offset=j * 8 * KIB)
-            nc.sync.dma_start(h[:], plane_rows(hT, j))
-            listed[j] = big.tile([P, LISTED], F32, name="listed%d" % j, offset=(80 + 4 * (j % 3)) * KIB)
+            nc.sync.dma_start(h[:], plane_rows(hT, ORDER[j]))
+            listed[j] = big.tile([P, LISTED], F32, name="listed%d" % j, offset=(80, 84, 120)[j % 3] * KIB)
             nc.vector.tensor_copy(listed[j][:], h[:].indirect(offsets[:]))
 
-        squared = big.tile([P, LISTED], F32, name="squared", offset=112 * KIB)
+        squared = big.tile([P, LISTED], F32, name="squared", offset=108 * KIB)
 
         def weigh_on_gpsimd(j):
-            f = big.tile([P, LISTED], F32, name="factor%d" % j, offset=(92 + 4 * j) * KIB)
+            f = big.tile([P, LISTED], F32, name="factor%d" % j, offset=(88 + 4 * j) * KIB)
             for e in range(EXPERTS):
                 nc.scalar.activation(squared[:, half(e)], listed[j][:, half(e)], SQUARE)
             for e in range(EXPERTS):
                 nc.scalar.activation(f[:, half(e)], squared[:, half(e)], COPY, bias=1.0, scale=-1.0)
             nc.gpsimd.tensor_tensor(f[:], f[:], ts_spread[:], MULT)
-            factor[j] = f[:]
-            for e in range(EXPERTS):
-                factor[j, e] = f[:, half(e)]
+            factor[j] = f
 
         squares = {}
 
         def square(j):
             if j == ON_GPSIMD:
-                kept = big.tile([P, PLANES - ON_GPSIMD, LISTED], F32, name="squares", offset=112 * KIB)
+                kept = big.tile([P, PLANES - ON_GPSIMD, LISTED], F32, name="squares", offset=108 * KIB)
                 for k in range(ON_GPSIMD, PLANES):
                     squares[k] = kept[:, k - ON_GPSIMD, :]
             nc.scalar.activation(squares[j], listed[j][:], SQUARE)
 
         turned_planes = range(ON_GPSIMD, PLANES)
-
-        def factor_place(j, e):
-            if (j, e) == (PLANES - 1, 0):
-                return second_other[:, SLOTS + SLOTS // 2 : 2 * SLOTS + SLOTS // 2]
-            if (j, e) == (PACK + 1, 0):
-                tile = shared.tile([P, SLOTS], F32, name="factor50", align_bytes=64, offset=0)
-                return tile[:]
-            if j == PACK + 2:
-                tile = shared.tile([P, SLOTS], F32, name="factor6%d" % e, align_bytes=64, offset=(2 + 4 * e) * KIB)
-                return tile[:]
-            tile = keep.tile([P, SLOTS], F32, name="factor%d%d" % (j, e))
-            return tile[:]
+        for j in turned_planes:
+            place = (j - ON_GPSIMD) * 4 * KIB
+            if j == PLANES - 2:
+                for e in range(EXPERTS):
+                    tile = shared.tile([P, SLOTS], F32, name="factor%d%d" % (j, e), align_bytes=64, offset=place + e * 2 * KIB)
+                    factor[j, e] = tile[:]
+            else:
+                factor[j] = shared.tile([P, LISTED], F32, name="factor%d" % j, align_bytes=64, offset=place)
+                for e in range(EXPERTS):
+                    factor[j, e] = factor[j][:, half(e)]
 
         def weigh_turned(e):
             weighed = ring.tile([P, BLOCKS, len(turned_planes), P], F32, name="weighed")
@@ -160,60 +157,68 @@ def tile_attend_gex_tnh_x_kernel(tc, dyT, hT, ts, wm, offs, out):
                 back = psum.tile([P, BLOCKS, P], F32, name="back", tag="turn", bufs=5)
                 for b in range(BLOCKS):
                     nc.tensor.transpose(back[:, b, :], weighed[:, b, k, :], identity[:])
-                factor[j, e] = factor_place(j, e)
                 nc.scalar.copy(factor[j, e], back[:].rearrange("p b s -> p (b s)"))
 
         dy = {}
 
         def load_dy(j):
             dy[j] = big.tile([P, TOKENS], F32, name="dy%d" % j, offset=j * 8 * KIB)
-            nc.sync.dma_start(dy[j][:], plane_rows(dyT, j))
+            nc.sync.dma_start(dy[j][:], plane_rows(dyT, ORDER[j]))
 
-        def gather_dy_both(j):
-            nc.vector.tensor_tensor(dz_first[:, j, :], dy[j][:].indirect(offsets[:]), factor[j], MULT)
+        def dz_planes(g):
+            if g == 0:
+                return dz_first[:]
+            return dz_second[:, 0 : PACK * LISTED].rearrange("p (t s) -> p t s", t=PACK)
 
-        def gather_dy(j, e):
-            nc.vector.tensor_tensor(dz_second[e][:, (j - PACK) * SLOTS : (j - PACK + 1) * SLOTS], dy[j][:].indirect(slots_of(e)), factor[j, e], MULT)
+        def last_pair(part):
+            return dz_planes(1)[:, 2 + part, 0:SLOTS].rearrange("p (t s) -> p t s", t=2)
 
-        dz_bf = {}
+        def gather_dy(j, start, stop):
+            g, t = divmod(ORDER[j], PACK)
+            e, inside = divmod(start, SLOTS)
+            if j >= PLANES - 2 and e == 0:
+                dz = last_pair(start // HALF)[:, t - 2, :]
+            else:
+                dz = dz_planes(g)[:, t, start:stop]
+            if j >= PLANES - 2:
+                weights = factor[j, e][:, inside : inside + stop - start]
+            else:
+                weights = factor[j][:, start:stop]
+            nc.vector.tensor_tensor(dz, dy[j][:].indirect(offsets[:, start // 16 : stop // 16]), weights, MULT)
+
+        def words(tile, start, count):
+            return tile[:, start * KIB // 4 : (start + count) * KIB // 4]
+
+        arena = {}
+
+        def arena_tile():
+            if not arena:
+                arena[0] = big.tile([P, 32 * KIB // 4], F32, name="arena", align_bytes=64, offset=0)
+            return arena[0]
+
+        first_bf = big.tile([P, SLOTS * PACK], BF16, name="first_bf", align_bytes=64, offset=80 * KIB)
+        dz_bf = {(0, 0): first_bf[:], (1, 0): late.bitcast(BF16)}
+        first_flat = dz_first[:].rearrange("p t s -> p (t s)")
         dz_codes = {}
         dz_scales = {}
 
-        def interleave_dz(g, e):
-            src = dz_first[:, :, half(e)] if g == 0 else dz_second[e].rearrange("p (t s) -> p t s", t=PACK)
-            if (g, e) == (1, 0):
-                dz_bf[g, e] = second_other[:, (PACK - 1) * SLOTS : (PACK + 1) * SLOTS].bitcast(BF16)
-            elif (g, e) == (1, 1):
-                tile = shared.tile([P, SLOTS * PACK], BF16, name="dz_bf11", align_bytes=64, offset=2 * KIB)
-                dz_bf[g, e] = tile[:]
-            elif (g, e) == (0, 1):
-                tile = big.tile([P, SLOTS * PACK], BF16, name="dz_bf01", align_bytes=64, offset=88 * KIB)
-                dz_bf[g, e] = tile[:]
-            else:
-                tile = keep.tile([P, SLOTS * PACK], BF16, name="dz_bf%d%d" % (g, e), align_bytes=64)
-                dz_bf[g, e] = tile[:]
+        def interleave_dz(g, e, places=slice(0, PACK), slots=slice(0, SLOTS), src=None):
+            if src is None:
+                src = dz_planes(g)[:, places, half(e)]
+            dst = dz_bf[g, e].rearrange("p (s t) -> p s t", t=PACK)[:, slots, places]
             nc.scalar.activation(
-                dz_bf[g, e].rearrange("p (c i t) -> p c t i", i=RUN, t=PACK),
+                dst.rearrange("p (c i) t -> p c t i", i=RUN),
                 src.rearrange("p t (c i) -> p c t i", i=RUN),
                 COPY,
             )
 
         def quantize_dz(g, e):
             if (g, e) == (0, 0):
-                tile = shared.tile([P, SLOTS], U32, name="dz_codes00", align_bytes=64, offset=0)
-                dz_codes[g, e] = tile[:]
-            elif (g, e) == (0, 1):
-                tile = shared.tile([P, SLOTS], U32, name="dz_codes01", align_bytes=64, offset=6 * KIB)
-                dz_codes[g, e] = tile[:]
+                dz_codes[g, e] = shared.tile([P, SLOTS], U32, name="dz_codes00", align_bytes=64, offset=2 * KIB)
             else:
-                tile = keep.tile([P, SLOTS], U32, name="dz_codes%d%d" % (g, e), align_bytes=64)
-                dz_codes[g, e] = tile[:]
+                dz_codes[g, e] = keep.tile([P, SLOTS], U32, name="dz_codes%d%d" % (g, e), align_bytes=64)
             dz_scales[g, e] = keep.tile([P, SLOTS], U8, name="dz_scales%d%d" % (g, e), align_bytes=64)
-            nc.vector.quantize_mx(
-                out=dz_codes[g, e].bitcast(E5M2),
-                scales=dz_scales[g, e][:],
-                in_=dz_bf[g, e],
-            )
+            nc.vector.quantize_mx(out=dz_codes[g, e][:].bitcast(E5M2), scales=dz_scales[g, e][:], in_=dz_bf[g, e])
 
         stage = {}
         w_bf = {}
@@ -221,59 +226,65 @@ def tile_attend_gex_tnh_x_kernel(tc, dyT, hT, ts, wm, offs, out):
         w_scales = {}
 
         def raw(i):
-            return stage[i][:].rearrange("p (g t d) -> p g t d", g=PASSES, t=PACK)
+            return stage[i].rearrange("p (g t d) -> p g t d", g=PASSES, t=PACK)
 
         def load_w(i):
             e, m, tiles = PIECES[i]
-            place = (88, 92, 96, 100, 32, 64)[i]
-            stage[i] = big.tile([P, tiles * PLANES * P], F32, name="stage%d" % i, offset=place * KIB)
+            stage[i] = late if i == 0 else words(arena_tile(), (0, 0, 4, 12, 16, 24)[i], 4 * tiles)
             rows = wm[e].rearrange("(g p t) d -> p g t d", g=PASSES, t=PACK)
             for g in range(PASSES):
                 nc.sync.dma_start(raw(i)[:, g, :, :], rows[:, g, :, m * P : (m + tiles) * P])
 
+        def w_bf_place(i):
+            if i == 0:
+                tile = keep.tile([P, SLOTS], F32, name="w_bf0", align_bytes=64)
+                return tile[:]
+            if i == 2:
+                tile = shared.tile([P, 2 * SLOTS], F32, name="w_bf2", align_bytes=64, offset=12 * KIB)
+                return tile[:]
+            if i == 3:
+                return dz_planes(1)[:, 1, half(1)]
+            start, count = {1: (22, 2), 4: (14, 2), 5: (18, 4)}[i]
+            return words(arena_tile(), start, count)
+
         def interleave_w(i):
-            width = PIECES[i][2] * P
-            tile = ring.tile([P, PASSES, width, PACK], BF16, name="w_bf%d" % i, tag="w_bf", align_bytes=64)
-            w_bf[i] = tile[:]
+            w_bf[i] = w_bf_place(i).bitcast(BF16)
             nc.scalar.copy(
-                w_bf[i].rearrange("p g (c i) t -> p g c t i", i=RUN),
+                w_bf[i].rearrange("p (g c i t) -> p g c t i", g=PASSES, i=RUN, t=PACK),
                 raw(i).rearrange("p g t (c i) -> p g c t i", i=RUN),
             )
 
         def quantize_w(i):
-            words = PASSES * PIECES[i][2] * P
+            count = PASSES * PIECES[i][2] * P
             if i == 0:
-                w_codes[i] = shared.tile([P, words], U32, name="w_codes0", align_bytes=64, offset=2 * KIB)
+                w_codes[i] = shared.tile([P, count], U32, name="w_codes0", align_bytes=64, offset=12 * KIB)
             else:
-                w_codes[i] = keep.tile([P, words], U32, name="w_codes%d" % i, align_bytes=64)
-            w_scales[i] = keep.tile([P, words], U8, name="w_scales%d" % i, align_bytes=64)
-            nc.vector.quantize_mx(
-                out=w_codes[i][:].bitcast(E4M3),
-                scales=w_scales[i][:],
-                in_=w_bf[i].rearrange("p g c t -> p (g c t)"),
-            )
+                w_codes[i] = keep.tile([P, count], U32, name="w_codes%d" % i, align_bytes=64)
+            w_scales[i] = keep.tile([P, count], U8, name="w_scales%d" % i, align_bytes=64)
+            nc.vector.quantize_mx(out=w_codes[i][:].bitcast(E4M3), scales=w_scales[i][:], in_=w_bf[i])
 
         acc = {}
         dx = {}
 
-        def multiply(e, m):
+        def multiply(e, m, passes=range(PASSES)):
             i = [k for k, (pe, pm, tiles) in enumerate(PIECES) if pe == e and pm <= m < pm + tiles][0]
             first, width = PIECES[i][1], PIECES[i][2] * P
-            acc[e, m] = psum.tile([P, SLOTS], F32, name="acc", tag="acc", bufs=3)
-            for g in range(PASSES):
+            if (e, m) not in acc:
+                acc[e, m] = psum.tile([P, SLOTS], F32, name="acc", tag="acc", bufs=3)
+            for g in passes:
                 cols = slice(g * width + (m - first) * P, g * width + (m - first + 1) * P)
                 nc.tensor.matmul_mx(
                     out=acc[e, m][:],
                     lhsT=w_codes[i][:, cols].bitcast(E4M3),
                     lhsT_scale=w_scales[i][:, cols],
-                    rhs=dz_codes[g, e].bitcast(E5M2),
+                    rhs=dz_codes[g, e][:].bitcast(E5M2),
                     rhs_scale=dz_scales[g, e][:],
                     start=(g == 0),
                     stop=(g == PASSES - 1),
                 )
 
-        def drain(e, m, i, start=0):
-            dx[e, m] = stage[i][:, start : start + SLOTS]
+        def drain(e, m, place):
+            dx[e, m] = place
             nc.scalar.copy(dx[e, m], acc[e, m][:])
 
         def scatter(e, m):
@@ -298,56 +309,62 @@ def tile_attend_gex_tnh_x_kernel(tc, dyT, hT, ts, wm, offs, out):
             if j == PACK + 1:
                 load_w(0)
         for j in range(PACK):
-            gather_dy_both(j)
-            if j < PACK - 1:
-                load_w(j + 1)
+            gather_dy(j, 0, LISTED)
+        for i in range(1, len(PIECES)):
+            load_w(i)
         interleave_dz(0, 0)
-        interleave_w(0)
-        interleave_dz(0, 1)
-        gather_dy(4, 0)
-        gather_dy(4, 1)
-        load_w(4)
-        load_w(5)
-        gather_dy(5, 0)
+        gather_dy(4, 0, LISTED)
+        gather_dy(5, 0, LISTED)
         quantize_dz(0, 0)
-        gather_dy(6, 0)
+        interleave_w(0)
+        interleave_dz(1, 0, places=slice(0, 2))
+        for part in range(2):
+            gather_dy(6, part * HALF, (part + 1) * HALF)
         quantize_w(0)
-        gather_dy(7, 0)
-        interleave_dz(1, 0)
-        gather_dy(5, 1)
-        gather_dy(6, 1)
-        quantize_dz(0, 1)
+        multiply(0, 0, passes=[0])
+        for part in range(2):
+            slots = slice(part * HALF, (part + 1) * HALF)
+            gather_dy(7, slots.start, slots.stop)
+            interleave_dz(1, 0, places=slice(2, PACK), slots=slots, src=last_pair(part))
+        gather_dy(7, SLOTS, LISTED)
         quantize_dz(1, 0)
-        multiply(0, 0)
-        gather_dy(7, 1)
+        multiply(0, 0, passes=[1])
+        gather_dy(6, SLOTS, LISTED)
         interleave_w(1)
         quantize_w(1)
         multiply(0, 1)
-        drain(0, 0, 1)
+        drain(0, 0, words(arena_tile(), 0, 2))
         scatter(0, 0)
         interleave_w(2)
         quantize_w(2)
         multiply(0, 2)
-        drain(0, 1, 2)
-        scatter(0, 1)
-        interleave_w(3)
-        quantize_w(3)
         multiply(0, 3)
-        drain(0, 2, 3)
+        drain(0, 1, words(arena_tile(), 4, 2))
+        scatter(0, 1)
+        dz_bf[0, 1] = words(arena_tile(), 6, 4).bitcast(BF16)
+        interleave_dz(0, 1)
+        quantize_dz(0, 1)
+        drain(0, 2, words(first_flat, 10, 2))
         scatter(0, 2)
+        dz_bf[1, 1] = words(first_flat, 2, 4).bitcast(BF16)
         interleave_dz(1, 1)
         quantize_dz(1, 1)
+        interleave_w(3)
+        quantize_w(3)
+        multiply(1, 0)
+        drain(0, 3, words(arena_tile(), 12, 2))
+        scatter(0, 3)
         interleave_w(4)
         quantize_w(4)
-        multiply(1, 0)
         multiply(1, 1)
-        drain(0, 3, 4)
-        scatter(0, 3)
+        drain(1, 0, words(arena_tile(), 16, 2))
+        scatter(1, 0)
+        store(0)
         interleave_w(5)
         quantize_w(5)
         multiply(1, 2)
         multiply(1, 3)
-        for m in range(D_TILES):
-            drain(1, m, 5, m * SLOTS)
+        for m in range(1, D_TILES):
+            drain(1, m, words(arena_tile(), 22 + 2 * m, 2))
             scatter(1, m)
             store(m)

@@ -13,6 +13,7 @@ U8 = mybir.dt.uint8
 E4M3 = mybir.dt.float8_e4m3fn_x4
 E5M2 = mybir.dt.float8_e5m2_x4
 MULT = mybir.AluOpType.mult
+ADD = mybir.AluOpType.add
 COPY = mybir.ActivationFunctionType.Copy
 IDENTITY = mybir.ActivationFunctionType.Identity
 RELU = mybir.ActivationFunctionType.Relu
@@ -31,6 +32,7 @@ HALF = SLOTS // 2
 RUN = 4
 KIB = 1024
 ON_GPSIMD = 5
+WHOLE_ON_GPSIMD = 1
 TS_ROW = P - 1
 VECTOR_ZEROS = 768
 PIECES = ((0, 0, 1), (0, 1, 1), (0, 2, 2), (1, 0, 1), (1, 1, 1), (1, 2, 2))
@@ -70,17 +72,16 @@ def tile_attend_gex_tnh_x_kernel(tc, dyT, hT, ts, wm, offs, out):
         nc.gpsimd.iota(distance[:], [[-1, P]], base=0, channel_multiplier=1, allow_small_or_imprecise_dtypes=True)
         nc.scalar.activation(distance[:], distance[:], SQUARE)
         nc.scalar.activation(identity[:], distance[:], RELU, bias=1.0, scale=-1.0)
-        windows = [keep.tile([P, TOKENS], F32, name="out%d" % m) for m in range(D_TILES)]
+        windows = [keep.tile([P, TOKENS], F32, name="out%d" % m) for m in range(2)]
         for window in windows:
             nc.gpsimd.memset(window[:], 0.0)
         ts_listed = big.tile([P, LISTED], F32, name="ts_listed", offset=108 * KIB)
         for e in range(EXPERTS):
             nc.vector.tensor_copy(ts_listed[:, half(e)], ts_all[:].indirect(slots_of(e)))
 
-        ts_turned = big.tile([P, LISTED + 2 * P], F32, name="ts_turned", offset=95 * KIB + KIB // 2)
         ts_col = keep.tile([P, EXPERTS * BLOCKS], F32, name="ts_col")
         ts_col_neg = keep.tile([P, EXPERTS * BLOCKS], F32, name="ts_col_neg")
-        ts_spread = big.tile([P, LISTED], F32, name="ts_spread", offset=76 * KIB)
+        ts_spread = big.tile([P, LISTED], F32, name="ts_spread", offset=146 * KIB)
 
         def spread_ts():
             for e in range(EXPERTS):
@@ -88,15 +89,13 @@ def tile_attend_gex_tnh_x_kernel(tc, dyT, hT, ts, wm, offs, out):
                 for b in range(BLOCKS):
                     c = e * SLOTS + b * P
                     nc.tensor.transpose(bank[:, b, :], ts_listed[:, c : c + P], identity[:])
-                nc.scalar.copy(ts_turned[:, e * BLOCKS : (e + 1) * BLOCKS], bank[:, :, TS_ROW])
-            nc.scalar.copy(ts_col[:], ts_turned[:, 0 : EXPERTS * BLOCKS])
-            nc.scalar.activation(ts_col_neg[:], ts_turned[:, 0 : EXPERTS * BLOCKS], COPY, scale=-1.0)
-            for e in range(EXPERTS):
+                nc.scalar.copy(ts_col[:, e * BLOCKS : (e + 1) * BLOCKS], bank[:, :, TS_ROW])
                 bank = psum.tile([P, BLOCKS, P], F32, name="turned", tag="turn", bufs=5)
                 for b in range(BLOCKS):
                     c = e * BLOCKS + b
-                    nc.tensor.transpose(bank[:, b, :], ts_turned[:, c : c + 1].to_broadcast([P, P]), identity[:])
+                    nc.tensor.transpose(bank[:, b, :], ts_col[:, c : c + 1].to_broadcast([P, P]), identity[:])
                 nc.scalar.copy(ts_spread[:, half(e)], bank[:].rearrange("p b s -> p (b s)"))
+            nc.scalar.activation(ts_col_neg[:], ts_col[:], COPY, scale=-1.0)
 
         dz_first = big.tile([P, PACK, LISTED], F32, name="dz_first", align_bytes=64, offset=64 * KIB)
         dz_second = big.tile([P, PACK * LISTED + SLOTS], F32, name="dz_second", align_bytes=64, offset=120 * KIB)
@@ -110,16 +109,34 @@ def tile_attend_gex_tnh_x_kernel(tc, dyT, hT, ts, wm, offs, out):
             listed[j] = big.tile([P, LISTED], F32, name="listed%d" % j, offset=(80, 84, 120)[j % 3] * KIB)
             nc.vector.tensor_copy(listed[j][:], h[:].indirect(offsets[:]))
 
+        def pieces(j):
+            if j < ON_GPSIMD:
+                return [(0, LISTED)]
+            if j < PLANES - 2:
+                return [(0, SLOTS), (SLOTS, LISTED)]
+            return [(0, HALF), (HALF, SLOTS), (SLOTS, LISTED)]
+
+        held = {(5, 0): 2, (6, 0): 4}
+        for j in range(ON_GPSIMD, PLANES):
+            for start, stop in pieces(j):
+                name = "factor%d_%d" % (j, start)
+                if (j, start) in held:
+                    factor[j, start] = shared.tile([P, stop - start], F32, name=name, align_bytes=64, offset=held[j, start] * KIB)
+                else:
+                    factor[j, start] = keep.tile([P, stop - start], F32, name=name)
+
         squared = big.tile([P, LISTED], F32, name="squared", offset=108 * KIB)
 
         def weigh_on_gpsimd(j):
-            f = big.tile([P, LISTED], F32, name="factor%d" % j, offset=(88 + 4 * j) * KIB)
+            factor[j, 0] = big.tile([P, LISTED], F32, name="factor%d" % j, offset=(88 + 4 * j) * KIB)
             for e in range(EXPERTS):
                 nc.scalar.activation(squared[:, half(e)], listed[j][:, half(e)], SQUARE)
-            for e in range(EXPERTS):
-                nc.scalar.activation(f[:, half(e)], squared[:, half(e)], COPY, bias=1.0, scale=-1.0)
-            nc.gpsimd.tensor_tensor(f[:], f[:], ts_spread[:], MULT)
-            factor[j] = f
+            if j < WHOLE_ON_GPSIMD:
+                nc.gpsimd.tensor_scalar(factor[j, 0][:], squared[:], -1.0, 1.0, MULT, ADD)
+            else:
+                for e in range(EXPERTS):
+                    nc.scalar.activation(factor[j, 0][:, half(e)], squared[:, half(e)], COPY, bias=1.0, scale=-1.0)
+            nc.gpsimd.tensor_tensor(factor[j, 0][:], factor[j, 0][:], ts_spread[:], MULT)
 
         squares = {}
 
@@ -131,33 +148,26 @@ def tile_attend_gex_tnh_x_kernel(tc, dyT, hT, ts, wm, offs, out):
             nc.scalar.activation(squares[j], listed[j][:], SQUARE)
 
         turned_planes = range(ON_GPSIMD, PLANES)
-        for j in turned_planes:
-            place = (j - ON_GPSIMD) * 4 * KIB
-            if j == PLANES - 2:
-                for e in range(EXPERTS):
-                    tile = shared.tile([P, SLOTS], F32, name="factor%d%d" % (j, e), align_bytes=64, offset=place + e * 2 * KIB)
-                    factor[j, e] = tile[:]
-            else:
-                factor[j] = shared.tile([P, LISTED], F32, name="factor%d" % j, align_bytes=64, offset=place)
-                for e in range(EXPERTS):
-                    factor[j, e] = factor[j][:, half(e)]
 
-        def weigh_turned(e):
-            weighed = ring.tile([P, BLOCKS, len(turned_planes), P], F32, name="weighed")
+        def weigh_turned(group, e):
+            weighed = ring.tile([P, BLOCKS, len(group), P], F32, name="weighed")
             for b in range(BLOCKS):
-                there = psum.tile([P, len(turned_planes), P], F32, name="there", tag="turn", bufs=5)
+                there = psum.tile([P, len(group), P], F32, name="there", tag="turn", bufs=5)
                 c = e * SLOTS + b * P
-                for k, j in enumerate(turned_planes):
+                for k, j in enumerate(group):
                     nc.tensor.transpose(there[:, k, :], squares[j][:, c : c + P], identity[:])
                 c = e * BLOCKS + b
                 nc.scalar.activation(
                     weighed[:, b, :, :], there[:], IDENTITY, bias=ts_col[:, c : c + 1], scale=ts_col_neg[:, c : c + 1]
                 )
-            for k, j in enumerate(turned_planes):
+            for k, j in enumerate(group):
                 back = psum.tile([P, BLOCKS, P], F32, name="back", tag="turn", bufs=5)
                 for b in range(BLOCKS):
                     nc.tensor.transpose(back[:, b, :], weighed[:, b, k, :], identity[:])
-                nc.scalar.copy(factor[j, e], back[:].rearrange("p b s -> p (b s)"))
+                for start, stop in pieces(j):
+                    if start // SLOTS == e:
+                        columns = slice(start - e * SLOTS, stop - e * SLOTS)
+                        nc.scalar.copy(factor[j, start][:], back[:].rearrange("p b s -> p (b s)")[:, columns])
 
         dy = {}
 
@@ -175,16 +185,11 @@ def tile_attend_gex_tnh_x_kernel(tc, dyT, hT, ts, wm, offs, out):
 
         def gather_dy(j, start, stop):
             g, t = divmod(ORDER[j], PACK)
-            e, inside = divmod(start, SLOTS)
-            if j >= PLANES - 2 and e == 0:
+            if j >= PLANES - 2 and start < SLOTS:
                 dz = last_pair(start // HALF)[:, t - 2, :]
             else:
                 dz = dz_planes(g)[:, t, start:stop]
-            if j >= PLANES - 2:
-                weights = factor[j, e][:, inside : inside + stop - start]
-            else:
-                weights = factor[j][:, start:stop]
-            nc.vector.tensor_tensor(dz, dy[j][:].indirect(offsets[:, start // 16 : stop // 16]), weights, MULT)
+            nc.vector.tensor_tensor(dz, dy[j][:].indirect(offsets[:, start // 16 : stop // 16]), factor[j, start][:], MULT)
 
         def words(tile, start, count):
             return tile[:, start * KIB // 4 : (start + count) * KIB // 4]
@@ -196,8 +201,9 @@ def tile_attend_gex_tnh_x_kernel(tc, dyT, hT, ts, wm, offs, out):
                 arena[0] = big.tile([P, 32 * KIB // 4], F32, name="arena", align_bytes=64, offset=0)
             return arena[0]
 
+        dz_bf = {(1, 0): late.bitcast(BF16)}
         first_bf = big.tile([P, SLOTS * PACK], BF16, name="first_bf", align_bytes=64, offset=80 * KIB)
-        dz_bf = {(0, 0): first_bf[:], (1, 0): late.bitcast(BF16)}
+        dz_bf[0, 0] = first_bf[:]
         first_flat = dz_first[:].rearrange("p t s -> p (t s)")
         dz_codes = {}
         dz_scales = {}
@@ -240,7 +246,7 @@ def tile_attend_gex_tnh_x_kernel(tc, dyT, hT, ts, wm, offs, out):
                 tile = keep.tile([P, SLOTS], F32, name="w_bf0", align_bytes=64)
                 return tile[:]
             if i == 2:
-                tile = shared.tile([P, 2 * SLOTS], F32, name="w_bf2", align_bytes=64, offset=12 * KIB)
+                tile = shared.tile([P, 2 * SLOTS], F32, name="w_bf2", align_bytes=64, offset=4 * KIB)
                 return tile[:]
             if i == 3:
                 return dz_planes(1)[:, 1, half(1)]
@@ -257,7 +263,7 @@ def tile_attend_gex_tnh_x_kernel(tc, dyT, hT, ts, wm, offs, out):
         def quantize_w(i):
             count = PASSES * PIECES[i][2] * P
             if i == 0:
-                w_codes[i] = shared.tile([P, count], U32, name="w_codes0", align_bytes=64, offset=12 * KIB)
+                w_codes[i] = shared.tile([P, count], U32, name="w_codes0", align_bytes=64, offset=4 * KIB)
             else:
                 w_codes[i] = keep.tile([P, count], U32, name="w_codes%d" % i, align_bytes=64)
             w_scales[i] = keep.tile([P, count], U8, name="w_scales%d" % i, align_bytes=64)
@@ -302,19 +308,26 @@ def tile_attend_gex_tnh_x_kernel(tc, dyT, hT, ts, wm, offs, out):
                 weigh_on_gpsimd(j)
             else:
                 square(j)
+            if j == ON_GPSIMD:
+                for e in range(EXPERTS):
+                    weigh_turned([j], e)
+        for m in range(2, D_TILES):
+            windows.append(big.tile([P, TOKENS], F32, name="out%d" % m, offset=(140 + 8 * (m - 2)) * KIB))
+            nc.gpsimd.memset(windows[m][:], 0.0)
         for e in range(EXPERTS):
-            weigh_turned(e)
+            weigh_turned(turned_planes[1:], e)
         for j in range(PLANES):
             load_dy(j)
             if j == PACK + 1:
                 load_w(0)
         for j in range(PACK):
             gather_dy(j, 0, LISTED)
+        interleave_dz(0, 0)
         for i in range(1, len(PIECES)):
             load_w(i)
-        interleave_dz(0, 0)
-        gather_dy(4, 0, LISTED)
-        gather_dy(5, 0, LISTED)
+        for j in range(PACK, PACK + 2):
+            for start, stop in pieces(j):
+                gather_dy(j, start, stop)
         quantize_dz(0, 0)
         interleave_w(0)
         interleave_dz(1, 0, places=slice(0, 2))

@@ -106,7 +106,7 @@ def tile_attend_gex_tnh_x_kernel(tc, dyT, hT, ts, wm, offs, out):
         def gather_h(j):
             h = big.tile([P, TOKENS], F32, name="h%d" % j, offset=j * 8 * KIB)
             nc.sync.dma_start(h[:], plane_rows(hT, ORDER[j]))
-            listed[j] = big.tile([P, LISTED], F32, name="listed%d" % j, offset=(80, 84, 120)[j % 3] * KIB)
+            listed[j] = big.tile([P, LISTED], F32, name="listed%d" % j, offset=(80, 84, 120, 80, 84, 156, 80, 84)[j] * KIB)
             nc.vector.tensor_copy(listed[j][:], h[:].indirect(offsets[:]))
 
         def pieces(j):
@@ -116,7 +116,7 @@ def tile_attend_gex_tnh_x_kernel(tc, dyT, hT, ts, wm, offs, out):
                 return [(0, SLOTS), (SLOTS, LISTED)]
             return [(0, HALF), (HALF, SLOTS), (SLOTS, LISTED)]
 
-        held = {(5, 0): 2, (6, 0): 4}
+        held = {(5, 0): 2, (6, 0): 8}
         for j in range(ON_GPSIMD, PLANES):
             for start, stop in pieces(j):
                 name = "factor%d_%d" % (j, start)
@@ -202,9 +202,9 @@ def tile_attend_gex_tnh_x_kernel(tc, dyT, hT, ts, wm, offs, out):
             return arena[0]
 
         dz_bf = {(1, 0): late.bitcast(BF16)}
-        first_bf = big.tile([P, SLOTS * PACK], BF16, name="first_bf", align_bytes=64, offset=80 * KIB)
-        dz_bf[0, 0] = first_bf[:]
-        first_flat = dz_first[:].rearrange("p t s -> p (t s)")
+        for e in range(EXPERTS):
+            tile = big.tile([P, SLOTS * PACK], BF16, name="first_bf%d" % e, align_bytes=64, offset=(80 + 4 * e) * KIB)
+            dz_bf[0, e] = tile[:]
         dz_codes = {}
         dz_scales = {}
 
@@ -219,8 +219,8 @@ def tile_attend_gex_tnh_x_kernel(tc, dyT, hT, ts, wm, offs, out):
             )
 
         def quantize_dz(g, e):
-            if (g, e) == (0, 0):
-                dz_codes[g, e] = shared.tile([P, SLOTS], U32, name="dz_codes00", align_bytes=64, offset=2 * KIB)
+            if g == 0:
+                dz_codes[g, e] = shared.tile([P, SLOTS], U32, name="dz_codes0%d" % e, align_bytes=64, offset=(1 + 7 * e) * KIB)
             else:
                 dz_codes[g, e] = keep.tile([P, SLOTS], U32, name="dz_codes%d%d" % (g, e), align_bytes=64)
             dz_scales[g, e] = keep.tile([P, SLOTS], U8, name="dz_scales%d%d" % (g, e), align_bytes=64)
@@ -246,7 +246,7 @@ def tile_attend_gex_tnh_x_kernel(tc, dyT, hT, ts, wm, offs, out):
                 tile = keep.tile([P, SLOTS], F32, name="w_bf0", align_bytes=64)
                 return tile[:]
             if i == 2:
-                tile = shared.tile([P, 2 * SLOTS], F32, name="w_bf2", align_bytes=64, offset=4 * KIB)
+                tile = shared.tile([P, 2 * SLOTS], F32, name="w_bf2", align_bytes=64, offset=3 * KIB)
                 return tile[:]
             if i == 3:
                 return dz_planes(1)[:, 1, half(1)]
@@ -263,7 +263,7 @@ def tile_attend_gex_tnh_x_kernel(tc, dyT, hT, ts, wm, offs, out):
         def quantize_w(i):
             count = PASSES * PIECES[i][2] * P
             if i == 0:
-                w_codes[i] = shared.tile([P, count], U32, name="w_codes0", align_bytes=64, offset=4 * KIB)
+                w_codes[i] = shared.tile([P, count], U32, name="w_codes0", align_bytes=64, offset=3 * KIB)
             else:
                 w_codes[i] = keep.tile([P, count], U32, name="w_codes%d" % i, align_bytes=64)
             w_scales[i] = keep.tile([P, count], U8, name="w_scales%d" % i, align_bytes=64)
@@ -318,23 +318,25 @@ def tile_attend_gex_tnh_x_kernel(tc, dyT, hT, ts, wm, offs, out):
             weigh_turned(turned_planes[1:], e)
         for j in range(PLANES):
             load_dy(j)
-            if j == PACK + 1:
+            if j == 2:
                 load_w(0)
+        interleave_w(0)
         for j in range(PACK):
             gather_dy(j, 0, LISTED)
-        interleave_dz(0, 0)
+        for e in range(EXPERTS):
+            interleave_dz(0, e)
         for i in range(1, len(PIECES)):
             load_w(i)
         for j in range(PACK, PACK + 2):
             for start, stop in pieces(j):
                 gather_dy(j, start, stop)
         quantize_dz(0, 0)
-        interleave_w(0)
+        quantize_w(0)
+        multiply(0, 0, passes=[0])
         interleave_dz(1, 0, places=slice(0, 2))
         for part in range(2):
             gather_dy(6, part * HALF, (part + 1) * HALF)
-        quantize_w(0)
-        multiply(0, 0, passes=[0])
+        quantize_dz(0, 1)
         for part in range(2):
             slots = slice(part * HALF, (part + 1) * HALF)
             gather_dy(7, slots.start, slots.stop)
@@ -354,14 +356,11 @@ def tile_attend_gex_tnh_x_kernel(tc, dyT, hT, ts, wm, offs, out):
         multiply(0, 3)
         drain(0, 1, words(arena_tile(), 4, 2))
         scatter(0, 1)
-        dz_bf[0, 1] = words(arena_tile(), 6, 4).bitcast(BF16)
-        interleave_dz(0, 1)
-        quantize_dz(0, 1)
-        drain(0, 2, words(first_flat, 10, 2))
-        scatter(0, 2)
-        dz_bf[1, 1] = words(first_flat, 2, 4).bitcast(BF16)
+        dz_bf[1, 1] = words(arena_tile(), 6, 4).bitcast(BF16)
         interleave_dz(1, 1)
         quantize_dz(1, 1)
+        drain(0, 2, dz_planes(1)[:, 0, half(1)])
+        scatter(0, 2)
         interleave_w(3)
         quantize_w(3)
         multiply(1, 0)

@@ -31,7 +31,7 @@ D_TILES = D_IN // P
 HALF = SLOTS // 2
 RUN = 4
 KIB = 1024
-ON_GPSIMD = 5
+ON_GPSIMD = 6
 WHOLE_ON_GPSIMD = 1
 TS_ROW = P - 1
 VECTOR_ZEROS = 768
@@ -72,16 +72,16 @@ def tile_attend_gex_tnh_x_kernel(tc, dyT, hT, ts, wm, offs, out):
         nc.gpsimd.iota(distance[:], [[-1, P]], base=0, channel_multiplier=1, allow_small_or_imprecise_dtypes=True)
         nc.scalar.activation(distance[:], distance[:], SQUARE)
         nc.scalar.activation(identity[:], distance[:], RELU, bias=1.0, scale=-1.0)
-        windows = [keep.tile([P, TOKENS], F32, name="out%d" % m) for m in range(2)]
+        windows = [keep.tile([P, TOKENS], F32, name="out%d" % m) for m in range(D_TILES - 1)]
         for window in windows:
             nc.gpsimd.memset(window[:], 0.0)
-        ts_listed = big.tile([P, LISTED], F32, name="ts_listed", offset=108 * KIB)
+        ts_listed = big.tile([P, LISTED], F32, name="ts_listed", offset=147 * KIB)
         for e in range(EXPERTS):
             nc.vector.tensor_copy(ts_listed[:, half(e)], ts_all[:].indirect(slots_of(e)))
 
         ts_col = keep.tile([P, EXPERTS * BLOCKS], F32, name="ts_col")
         ts_col_neg = keep.tile([P, EXPERTS * BLOCKS], F32, name="ts_col_neg")
-        ts_spread = big.tile([P, LISTED], F32, name="ts_spread", offset=146 * KIB)
+        ts_spread = big.tile([P, LISTED], F32, name="ts_spread", offset=108 * KIB)
 
         def spread_ts():
             for e in range(EXPERTS):
@@ -106,18 +106,18 @@ def tile_attend_gex_tnh_x_kernel(tc, dyT, hT, ts, wm, offs, out):
         def gather_h(j):
             h = big.tile([P, TOKENS], F32, name="h%d" % j, offset=j * 8 * KIB)
             nc.sync.dma_start(h[:], plane_rows(hT, ORDER[j]))
-            listed[j] = big.tile([P, LISTED], F32, name="listed%d" % j, offset=(80, 84, 120, 80, 84, 156, 80, 84)[j] * KIB)
+            listed[j] = big.tile([P, LISTED], F32, name="listed%d" % j, offset=(80, 84, 120)[j % 3] * KIB)
             nc.vector.tensor_copy(listed[j][:], h[:].indirect(offsets[:]))
 
         def pieces(j):
-            if j < ON_GPSIMD:
+            if j <= PACK:
                 return [(0, LISTED)]
             if j < PLANES - 2:
                 return [(0, SLOTS), (SLOTS, LISTED)]
             return [(0, HALF), (HALF, SLOTS), (SLOTS, LISTED)]
 
-        held = {(5, 0): 2, (6, 0): 8}
-        for j in range(ON_GPSIMD, PLANES):
+        held = {(5, 0): 0, (6, 0): 4}
+        for j in range(PACK + 1, PLANES):
             for start, stop in pieces(j):
                 name = "factor%d_%d" % (j, start)
                 if (j, start) in held:
@@ -125,24 +125,31 @@ def tile_attend_gex_tnh_x_kernel(tc, dyT, hT, ts, wm, offs, out):
                 else:
                     factor[j, start] = keep.tile([P, stop - start], F32, name=name)
 
-        squared = big.tile([P, LISTED], F32, name="squared", offset=108 * KIB)
+        squared = big.tile([P, LISTED], F32, name="squared", offset=147 * KIB)
 
         def weigh_on_gpsimd(j):
-            factor[j, 0] = big.tile([P, LISTED], F32, name="factor%d" % j, offset=(88 + 4 * j) * KIB)
+            if j <= PACK:
+                factor[j, 0] = big.tile([P, LISTED], F32, name="factor%d" % j, offset=(88 + 4 * j) * KIB)
+                halves = [factor[j, 0][:, half(e)] for e in range(EXPERTS)]
+            else:
+                halves = [factor[j, e * SLOTS][:] for e in range(EXPERTS)]
             for e in range(EXPERTS):
                 nc.scalar.activation(squared[:, half(e)], listed[j][:, half(e)], SQUARE)
             if j < WHOLE_ON_GPSIMD:
                 nc.gpsimd.tensor_scalar(factor[j, 0][:], squared[:], -1.0, 1.0, MULT, ADD)
             else:
                 for e in range(EXPERTS):
-                    nc.scalar.activation(factor[j, 0][:, half(e)], squared[:, half(e)], COPY, bias=1.0, scale=-1.0)
-            nc.gpsimd.tensor_tensor(factor[j, 0][:], factor[j, 0][:], ts_spread[:], MULT)
+                    nc.scalar.activation(halves[e], squared[:, half(e)], COPY, bias=1.0, scale=-1.0)
+            if j < PACK:
+                nc.gpsimd.tensor_tensor(factor[j, 0][:], factor[j, 0][:], ts_spread[:], MULT)
+            else:
+                nc.gpsimd.tensor_tensor(halves[0], halves[0], ts_spread[:, half(0)], MULT)
 
         squares = {}
 
         def square(j):
             if j == ON_GPSIMD:
-                kept = big.tile([P, PLANES - ON_GPSIMD, LISTED], F32, name="squares", offset=108 * KIB)
+                kept = big.tile([P, PLANES - ON_GPSIMD, LISTED], F32, name="squares", offset=149 * KIB)
                 for k in range(ON_GPSIMD, PLANES):
                     squares[k] = kept[:, k - ON_GPSIMD, :]
             nc.scalar.activation(squares[j], listed[j][:], SQUARE)
@@ -220,11 +227,18 @@ def tile_attend_gex_tnh_x_kernel(tc, dyT, hT, ts, wm, offs, out):
 
         def quantize_dz(g, e):
             if g == 0:
-                dz_codes[g, e] = shared.tile([P, SLOTS], U32, name="dz_codes0%d" % e, align_bytes=64, offset=(1 + 7 * e) * KIB)
+                dz_codes[g, e] = shared.tile([P, SLOTS], U32, name="dz_codes0%d" % e, align_bytes=64, offset=5 * e * KIB // 2)
             else:
                 dz_codes[g, e] = keep.tile([P, SLOTS], U32, name="dz_codes%d%d" % (g, e), align_bytes=64)
             dz_scales[g, e] = keep.tile([P, SLOTS], U8, name="dz_scales%d%d" % (g, e), align_bytes=64)
             nc.vector.quantize_mx(out=dz_codes[g, e][:].bitcast(E5M2), scales=dz_scales[g, e][:], in_=dz_bf[g, e])
+
+        weighted = {}
+
+        def weigh_late(pair):
+            weighted[pair] = shared.tile([P, 2, SLOTS], F32, name="weighted%d" % pair, align_bytes=64, offset=(20, 9)[pair] * KIB // 2)
+            for k in range(2):
+                nc.gpsimd.tensor_tensor(weighted[pair][:, k, :], dz_planes(1)[:, 2 * pair + k, half(1)], ts_spread[:, half(1)], MULT)
 
         stage = {}
         w_bf = {}
@@ -246,11 +260,14 @@ def tile_attend_gex_tnh_x_kernel(tc, dyT, hT, ts, wm, offs, out):
                 tile = keep.tile([P, SLOTS], F32, name="w_bf0", align_bytes=64)
                 return tile[:]
             if i == 2:
-                tile = shared.tile([P, 2 * SLOTS], F32, name="w_bf2", align_bytes=64, offset=3 * KIB)
+                tile = shared.tile([P, 2 * SLOTS], F32, name="w_bf2", align_bytes=64, offset=9 * KIB // 2)
+                return tile[:]
+            if i == 1:
+                tile = shared.tile([P, SLOTS], F32, name="w_bf1", align_bytes=64, offset=10 * KIB)
                 return tile[:]
             if i == 3:
-                return dz_planes(1)[:, 1, half(1)]
-            start, count = {1: (22, 2), 4: (14, 2), 5: (18, 4)}[i]
+                return weighted[1][:, 0, :]
+            start, count = {4: (14, 2), 5: (18, 4)}[i]
             return words(arena_tile(), start, count)
 
         def interleave_w(i):
@@ -263,7 +280,7 @@ def tile_attend_gex_tnh_x_kernel(tc, dyT, hT, ts, wm, offs, out):
         def quantize_w(i):
             count = PASSES * PIECES[i][2] * P
             if i == 0:
-                w_codes[i] = shared.tile([P, count], U32, name="w_codes0", align_bytes=64, offset=3 * KIB)
+                w_codes[i] = shared.tile([P, count], U32, name="w_codes0", align_bytes=64, offset=9 * KIB // 2)
             else:
                 w_codes[i] = keep.tile([P, count], U32, name="w_codes%d" % i, align_bytes=64)
             w_scales[i] = keep.tile([P, count], U8, name="w_scales%d" % i, align_bytes=64)
@@ -308,19 +325,15 @@ def tile_attend_gex_tnh_x_kernel(tc, dyT, hT, ts, wm, offs, out):
                 weigh_on_gpsimd(j)
             else:
                 square(j)
-            if j == ON_GPSIMD:
-                for e in range(EXPERTS):
-                    weigh_turned([j], e)
-        for m in range(2, D_TILES):
-            windows.append(big.tile([P, TOKENS], F32, name="out%d" % m, offset=(140 + 8 * (m - 2)) * KIB))
-            nc.gpsimd.memset(windows[m][:], 0.0)
-        for e in range(EXPERTS):
-            weigh_turned(turned_planes[1:], e)
+        windows.append(big.tile([P, TOKENS], F32, name="out_last", offset=140 * KIB))
+        nc.gpsimd.memset(windows[D_TILES - 1][:], 0.0)
+        weigh_turned(turned_planes, 0)
+        for j in turned_planes:
+            nc.scalar.activation(factor[j, SLOTS][:], squares[j][:, half(1)], COPY, bias=1.0, scale=-1.0)
         for j in range(PLANES):
             load_dy(j)
-            if j == 2:
+            if j == PACK + 1:
                 load_w(0)
-        interleave_w(0)
         for j in range(PACK):
             gather_dy(j, 0, LISTED)
         for e in range(EXPERTS):
@@ -331,12 +344,13 @@ def tile_attend_gex_tnh_x_kernel(tc, dyT, hT, ts, wm, offs, out):
             for start, stop in pieces(j):
                 gather_dy(j, start, stop)
         quantize_dz(0, 0)
-        quantize_w(0)
-        multiply(0, 0, passes=[0])
+        interleave_w(0)
         interleave_dz(1, 0, places=slice(0, 2))
         for part in range(2):
             gather_dy(6, part * HALF, (part + 1) * HALF)
         quantize_dz(0, 1)
+        quantize_w(0)
+        multiply(0, 0, passes=[0])
         for part in range(2):
             slots = slice(part * HALF, (part + 1) * HALF)
             gather_dy(7, slots.start, slots.stop)
@@ -348,19 +362,22 @@ def tile_attend_gex_tnh_x_kernel(tc, dyT, hT, ts, wm, offs, out):
         interleave_w(1)
         quantize_w(1)
         multiply(0, 1)
+        weigh_late(0)
         drain(0, 0, words(arena_tile(), 0, 2))
         scatter(0, 0)
         interleave_w(2)
         quantize_w(2)
         multiply(0, 2)
         multiply(0, 3)
+        weigh_late(1)
         drain(0, 1, words(arena_tile(), 4, 2))
         scatter(0, 1)
         dz_bf[1, 1] = words(arena_tile(), 6, 4).bitcast(BF16)
-        interleave_dz(1, 1)
-        quantize_dz(1, 1)
+        interleave_dz(1, 1, places=slice(0, 2), src=weighted[0][:])
         drain(0, 2, dz_planes(1)[:, 0, half(1)])
         scatter(0, 2)
+        interleave_dz(1, 1, places=slice(2, PACK), src=weighted[1][:])
+        quantize_dz(1, 1)
         interleave_w(3)
         quantize_w(3)
         multiply(1, 0)

@@ -35,7 +35,7 @@ ON_GPSIMD = 6
 WHOLE_ON_GPSIMD = 1
 TS_ROW = P - 1
 VECTOR_ZEROS = 768
-PIECES = ((0, 0, 1), (0, 1, 1), (0, 2, 2), (1, 0, 1), (1, 1, 1), (1, 2, 2))
+PIECES = ((0, (0,), 0, 2), (0, (1,), 0, 1), (0, (1,), 1, 1), (0, (0, 1), 2, 2), (1, (0, 1), 0, 1), (1, (0, 1), 1, 1), (1, (0, 1), 2, 2))
 ORDER = (0, 1, 2, 3, 4, 5, 7, 6)
 
 
@@ -44,7 +44,7 @@ def tile_attend_gex_tnh_x_kernel(tc, dyT, hT, ts, wm, offs, out):
 
     with ExitStack() as ctx:
         keep = ctx.enter_context(tc.tile_pool(name="keep", bufs=1))
-        ring = ctx.enter_context(tc.tile_pool(name="ring", bufs=2))
+        ring = ctx.enter_context(tc.tile_pool(name="ring", bufs=1))
         big = ctx.enter_context(tc.tile_pool(name="big", bufs=1))
         shared = ctx.enter_context(tc.tile_pool(name="shared", bufs=1))
         psum = ctx.enter_context(tc.psum_pool(name="psum", bufs=4))
@@ -75,7 +75,7 @@ def tile_attend_gex_tnh_x_kernel(tc, dyT, hT, ts, wm, offs, out):
         windows = [keep.tile([P, TOKENS], F32, name="out%d" % m) for m in range(D_TILES - 1)]
         for window in windows:
             nc.gpsimd.memset(window[:], 0.0)
-        ts_listed = big.tile([P, LISTED], F32, name="ts_listed", offset=147 * KIB)
+        ts_listed = big.tile([P, LISTED], F32, name="ts_listed", offset=119 * KIB)
         for e in range(EXPERTS):
             nc.vector.tensor_copy(ts_listed[:, half(e)], ts_all[:].indirect(slots_of(e)))
 
@@ -98,15 +98,15 @@ def tile_attend_gex_tnh_x_kernel(tc, dyT, hT, ts, wm, offs, out):
             nc.scalar.activation(ts_col_neg[:], ts_col[:], COPY, scale=-1.0)
 
         dz_first = big.tile([P, PACK, LISTED], F32, name="dz_first", align_bytes=64, offset=64 * KIB)
-        dz_second = big.tile([P, PACK * LISTED + SLOTS], F32, name="dz_second", align_bytes=64, offset=120 * KIB)
-        late = dz_second[:, PACK * LISTED - SLOTS : PACK * LISTED + SLOTS]
+        dz_second = big.tile([P, PACK * LISTED + SLOTS + HALF], F32, name="dz_second", align_bytes=64, offset=138 * KIB)
+        late = dz_second[:, PACK * LISTED - HALF : PACK * LISTED + SLOTS + HALF]
         factor = {}
         listed = {}
 
         def gather_h(j):
             h = big.tile([P, TOKENS], F32, name="h%d" % j, offset=j * 8 * KIB)
             nc.sync.dma_start(h[:], plane_rows(hT, ORDER[j]))
-            listed[j] = big.tile([P, LISTED], F32, name="listed%d" % j, offset=(80, 84, 120)[j % 3] * KIB)
+            listed[j] = big.tile([P, LISTED], F32, name="listed%d" % j, offset=(80, 84, 130)[j % 3] * KIB)
             nc.vector.tensor_copy(listed[j][:], h[:].indirect(offsets[:]))
 
         def pieces(j):
@@ -125,7 +125,7 @@ def tile_attend_gex_tnh_x_kernel(tc, dyT, hT, ts, wm, offs, out):
                 else:
                     factor[j, start] = keep.tile([P, stop - start], F32, name=name)
 
-        squared = big.tile([P, LISTED], F32, name="squared", offset=147 * KIB)
+        squared = big.tile([P, LISTED], F32, name="squared", offset=119 * KIB)
 
         def weigh_on_gpsimd(j):
             if j <= PACK:
@@ -149,7 +149,7 @@ def tile_attend_gex_tnh_x_kernel(tc, dyT, hT, ts, wm, offs, out):
 
         def square(j):
             if j == ON_GPSIMD:
-                kept = big.tile([P, PLANES - ON_GPSIMD, LISTED], F32, name="squares", offset=149 * KIB)
+                kept = big.tile([P, PLANES - ON_GPSIMD, LISTED], F32, name="squares", offset=121 * KIB)
                 for k in range(ON_GPSIMD, PLANES):
                     squares[k] = kept[:, k - ON_GPSIMD, :]
             nc.scalar.activation(squares[j], listed[j][:], SQUARE)
@@ -234,9 +234,15 @@ def tile_attend_gex_tnh_x_kernel(tc, dyT, hT, ts, wm, offs, out):
             nc.vector.quantize_mx(out=dz_codes[g, e][:].bitcast(E5M2), scales=dz_scales[g, e][:], in_=dz_bf[g, e])
 
         weighted = {}
+        after = {}
 
         def weigh_late(pair):
-            weighted[pair] = shared.tile([P, 2, SLOTS], F32, name="weighted%d" % pair, align_bytes=64, offset=(20, 9)[pair] * KIB // 2)
+            if pair == 0:
+                after[0] = shared.tile([P, LISTED], F32, name="after0", align_bytes=64, offset=14 * KIB)
+                weighted[0] = after[0][:].rearrange("p (t s) -> p t s", t=2)
+            else:
+                after[1] = shared.tile([P, 2 * LISTED], F32, name="after1", align_bytes=64, offset=6 * KIB)
+                weighted[1] = after[1][:, 3 * P : 3 * P + LISTED].rearrange("p (t s) -> p t s", t=2)
             for k in range(2):
                 nc.gpsimd.tensor_tensor(weighted[pair][:, k, :], dz_planes(1)[:, 2 * pair + k, half(1)], ts_spread[:, half(1)], MULT)
 
@@ -245,61 +251,67 @@ def tile_attend_gex_tnh_x_kernel(tc, dyT, hT, ts, wm, offs, out):
         w_codes = {}
         w_scales = {}
 
-        def raw(i):
-            return stage[i].rearrange("p (g t d) -> p g t d", g=PASSES, t=PACK)
-
-        def load_w(i):
-            e, m, tiles = PIECES[i]
-            stage[i] = late if i == 0 else words(arena_tile(), (0, 0, 4, 12, 16, 24)[i], 4 * tiles)
-            rows = wm[e].rearrange("(g p t) d -> p g t d", g=PASSES, t=PACK)
-            for g in range(PASSES):
-                nc.sync.dma_start(raw(i)[:, g, :, :], rows[:, g, :, m * P : (m + tiles) * P])
+        def load_w(e, g):
+            if (e, g) == (0, 0):
+                tile = big.tile([P, PACK * D_IN], F32, name="stage00", offset=130 * KIB)
+                stage[e, g] = tile[:]
+            else:
+                stage[e, g] = words(arena_tile(), 8 * (PASSES * e + g - 1), 8)
+            rows = wm[e][g * K_PASS : (g + 1) * K_PASS, :]
+            nc.sync.dma_start(stage[e, g], rows.rearrange("(p t) d -> p (t d)", t=PACK))
 
         def w_bf_place(i):
             if i == 0:
                 tile = keep.tile([P, SLOTS], F32, name="w_bf0", align_bytes=64)
                 return tile[:]
-            if i == 2:
-                tile = shared.tile([P, 2 * SLOTS], F32, name="w_bf2", align_bytes=64, offset=9 * KIB // 2)
-                return tile[:]
             if i == 1:
-                tile = shared.tile([P, SLOTS], F32, name="w_bf1", align_bytes=64, offset=10 * KIB)
+                return dz_second[:, PACK * LISTED - SLOTS : PACK * LISTED - HALF]
+            if i == 2:
+                tile = shared.tile([P, HALF], F32, name="w_bf2", align_bytes=64, offset=14 * KIB)
                 return tile[:]
             if i == 3:
-                return weighted[1][:, 0, :]
-            start, count = {4: (14, 2), 5: (18, 4)}[i]
-            return words(arena_tile(), start, count)
+                tile = shared.tile([P, LISTED], F32, name="w_bf3", align_bytes=64, offset=6 * KIB)
+                return tile[:]
+            if i == 4:
+                return words(arena_tile(), 2, 2)
+            return words(after[1], 2 * (i - 4), 2 * (i - 4))
 
         def interleave_w(i):
+            e, passes, m, tiles = PIECES[i]
             w_bf[i] = w_bf_place(i).bitcast(BF16)
-            nc.scalar.copy(
-                w_bf[i].rearrange("p (g c i t) -> p g c t i", g=PASSES, i=RUN, t=PACK),
-                raw(i).rearrange("p g t (c i) -> p g c t i", i=RUN),
-            )
+            grouped = w_bf[i].rearrange("p (g c i t) -> p g c t i", g=len(passes), i=RUN, t=PACK)
+            for k, g in enumerate(passes):
+                columns = stage[e, g].rearrange("p (t d) -> p t d", t=PACK)[:, :, m * P : (m + tiles) * P]
+                nc.scalar.copy(grouped[:, k], columns.rearrange("p t (c i) -> p c t i", i=RUN))
 
         def quantize_w(i):
-            count = PASSES * PIECES[i][2] * P
-            if i == 0:
-                w_codes[i] = shared.tile([P, count], U32, name="w_codes0", align_bytes=64, offset=9 * KIB // 2)
+            e, passes, m, tiles = PIECES[i]
+            count = len(passes) * tiles * P
+            if i == 1:
+                codes = shared.tile([P, count], U32, name="w_codes1", align_bytes=64, offset=6 * KIB)
+            elif i == 0:
+                codes = shared.tile([P, count], U32, name="w_codes0", align_bytes=64, offset=9 * KIB // 2)
             else:
-                w_codes[i] = keep.tile([P, count], U32, name="w_codes%d" % i, align_bytes=64)
-            w_scales[i] = keep.tile([P, count], U8, name="w_scales%d" % i, align_bytes=64)
-            nc.vector.quantize_mx(out=w_codes[i][:].bitcast(E4M3), scales=w_scales[i][:], in_=w_bf[i])
+                codes = keep.tile([P, count], U32, name="w_codes%d" % i, align_bytes=64)
+            scales = keep.tile([P, count], U8, name="w_scales%d" % i, align_bytes=64)
+            nc.vector.quantize_mx(out=codes[:].bitcast(E4M3), scales=scales[:], in_=w_bf[i])
+            for k, g in enumerate(passes):
+                for n in range(tiles):
+                    cols = slice((k * tiles + n) * P, (k * tiles + n + 1) * P)
+                    w_codes[e, g, m + n] = codes[:, cols]
+                    w_scales[e, g, m + n] = scales[:, cols]
 
         acc = {}
         dx = {}
 
         def multiply(e, m, passes=range(PASSES)):
-            i = [k for k, (pe, pm, tiles) in enumerate(PIECES) if pe == e and pm <= m < pm + tiles][0]
-            first, width = PIECES[i][1], PIECES[i][2] * P
             if (e, m) not in acc:
                 acc[e, m] = psum.tile([P, SLOTS], F32, name="acc", tag="acc", bufs=3)
             for g in passes:
-                cols = slice(g * width + (m - first) * P, g * width + (m - first + 1) * P)
                 nc.tensor.matmul_mx(
                     out=acc[e, m][:],
-                    lhsT=w_codes[i][:, cols].bitcast(E4M3),
-                    lhsT_scale=w_scales[i][:, cols],
+                    lhsT=w_codes[e, g, m].bitcast(E4M3),
+                    lhsT_scale=w_scales[e, g, m],
                     rhs=dz_codes[g, e][:].bitcast(E5M2),
                     rhs_scale=dz_scales[g, e][:],
                     start=(g == 0),
@@ -325,7 +337,7 @@ def tile_attend_gex_tnh_x_kernel(tc, dyT, hT, ts, wm, offs, out):
                 weigh_on_gpsimd(j)
             else:
                 square(j)
-        windows.append(big.tile([P, TOKENS], F32, name="out_last", offset=140 * KIB))
+        windows.append(big.tile([P, TOKENS], F32, name="out_last", offset=112 * KIB))
         nc.gpsimd.memset(windows[D_TILES - 1][:], 0.0)
         weigh_turned(turned_planes, 0)
         for j in turned_planes:
@@ -333,67 +345,72 @@ def tile_attend_gex_tnh_x_kernel(tc, dyT, hT, ts, wm, offs, out):
         for j in range(PLANES):
             load_dy(j)
             if j == PACK + 1:
-                load_w(0)
-        for j in range(PACK):
-            gather_dy(j, 0, LISTED)
-        for e in range(EXPERTS):
-            interleave_dz(0, e)
-        for i in range(1, len(PIECES)):
-            load_w(i)
+                load_w(0, 0)
+        for pair in range(2):
+            for j in range(2 * pair, 2 * pair + 2):
+                gather_dy(j, 0, LISTED)
+            for e in range(EXPERTS):
+                interleave_dz(0, e, places=slice(2 * pair, 2 * pair + 2))
+        load_w(0, 1)
+        for g in range(PASSES):
+            load_w(1, g)
         for j in range(PACK, PACK + 2):
             for start, stop in pieces(j):
                 gather_dy(j, start, stop)
         quantize_dz(0, 0)
-        interleave_w(0)
         interleave_dz(1, 0, places=slice(0, 2))
+        interleave_w(0)
         for part in range(2):
             gather_dy(6, part * HALF, (part + 1) * HALF)
         quantize_dz(0, 1)
         quantize_w(0)
         multiply(0, 0, passes=[0])
+        multiply(0, 1, passes=[0])
         for part in range(2):
             slots = slice(part * HALF, (part + 1) * HALF)
             gather_dy(7, slots.start, slots.stop)
             interleave_dz(1, 0, places=slice(2, PACK), slots=slots, src=last_pair(part))
         gather_dy(7, SLOTS, LISTED)
         quantize_dz(1, 0)
-        multiply(0, 0, passes=[1])
-        gather_dy(6, SLOTS, LISTED)
         interleave_w(1)
         quantize_w(1)
-        multiply(0, 1)
-        weigh_late(0)
-        drain(0, 0, words(arena_tile(), 0, 2))
-        scatter(0, 0)
+        multiply(0, 0, passes=[1])
+        gather_dy(6, SLOTS, LISTED)
         interleave_w(2)
         quantize_w(2)
+        multiply(0, 1, passes=[1])
+        weigh_late(0)
+        drain(0, 0, words(arena_tile(), 24, 2))
+        scatter(0, 0)
+        interleave_w(3)
+        quantize_w(3)
         multiply(0, 2)
         multiply(0, 3)
         weigh_late(1)
-        drain(0, 1, words(arena_tile(), 4, 2))
+        drain(0, 1, words(arena_tile(), 0, 2))
         scatter(0, 1)
-        dz_bf[1, 1] = words(arena_tile(), 6, 4).bitcast(BF16)
-        interleave_dz(1, 1, places=slice(0, 2), src=weighted[0][:])
-        drain(0, 2, dz_planes(1)[:, 0, half(1)])
+        dz_bf[1, 1] = words(arena_tile(), 4, 4).bitcast(BF16)
+        interleave_dz(1, 1, places=slice(0, 2), src=weighted[0])
+        drain(0, 2, words(after[0], 0, 2))
         scatter(0, 2)
-        interleave_dz(1, 1, places=slice(2, PACK), src=weighted[1][:])
-        quantize_dz(1, 1)
-        interleave_w(3)
-        quantize_w(3)
-        multiply(1, 0)
-        drain(0, 3, words(arena_tile(), 12, 2))
-        scatter(0, 3)
         interleave_w(4)
         quantize_w(4)
+        interleave_dz(1, 1, places=slice(2, PACK), src=weighted[1])
+        quantize_dz(1, 1)
+        multiply(1, 0)
+        drain(0, 3, words(after[1], 0, 2))
+        scatter(0, 3)
+        for i in (5, 6):
+            interleave_w(i)
+        quantize_w(5)
         multiply(1, 1)
-        drain(1, 0, words(arena_tile(), 16, 2))
+        drain(1, 0, words(arena_tile(), 26, 2))
         scatter(1, 0)
         store(0)
-        interleave_w(5)
-        quantize_w(5)
+        quantize_w(6)
         multiply(1, 2)
         multiply(1, 3)
         for m in range(1, D_TILES):
-            drain(1, m, words(arena_tile(), 22 + 2 * m, 2))
+            drain(1, m, words(arena_tile(), 8 + 2 * m, 2))
             scatter(1, m)
             store(m)

@@ -15,7 +15,6 @@ E5M2 = mybir.dt.float8_e5m2_x4
 MULT = mybir.AluOpType.mult
 ADD = mybir.AluOpType.add
 COPY = mybir.ActivationFunctionType.Copy
-IDENTITY = mybir.ActivationFunctionType.Identity
 RELU = mybir.ActivationFunctionType.Relu
 SQUARE = mybir.ActivationFunctionType.Square
 
@@ -29,14 +28,14 @@ LIST_COLS = SLOTS // 16
 BLOCKS = SLOTS // P
 D_TILES = D_IN // P
 HALF = SLOTS // 2
-RUN = 4
 KIB = 1024
-ON_GPSIMD = 6
-WHOLE_ON_GPSIMD = 1
+LOAD_PLACES = 6
+RUN = 4
+LEAD = 2
 TS_ROW = P - 1
 VECTOR_ZEROS = 768
-PIECES = ((0, (0,), 0, 2), (0, (1,), 0, 1), (0, (1,), 1, 1), (0, (0, 1), 2, 2), (1, (0, 1), 0, 1), (1, (0, 1), 1, 1), (1, (0, 1), 2, 2))
-ORDER = (0, 1, 2, 3, 4, 5, 7, 6)
+W_COLS = 2 * P
+PIECES = ((0, 0), (0, 1), (1, 0), (1, 1))
 
 
 def tile_attend_gex_tnh_x_kernel(tc, dyT, hT, ts, wm, offs, out):
@@ -46,14 +45,13 @@ def tile_attend_gex_tnh_x_kernel(tc, dyT, hT, ts, wm, offs, out):
         keep = ctx.enter_context(tc.tile_pool(name="keep", bufs=1))
         ring = ctx.enter_context(tc.tile_pool(name="ring", bufs=1))
         big = ctx.enter_context(tc.tile_pool(name="big", bufs=1))
-        shared = ctx.enter_context(tc.tile_pool(name="shared", bufs=1))
-        psum = ctx.enter_context(tc.psum_pool(name="psum", bufs=4))
+        psum = ctx.enter_context(tc.psum_pool(name="psum", bufs=1))
 
         offsets = keep.tile([P, LISTED // 16], U16, name="offsets")
         nc.sync.dma_start(offsets[:], offs)
 
-        def slots_of(e):
-            return offsets[:, e * LIST_COLS : (e + 1) * LIST_COLS]
+        def slots_of(e, start=0, stop=SLOTS):
+            return offsets[:, (e * SLOTS + start) // 16 : (e * SLOTS + stop) // 16]
 
         def plane_rows(x, j):
             g, t = divmod(j, PACK)
@@ -62,355 +60,251 @@ def tile_attend_gex_tnh_x_kernel(tc, dyT, hT, ts, wm, offs, out):
         def half(e):
             return slice(e * SLOTS, (e + 1) * SLOTS)
 
-        ts_all = big.tile([P, TOKENS], F32, name="ts_all", offset=64 * KIB)
+        loads = []
+
+        def placed(shape, dtype, name, kib):
+            return big.tile(shape, dtype, name=name, align_bytes=64, offset=kib * KIB)
+
+        def loaded(shape, name):
+            loads.append(name)
+            return placed(shape, F32, name, 8 * ((len(loads) - 1) % LOAD_PLACES))
+
+        def in_runs(planes):
+            return planes.rearrange("p t (c i) -> p c t i", i=RUN)
+
+        def woven(tile):
+            return tile.rearrange("p (c i t) -> p c t i", i=RUN, t=PACK)
+
+        identity = keep.tile([P, P], F32, name="identity")
+        distance = placed([P, P], F32, "distance", 88)
+        nc.gpsimd.iota(distance[:], [[-1, P]], base=0, channel_multiplier=1, allow_small_or_imprecise_dtypes=True)
+        nc.scalar.activation(distance[:], distance[:], SQUARE)
+        nc.scalar.activation(identity[:], distance[:], RELU, bias=1.0, scale=-1.0)
+        ts_all = placed([P, TOKENS], F32, "ts_all", 80)
         nc.sync.dma_start(ts_all[TS_ROW : TS_ROW + 1, :], ts[TS_ROW : TS_ROW + 1, :])
         nc.gpsimd.memset(ts_all[0:TS_ROW, VECTOR_ZEROS:TOKENS], 0.0)
         nc.vector.memset(ts_all[0:TS_ROW, 0 : VECTOR_ZEROS - 1], 0.0)
         nc.vector.memset(ts_all[0:TS_ROW, VECTOR_ZEROS - 1 : VECTOR_ZEROS], 0.0)
-        identity = keep.tile([P, P], F32, name="identity")
-        distance = keep.tile([P, P], F32, name="distance")
-        nc.gpsimd.iota(distance[:], [[-1, P]], base=0, channel_multiplier=1, allow_small_or_imprecise_dtypes=True)
-        nc.scalar.activation(distance[:], distance[:], SQUARE)
-        nc.scalar.activation(identity[:], distance[:], RELU, bias=1.0, scale=-1.0)
-        windows = [keep.tile([P, TOKENS], F32, name="out%d" % m) for m in range(D_TILES - 1)]
+        windows = [keep.tile([P, TOKENS], F32, name="out%d" % m) for m in range(D_TILES)]
         for window in windows:
             nc.gpsimd.memset(window[:], 0.0)
-        ts_listed = big.tile([P, LISTED], F32, name="ts_listed", offset=119 * KIB)
+        ts_listed = keep.tile([P, LISTED], F32, name="ts_listed")
+        minus_ts_col = placed([P, EXPERTS * BLOCKS], F32, "minus_ts_col", 89)
+        minus_ts = []
         for e in range(EXPERTS):
             nc.vector.tensor_copy(ts_listed[:, half(e)], ts_all[:].indirect(slots_of(e)))
-
-        ts_col = keep.tile([P, EXPERTS * BLOCKS], F32, name="ts_col")
-        ts_col_neg = keep.tile([P, EXPERTS * BLOCKS], F32, name="ts_col_neg")
-        ts_spread = big.tile([P, LISTED], F32, name="ts_spread", offset=108 * KIB)
-
-        def spread_ts():
-            for e in range(EXPERTS):
-                bank = psum.tile([P, BLOCKS, P], F32, name="turned", tag="turn", bufs=5)
-                for b in range(BLOCKS):
-                    c = e * SLOTS + b * P
-                    nc.tensor.transpose(bank[:, b, :], ts_listed[:, c : c + P], identity[:])
-                nc.scalar.copy(ts_col[:, e * BLOCKS : (e + 1) * BLOCKS], bank[:, :, TS_ROW])
-                bank = psum.tile([P, BLOCKS, P], F32, name="turned", tag="turn", bufs=5)
-                for b in range(BLOCKS):
-                    c = e * BLOCKS + b
-                    nc.tensor.transpose(bank[:, b, :], ts_col[:, c : c + 1].to_broadcast([P, P]), identity[:])
-                nc.scalar.copy(ts_spread[:, half(e)], bank[:].rearrange("p b s -> p (b s)"))
-            nc.scalar.activation(ts_col_neg[:], ts_col[:], COPY, scale=-1.0)
-
-        dz_first = big.tile([P, PACK, LISTED], F32, name="dz_first", align_bytes=64, offset=64 * KIB)
-        dz_second = big.tile([P, PACK * LISTED + SLOTS + HALF], F32, name="dz_second", align_bytes=64, offset=138 * KIB)
-        late = dz_second[:, PACK * LISTED - HALF : PACK * LISTED + SLOTS + HALF]
-        factor = {}
-        listed = {}
-
-        def gather_h(j):
-            h = big.tile([P, TOKENS], F32, name="h%d" % j, offset=j * 8 * KIB)
-            nc.sync.dma_start(h[:], plane_rows(hT, ORDER[j]))
-            listed[j] = big.tile([P, LISTED], F32, name="listed%d" % j, offset=(80, 84, 130)[j % 3] * KIB)
-            nc.vector.tensor_copy(listed[j][:], h[:].indirect(offsets[:]))
-
-        def pieces(j):
-            if j <= PACK:
-                return [(0, LISTED)]
-            if j < PLANES - 2:
-                return [(0, SLOTS), (SLOTS, LISTED)]
-            return [(0, HALF), (HALF, SLOTS), (SLOTS, LISTED)]
-
-        held = {(5, 0): 0, (6, 0): 4}
-        for j in range(PACK + 1, PLANES):
-            for start, stop in pieces(j):
-                name = "factor%d_%d" % (j, start)
-                if (j, start) in held:
-                    factor[j, start] = shared.tile([P, stop - start], F32, name=name, align_bytes=64, offset=held[j, start] * KIB)
-                else:
-                    factor[j, start] = keep.tile([P, stop - start], F32, name=name)
-
-        squared = big.tile([P, LISTED], F32, name="squared", offset=119 * KIB)
-
-        def weigh_on_gpsimd(j):
-            if j <= PACK:
-                factor[j, 0] = big.tile([P, LISTED], F32, name="factor%d" % j, offset=(88 + 4 * j) * KIB)
-                halves = [factor[j, 0][:, half(e)] for e in range(EXPERTS)]
-            else:
-                halves = [factor[j, e * SLOTS][:] for e in range(EXPERTS)]
-            for e in range(EXPERTS):
-                nc.scalar.activation(squared[:, half(e)], listed[j][:, half(e)], SQUARE)
-            if j < WHOLE_ON_GPSIMD:
-                nc.gpsimd.tensor_scalar(factor[j, 0][:], squared[:], -1.0, 1.0, MULT, ADD)
-            else:
-                for e in range(EXPERTS):
-                    nc.scalar.activation(halves[e], squared[:, half(e)], COPY, bias=1.0, scale=-1.0)
-            if j < PACK:
-                nc.gpsimd.tensor_tensor(factor[j, 0][:], factor[j, 0][:], ts_spread[:], MULT)
-            else:
-                nc.gpsimd.tensor_tensor(halves[0], halves[0], ts_spread[:, half(0)], MULT)
-
-        squares = {}
-
-        def square(j):
-            if j == ON_GPSIMD:
-                kept = big.tile([P, PLANES - ON_GPSIMD, LISTED], F32, name="squares", offset=121 * KIB)
-                for k in range(ON_GPSIMD, PLANES):
-                    squares[k] = kept[:, k - ON_GPSIMD, :]
-            nc.scalar.activation(squares[j], listed[j][:], SQUARE)
-
-        turned_planes = range(ON_GPSIMD, PLANES)
-
-        def weigh_turned(group, e):
-            weighed = ring.tile([P, BLOCKS, len(group), P], F32, name="weighed")
+        for e in range(EXPERTS):
+            bank = psum.tile([P, BLOCKS, P], F32, name="turned", tag="bank", bufs=6)
             for b in range(BLOCKS):
-                there = psum.tile([P, len(group), P], F32, name="there", tag="turn", bufs=5)
                 c = e * SLOTS + b * P
-                for k, j in enumerate(group):
-                    nc.tensor.transpose(there[:, k, :], squares[j][:, c : c + P], identity[:])
+                nc.tensor.transpose(bank[:, b, :], ts_listed[:, c : c + P], identity[:])
+            nc.scalar.activation(minus_ts_col[:, e * BLOCKS : (e + 1) * BLOCKS], bank[:, :, TS_ROW], COPY, scale=-1.0)
+            spread = psum.tile([P, SLOTS], F32, name="minus_ts%d" % e)
+            for b in range(BLOCKS):
                 c = e * BLOCKS + b
-                nc.scalar.activation(
-                    weighed[:, b, :, :], there[:], IDENTITY, bias=ts_col[:, c : c + 1], scale=ts_col_neg[:, c : c + 1]
-                )
-            for k, j in enumerate(group):
-                back = psum.tile([P, BLOCKS, P], F32, name="back", tag="turn", bufs=5)
-                for b in range(BLOCKS):
-                    nc.tensor.transpose(back[:, b, :], weighed[:, b, k, :], identity[:])
-                for start, stop in pieces(j):
-                    if start // SLOTS == e:
-                        columns = slice(start - e * SLOTS, stop - e * SLOTS)
-                        nc.scalar.copy(factor[j, start][:], back[:].rearrange("p b s -> p (b s)")[:, columns])
+                nc.tensor.transpose(spread[:, b * P : (b + 1) * P], minus_ts_col[:, c : c + 1].to_broadcast([P, P]), identity[:])
+            minus_ts.append(spread)
 
+        late_factor = keep.tile([P, PACK, SLOTS], F32, name="late_factor")
+        late_dy = [keep.tile([P, PACK, HALF], F32, name="late_dy%d" % part) for part in range(2)]
+        factor = {}
+
+        def part_of(part):
+            return slice(part * HALF, (part + 1) * HALF)
+
+        def weigh(j):
+            g, t = divmod(j, PACK)
+            h = loaded([P, TOKENS], "h%d" % j)
+            nc.sync.dma_start(h[:], plane_rows(hT, j))
+            if j < 2:
+                squares = placed([P, LISTED], F32, "squares%d" % j, 80 + 8 * j)
+            else:
+                squares = ring.tile([P, LISTED], F32, name="squares%d" % j, tag="squares", bufs=3)
+            for e in range(EXPERTS):
+                if j == 0:
+                    nc.vector.tensor_copy(squares[:, half(e)], h[:].indirect(slots_of(e)))
+                else:
+                    nc.scalar.activation(squares[:, half(e)], h[:].indirect(slots_of(e)), COPY)
+            for e in range(EXPERTS):
+                nc.scalar.activation(squares[:, half(e)], squares[:, half(e)], SQUARE)
+            if j == PLANES - 1:
+                whole = placed([P, SLOTS], F32, "factor_last", 48)
+            else:
+                whole = ring.tile([P, LISTED], F32, name="factor%d" % j, tag="factor", bufs=3)
+            factor[j] = whole
+            for e in range(EXPERTS):
+                place = late_factor[:, t, :] if (g, e) == (1, 1) else whole[:, half(e)]
+                nc.vector.scalar_tensor_tensor(place, squares[:, half(e)], -1.0, minus_ts[e][:], ADD, MULT)
+
+        dz_first = keep.tile([P, PACK, LISTED], F32, name="dz_first")
+        dz_second = [keep.tile([P, PACK, HALF], F32, name="dz_second%d" % part) for part in range(2)]
         dy = {}
 
-        def load_dy(j):
-            dy[j] = big.tile([P, TOKENS], F32, name="dy%d" % j, offset=j * 8 * KIB)
-            nc.sync.dma_start(dy[j][:], plane_rows(dyT, ORDER[j]))
-
-        def dz_planes(g):
+        def gather_dy(j):
+            g, t = divmod(j, PACK)
+            dy[j] = loaded([P, TOKENS], "dy%d" % j)
+            nc.sync.dma_start(dy[j][:], plane_rows(dyT, j))
             if g == 0:
-                return dz_first[:]
-            return dz_second[:, 0 : PACK * LISTED].rearrange("p (t s) -> p t s", t=PACK)
-
-        def last_pair(part):
-            return dz_planes(1)[:, 2 + part, 0:SLOTS].rearrange("p (t s) -> p t s", t=2)
-
-        def gather_dy(j, start, stop):
-            g, t = divmod(ORDER[j], PACK)
-            if j >= PLANES - 2 and start < SLOTS:
-                dz = last_pair(start // HALF)[:, t - 2, :]
+                nc.vector.tensor_tensor(dz_first[:, t, :], dy[j][:].indirect(offsets[:]), factor[j][:], MULT)
             else:
-                dz = dz_planes(g)[:, t, start:stop]
-            nc.vector.tensor_tensor(dz, dy[j][:].indirect(offsets[:, start // 16 : stop // 16]), factor[j, start][:], MULT)
+                for part in range(2):
+                    slots = part_of(part)
+                    nc.vector.tensor_tensor(
+                        dz_second[part][:, t, :], dy[j][:].indirect(slots_of(0, slots.start, slots.stop)), factor[j][:, slots], MULT
+                    )
+                for part in range(2):
+                    slots = part_of(part)
+                    nc.scalar.activation(late_dy[part][:, t, :], dy[j][:].indirect(slots_of(1, slots.start, slots.stop)), COPY)
 
-        def words(tile, start, count):
-            return tile[:, start * KIB // 4 : (start + count) * KIB // 4]
-
-        arena = {}
-
-        def arena_tile():
-            if not arena:
-                arena[0] = big.tile([P, 32 * KIB // 4], F32, name="arena", align_bytes=64, offset=0)
-            return arena[0]
-
-        dz_bf = {(1, 0): late.bitcast(BF16)}
-        for e in range(EXPERTS):
-            tile = big.tile([P, SLOTS * PACK], BF16, name="first_bf%d" % e, align_bytes=64, offset=(80 + 4 * e) * KIB)
-            dz_bf[0, e] = tile[:]
+        dz_bf = {}
         dz_codes = {}
         dz_scales = {}
 
-        def interleave_dz(g, e, places=slice(0, PACK), slots=slice(0, SLOTS), src=None):
-            if src is None:
-                src = dz_planes(g)[:, places, half(e)]
-            dst = dz_bf[g, e].rearrange("p (s t) -> p s t", t=PACK)[:, slots, places]
-            nc.scalar.activation(
-                dst.rearrange("p (c i) t -> p c t i", i=RUN),
-                src.rearrange("p t (c i) -> p c t i", i=RUN),
-                COPY,
-            )
+        def words_of(tile, part):
+            return woven(tile[:, part * HALF * PACK : (part + 1) * HALF * PACK])
+
+        def interleave_first(e):
+            dz_bf[0, e] = keep.tile([P, SLOTS * PACK], BF16, name="dz_bf0%d" % e, align_bytes=64)
+            nc.vector.tensor_copy(woven(dz_bf[0, e][:]), in_runs(dz_first[:, :, half(e)]))
+
+        def interleave_second():
+            dz_bf[1, 0] = keep.tile([P, SLOTS * PACK], BF16, name="dz_bf10", align_bytes=64)
+            nc.scalar.copy(words_of(dz_bf[1, 0], 0), in_runs(dz_second[0][:]))
+            nc.vector.tensor_copy(words_of(dz_bf[1, 0], 1), in_runs(dz_second[1][:]))
 
         def quantize_dz(g, e):
-            if g == 0:
-                dz_codes[g, e] = shared.tile([P, SLOTS], U32, name="dz_codes0%d" % e, align_bytes=64, offset=5 * e * KIB // 2)
-            else:
-                dz_codes[g, e] = keep.tile([P, SLOTS], U32, name="dz_codes%d%d" % (g, e), align_bytes=64)
+            dz_codes[g, e] = placed([P, SLOTS], U32, "dz_codes%d%d" % (g, e), 72 + 4 * g + 2 * e)
             dz_scales[g, e] = keep.tile([P, SLOTS], U8, name="dz_scales%d%d" % (g, e), align_bytes=64)
-            nc.vector.quantize_mx(out=dz_codes[g, e][:].bitcast(E5M2), scales=dz_scales[g, e][:], in_=dz_bf[g, e])
+            nc.vector.quantize_mx(out=dz_codes[g, e][:].bitcast(E5M2), scales=dz_scales[g, e][:], in_=dz_bf[g, e][:])
 
-        weighted = {}
-        after = {}
+        late_bf = {}
 
-        def weigh_late(pair):
-            if pair == 0:
-                after[0] = shared.tile([P, LISTED], F32, name="after0", align_bytes=64, offset=14 * KIB)
-                weighted[0] = after[0][:].rearrange("p (t s) -> p t s", t=2)
-            else:
-                after[1] = shared.tile([P, 2 * LISTED], F32, name="after1", align_bytes=64, offset=6 * KIB)
-                weighted[1] = after[1][:, 3 * P : 3 * P + LISTED].rearrange("p (t s) -> p t s", t=2)
-            for k in range(2):
-                nc.gpsimd.tensor_tensor(weighted[pair][:, k, :], dz_planes(1)[:, 2 * pair + k, half(1)], ts_spread[:, half(1)], MULT)
+        def finish_late(part):
+            late_bf[part] = placed([P, HALF * PACK], BF16, "late_bf%d" % part, (48, 52)[part])
+            nc.vector.tensor_tensor(
+                woven(late_bf[part][:]), in_runs(late_dy[part][:]), in_runs(late_factor[:, :, part_of(part)]), MULT
+            )
+
+        def quantize_late(part):
+            if part == 0:
+                dz_codes[1, 1] = placed([P, SLOTS], U32, "dz_codes11", 56)
+                dz_scales[1, 1] = keep.tile([P, SLOTS], U8, name="dz_scales11", align_bytes=64)
+            slots = part_of(part)
+            nc.vector.quantize_mx(out=dz_codes[1, 1][:, slots].bitcast(E5M2), scales=dz_scales[1, 1][:, slots], in_=late_bf[part][:])
 
         stage = {}
         w_bf = {}
         w_codes = {}
         w_scales = {}
 
-        def load_w(e, g):
-            if (e, g) == (0, 0):
-                tile = big.tile([P, PACK * D_IN], F32, name="stage00", offset=130 * KIB)
-                stage[e, g] = tile[:]
-            else:
-                stage[e, g] = words(arena_tile(), 8 * (PASSES * e + g - 1), 8)
-            rows = wm[e][g * K_PASS : (g + 1) * K_PASS, :]
-            nc.sync.dma_start(stage[e, g], rows.rearrange("(p t) d -> p (t d)", t=PACK))
+        def load_w(i):
+            e, n = PIECES[i]
+            stage[i] = placed([P, PASSES, PACK, W_COLS], F32, "stage%d" % i, 8 * (loads.index("dy%d" % (PACK + i)) % LOAD_PLACES))
+            for g in range(PASSES):
+                rows = wm[e][g * K_PASS : (g + 1) * K_PASS, n * W_COLS : (n + 1) * W_COLS]
+                nc.sync.dma_start(stage[i][:, g], rows.rearrange("(p t) d -> p t d", t=PACK))
 
-        def w_bf_place(i):
-            if i == 0:
-                tile = keep.tile([P, SLOTS], F32, name="w_bf0", align_bytes=64)
-                return tile[:]
-            if i == 1:
-                return dz_second[:, PACK * LISTED - SLOTS : PACK * LISTED - HALF]
-            if i == 2:
-                tile = shared.tile([P, HALF], F32, name="w_bf2", align_bytes=64, offset=14 * KIB)
-                return tile[:]
-            if i == 3:
-                tile = shared.tile([P, LISTED], F32, name="w_bf3", align_bytes=64, offset=6 * KIB)
-                return tile[:]
-            if i == 4:
-                return words(arena_tile(), 2, 2)
-            return words(after[1], 2 * (i - 4), 2 * (i - 4))
+        def interleave_w(i, first, count, copy, kib):
+            w_bf[i, first] = placed([P, PASSES * count * P * PACK], BF16, "w_bf%d%d" % (i, first), kib)
+            copy(
+                w_bf[i, first][:].rearrange("p (g c i t) -> p g c t i", g=PASSES, i=RUN, t=PACK),
+                stage[i][:, :, :, first * P : (first + count) * P].rearrange("p g t (c i) -> p g c t i", i=RUN),
+            )
 
-        def interleave_w(i):
-            e, passes, m, tiles = PIECES[i]
-            w_bf[i] = w_bf_place(i).bitcast(BF16)
-            grouped = w_bf[i].rearrange("p (g c i t) -> p g c t i", g=len(passes), i=RUN, t=PACK)
-            for k, g in enumerate(passes):
-                columns = stage[e, g].rearrange("p (t d) -> p t d", t=PACK)[:, :, m * P : (m + tiles) * P]
-                nc.scalar.copy(grouped[:, k], columns.rearrange("p t (c i) -> p c t i", i=RUN))
-
-        def quantize_w(i):
-            e, passes, m, tiles = PIECES[i]
-            count = len(passes) * tiles * P
-            if i == 1:
-                codes = shared.tile([P, count], U32, name="w_codes1", align_bytes=64, offset=6 * KIB)
-            elif i == 0:
-                codes = shared.tile([P, count], U32, name="w_codes0", align_bytes=64, offset=9 * KIB // 2)
-            else:
-                codes = keep.tile([P, count], U32, name="w_codes%d" % i, align_bytes=64)
-            scales = keep.tile([P, count], U8, name="w_scales%d" % i, align_bytes=64)
-            nc.vector.quantize_mx(out=codes[:].bitcast(E4M3), scales=scales[:], in_=w_bf[i])
-            for k, g in enumerate(passes):
-                for n in range(tiles):
-                    cols = slice((k * tiles + n) * P, (k * tiles + n + 1) * P)
-                    w_codes[e, g, m + n] = codes[:, cols]
-                    w_scales[e, g, m + n] = scales[:, cols]
+        def quantize_w(i, first, count, kib):
+            e, n = PIECES[i]
+            codes = placed([P, PASSES * count * P], U32, "w_codes%d%d" % (i, first), kib)
+            scales = keep.tile([P, PASSES * count * P], U8, name="w_scales%d%d" % (i, first), align_bytes=64)
+            nc.vector.quantize_mx(out=codes[:].bitcast(E4M3), scales=scales[:], in_=w_bf[i, first][:])
+            for g in range(PASSES):
+                for k in range(count):
+                    cols = slice((g * count + k) * P, (g * count + k + 1) * P)
+                    w_codes[e, 2 * n + first + k, g] = codes[:, cols]
+                    w_scales[e, 2 * n + first + k, g] = scales[:, cols]
 
         acc = {}
         dx = {}
 
-        def multiply(e, m, passes=range(PASSES)):
-            if (e, m) not in acc:
-                acc[e, m] = psum.tile([P, SLOTS], F32, name="acc", tag="acc", bufs=3)
-            for g in passes:
+        def multiply(e, m):
+            acc[e, m] = psum.tile([P, SLOTS], F32, name="acc", tag="bank", bufs=6)
+            for g in range(PASSES):
                 nc.tensor.matmul_mx(
                     out=acc[e, m][:],
-                    lhsT=w_codes[e, g, m].bitcast(E4M3),
-                    lhsT_scale=w_scales[e, g, m],
+                    lhsT=w_codes[e, m, g].bitcast(E4M3),
+                    lhsT_scale=w_scales[e, m, g],
                     rhs=dz_codes[g, e][:].bitcast(E5M2),
                     rhs_scale=dz_scales[g, e][:],
                     start=(g == 0),
                     stop=(g == PASSES - 1),
                 )
 
-        def drain(e, m, place):
-            dx[e, m] = place
-            nc.scalar.copy(dx[e, m], acc[e, m][:])
+        def on_vector(e, m):
+            nc.vector.tensor_copy(windows[m][:].indirect(slots_of(e)), dx[e, m][:])
 
-        def scatter(e, m):
-            nc.vector.tensor_copy(windows[m][:].indirect(slots_of(e)), dx[e, m])
+        def drain(e, m, copy, kib):
+            dx[e, m] = placed([P, SLOTS], F32, "dx%d%d" % (e, m), kib)
+            copy(dx[e, m][:], acc[e, m][:])
+
+        def on_scalar(*units):
+            for part in range(2):
+                slots = part_of(part)
+                for e, m in units:
+                    nc.scalar.activation(windows[m][:].indirect(slots_of(e, slots.start, slots.stop)), dx[e, m][:, slots], COPY)
 
         def store(m):
             nc.sync.dma_start(out[m * P : (m + 1) * P, :], windows[m][:])
 
-        spread_ts()
-        gather_h(0)
+        for j in range(LEAD):
+            weigh(j)
         for j in range(PLANES):
-            if j + 1 < PLANES:
-                gather_h(j + 1)
-            if j < ON_GPSIMD:
-                weigh_on_gpsimd(j)
-            else:
-                square(j)
-        windows.append(big.tile([P, TOKENS], F32, name="out_last", offset=112 * KIB))
-        nc.gpsimd.memset(windows[D_TILES - 1][:], 0.0)
-        weigh_turned(turned_planes, 0)
-        for j in turned_planes:
-            nc.scalar.activation(factor[j, SLOTS][:], squares[j][:, half(1)], COPY, bias=1.0, scale=-1.0)
-        for j in range(PLANES):
-            load_dy(j)
-            if j == PACK + 1:
-                load_w(0, 0)
-        for pair in range(2):
-            for j in range(2 * pair, 2 * pair + 2):
-                gather_dy(j, 0, LISTED)
-            for e in range(EXPERTS):
-                interleave_dz(0, e, places=slice(2 * pair, 2 * pair + 2))
-        load_w(0, 1)
-        for g in range(PASSES):
-            load_w(1, g)
-        for j in range(PACK, PACK + 2):
-            for start, stop in pieces(j):
-                gather_dy(j, start, stop)
-        quantize_dz(0, 0)
-        interleave_dz(1, 0, places=slice(0, 2))
-        interleave_w(0)
-        for part in range(2):
-            gather_dy(6, part * HALF, (part + 1) * HALF)
-        quantize_dz(0, 1)
-        quantize_w(0)
-        multiply(0, 0, passes=[0])
-        multiply(0, 1, passes=[0])
-        for part in range(2):
-            slots = slice(part * HALF, (part + 1) * HALF)
-            gather_dy(7, slots.start, slots.stop)
-            interleave_dz(1, 0, places=slice(2, PACK), slots=slots, src=last_pair(part))
-        gather_dy(7, SLOTS, LISTED)
+            if j + LEAD < PLANES:
+                weigh(j + LEAD)
+            gather_dy(j)
+            if j in (PACK, PACK + 1):
+                interleave_first(j - PACK)
+            if j in (PACK + 1, PACK + 2):
+                quantize_dz(0, j - PACK - 1)
+        for i in range(len(PIECES)):
+            load_w(i)
+        interleave_second()
+        interleave_w(0, 1, 1, nc.scalar.copy, 50)
+        interleave_w(0, 0, 1, nc.scalar.copy, 52)
+        finish_late(0)
         quantize_dz(1, 0)
-        interleave_w(1)
-        quantize_w(1)
-        multiply(0, 0, passes=[1])
-        gather_dy(6, SLOTS, LISTED)
-        interleave_w(2)
-        quantize_w(2)
-        multiply(0, 1, passes=[1])
-        weigh_late(0)
-        drain(0, 0, words(arena_tile(), 24, 2))
-        scatter(0, 0)
-        interleave_w(3)
-        quantize_w(3)
-        multiply(0, 2)
+        quantize_w(0, 1, 1, 68)
+        multiply(0, 1)
+        drain(0, 1, nc.scalar.copy, 80)
+        on_scalar((0, 1))
+        interleave_w(1, 0, 2, nc.vector.tensor_copy, 54)
+        quantize_w(0, 0, 1, 69)
+        multiply(0, 0)
+        quantize_w(1, 0, 2, 66)
         multiply(0, 3)
-        weigh_late(1)
-        drain(0, 1, words(arena_tile(), 0, 2))
-        scatter(0, 1)
-        dz_bf[1, 1] = words(arena_tile(), 4, 4).bitcast(BF16)
-        interleave_dz(1, 1, places=slice(0, 2), src=weighted[0])
-        drain(0, 2, words(after[0], 0, 2))
-        scatter(0, 2)
-        interleave_w(4)
-        quantize_w(4)
-        interleave_dz(1, 1, places=slice(2, PACK), src=weighted[1])
-        quantize_dz(1, 1)
-        multiply(1, 0)
-        drain(0, 3, words(after[1], 0, 2))
-        scatter(0, 3)
-        for i in (5, 6):
-            interleave_w(i)
-        quantize_w(5)
+        multiply(0, 2)
+        finish_late(1)
+        quantize_late(0)
+        drain(0, 0, nc.scalar.copy, 66)
+        drain(0, 2, nc.scalar.copy, 82)
+        on_scalar((0, 0), (0, 2))
+        interleave_w(2, 0, 2, nc.vector.tensor_copy, 58)
+        quantize_late(1)
+        quantize_w(2, 0, 2, 84)
         multiply(1, 1)
-        drain(1, 0, words(arena_tile(), 26, 2))
-        scatter(1, 0)
-        store(0)
-        quantize_w(6)
+        multiply(1, 0)
+        interleave_w(3, 0, 2, nc.vector.tensor_copy, 52)
+        quantize_w(3, 0, 2, 70)
         multiply(1, 2)
         multiply(1, 3)
-        for m in range(1, D_TILES):
-            drain(1, m, words(arena_tile(), 8 + 2 * m, 2))
-            scatter(1, m)
+        drain(1, 1, nc.vector.tensor_copy, 84)
+        drain(1, 0, nc.vector.tensor_copy, 62)
+        drain(1, 2, nc.vector.tensor_copy, 64)
+        for m in (1, 0, 2):
+            on_vector(1, m)
             store(m)
+        last = D_TILES - 1
+        both = placed([P, LISTED], F32, "dx_last", 68)
+        for e in range(EXPERTS):
+            nc.scalar.copy(both[:, half(e)], acc[e, last][:])
+        for start, stop in ((0, 384), (384, 768), (768, LISTED)):
+            nc.scalar.activation(windows[last][:].indirect(offsets[:, start // 16 : stop // 16]), both[:, start:stop], COPY)
+        store(last)

@@ -33,7 +33,6 @@ LOAD_PLACES = 6
 RUN = 4
 LEAD = 2
 TS_ROW = P - 1
-VECTOR_ZEROS = 768
 W_COLS = 2 * P
 PIECES = ((0, 0), (0, 1), (1, 0), (1, 1))
 
@@ -76,29 +75,28 @@ def tile_attend_gex_tnh_x_kernel(tc, dyT, hT, ts, wm, offs, out):
             return tile.rearrange("p (c i t) -> p c t i", i=RUN, t=PACK)
 
         identity = keep.tile([P, P], F32, name="identity")
-        distance = placed([P, P], F32, "distance", 88)
+        distance = placed([P, P], F32, "distance", 51)
         nc.gpsimd.iota(distance[:], [[-1, P]], base=0, channel_multiplier=1, allow_small_or_imprecise_dtypes=True)
         nc.scalar.activation(distance[:], distance[:], SQUARE)
         nc.scalar.activation(identity[:], distance[:], RELU, bias=1.0, scale=-1.0)
         ts_all = placed([P, TOKENS], F32, "ts_all", 80)
         nc.sync.dma_start(ts_all[TS_ROW : TS_ROW + 1, :], ts[TS_ROW : TS_ROW + 1, :])
-        nc.gpsimd.memset(ts_all[0:TS_ROW, VECTOR_ZEROS:TOKENS], 0.0)
-        nc.vector.memset(ts_all[0:TS_ROW, 0 : VECTOR_ZEROS - 1], 0.0)
-        nc.vector.memset(ts_all[0:TS_ROW, VECTOR_ZEROS - 1 : VECTOR_ZEROS], 0.0)
+        nc.vector.memset(ts_all[0:TS_ROW, 0 : TOKENS - 1], 0.0)
+        nc.vector.memset(ts_all[0:TS_ROW, TOKENS - 1 : TOKENS], 0.0)
         windows = [keep.tile([P, TOKENS], F32, name="out%d" % m) for m in range(D_TILES)]
         for window in windows:
             nc.gpsimd.memset(window[:], 0.0)
-        ts_listed = keep.tile([P, LISTED], F32, name="ts_listed")
-        minus_ts_col = placed([P, EXPERTS * BLOCKS], F32, "minus_ts_col", 89)
+        ts_listed = placed([P, LISTED], F32, "ts_listed", 50)
+        minus_ts_col = keep.tile([P, EXPERTS * BLOCKS], F32, name="minus_ts_col")
         minus_ts = []
-        for e in range(EXPERTS):
-            nc.vector.tensor_copy(ts_listed[:, half(e)], ts_all[:].indirect(slots_of(e)))
+        nc.vector.tensor_copy(ts_listed[:, half(0)], ts_all[:].indirect(slots_of(0)))
+        nc.scalar.activation(ts_listed[:, half(1)], ts_all[:].indirect(slots_of(1)), COPY)
         for e in range(EXPERTS):
             bank = psum.tile([P, BLOCKS, P], F32, name="turned", tag="bank", bufs=6)
             for b in range(BLOCKS):
                 c = e * SLOTS + b * P
                 nc.tensor.transpose(bank[:, b, :], ts_listed[:, c : c + P], identity[:])
-            nc.scalar.activation(minus_ts_col[:, e * BLOCKS : (e + 1) * BLOCKS], bank[:, :, TS_ROW], COPY, scale=-1.0)
+            nc.vector.tensor_scalar(minus_ts_col[:, e * BLOCKS : (e + 1) * BLOCKS], bank[:, :, TS_ROW], -1.0, None, MULT)
             spread = psum.tile([P, SLOTS], F32, name="minus_ts%d" % e)
             for b in range(BLOCKS):
                 c = e * BLOCKS + b
@@ -106,7 +104,7 @@ def tile_attend_gex_tnh_x_kernel(tc, dyT, hT, ts, wm, offs, out):
             minus_ts.append(spread)
 
         late_factor = keep.tile([P, PACK, SLOTS], F32, name="late_factor")
-        late_dy = [keep.tile([P, PACK, HALF], F32, name="late_dy%d" % part) for part in range(2)]
+        late_dy = keep.tile([P, PACK, SLOTS], F32, name="late_dy")
         factor = {}
 
         def part_of(part):
@@ -116,19 +114,16 @@ def tile_attend_gex_tnh_x_kernel(tc, dyT, hT, ts, wm, offs, out):
             g, t = divmod(j, PACK)
             h = loaded([P, TOKENS], "h%d" % j)
             nc.sync.dma_start(h[:], plane_rows(hT, j))
-            if j < 2:
-                squares = placed([P, LISTED], F32, "squares%d" % j, 80 + 8 * j)
-            else:
-                squares = ring.tile([P, LISTED], F32, name="squares%d" % j, tag="squares", bufs=3)
+            squares = placed([P, LISTED], F32, "squares%d" % j, (84, 52, 56)[j % 3])
             for e in range(EXPERTS):
-                if j == 0:
+                if j == 1:
                     nc.vector.tensor_copy(squares[:, half(e)], h[:].indirect(slots_of(e)))
                 else:
                     nc.scalar.activation(squares[:, half(e)], h[:].indirect(slots_of(e)), COPY)
             for e in range(EXPERTS):
                 nc.scalar.activation(squares[:, half(e)], squares[:, half(e)], SQUARE)
             if j == PLANES - 1:
-                whole = placed([P, SLOTS], F32, "factor_last", 48)
+                whole = placed([P, SLOTS], F32, "factor_last", 97)
             else:
                 whole = ring.tile([P, LISTED], F32, name="factor%d" % j, tag="factor", bufs=3)
             factor[j] = whole
@@ -137,7 +132,7 @@ def tile_attend_gex_tnh_x_kernel(tc, dyT, hT, ts, wm, offs, out):
                 nc.vector.scalar_tensor_tensor(place, squares[:, half(e)], -1.0, minus_ts[e][:], ADD, MULT)
 
         dz_first = keep.tile([P, PACK, LISTED], F32, name="dz_first")
-        dz_second = [keep.tile([P, PACK, HALF], F32, name="dz_second%d" % part) for part in range(2)]
+        dz_second = placed([P, PACK, SLOTS], F32, "dz_second", 104)
         dy = {}
 
         def gather_dy(j):
@@ -147,14 +142,12 @@ def tile_attend_gex_tnh_x_kernel(tc, dyT, hT, ts, wm, offs, out):
             if g == 0:
                 nc.vector.tensor_tensor(dz_first[:, t, :], dy[j][:].indirect(offsets[:]), factor[j][:], MULT)
             else:
-                for part in range(2):
-                    slots = part_of(part)
+                runs = [part_of(0), part_of(1)] if j == PLANES - 1 else [half(0)]
+                for slots in runs:
                     nc.vector.tensor_tensor(
-                        dz_second[part][:, t, :], dy[j][:].indirect(slots_of(0, slots.start, slots.stop)), factor[j][:, slots], MULT
+                        dz_second[:, t, slots], dy[j][:].indirect(slots_of(0, slots.start, slots.stop)), factor[j][:, slots], MULT
                     )
-                for part in range(2):
-                    slots = part_of(part)
-                    nc.scalar.activation(late_dy[part][:, t, :], dy[j][:].indirect(slots_of(1, slots.start, slots.stop)), COPY)
+                nc.scalar.activation(late_dy[:, t, :], dy[j][:].indirect(slots_of(1)), COPY)
 
         dz_bf = {}
         dz_codes = {}
@@ -169,8 +162,8 @@ def tile_attend_gex_tnh_x_kernel(tc, dyT, hT, ts, wm, offs, out):
 
         def interleave_second():
             dz_bf[1, 0] = keep.tile([P, SLOTS * PACK], BF16, name="dz_bf10", align_bytes=64)
-            nc.scalar.copy(words_of(dz_bf[1, 0], 0), in_runs(dz_second[0][:]))
-            nc.vector.tensor_copy(words_of(dz_bf[1, 0], 1), in_runs(dz_second[1][:]))
+            nc.scalar.copy(words_of(dz_bf[1, 0], 0), in_runs(dz_second[:, :, part_of(0)]))
+            nc.vector.tensor_copy(words_of(dz_bf[1, 0], 1), in_runs(dz_second[:, :, part_of(1)]))
 
         def quantize_dz(g, e):
             dz_codes[g, e] = placed([P, SLOTS], U32, "dz_codes%d%d" % (g, e), 72 + 4 * g + 2 * e)
@@ -180,14 +173,14 @@ def tile_attend_gex_tnh_x_kernel(tc, dyT, hT, ts, wm, offs, out):
         late_bf = {}
 
         def finish_late(part):
-            late_bf[part] = placed([P, HALF * PACK], BF16, "late_bf%d" % part, (48, 52)[part])
+            late_bf[part] = placed([P, HALF * PACK], BF16, "late_bf%d" % part, (96, 104)[part])
             nc.vector.tensor_tensor(
-                woven(late_bf[part][:]), in_runs(late_dy[part][:]), in_runs(late_factor[:, :, part_of(part)]), MULT
+                woven(late_bf[part][:]), in_runs(late_dy[:, :, part_of(part)]), in_runs(late_factor[:, :, part_of(part)]), MULT
             )
 
         def quantize_late(part):
             if part == 0:
-                dz_codes[1, 1] = placed([P, SLOTS], U32, "dz_codes11", 56)
+                dz_codes[1, 1] = placed([P, SLOTS], U32, "dz_codes11", 98)
                 dz_scales[1, 1] = keep.tile([P, SLOTS], U8, name="dz_scales11", align_bytes=64)
             slots = part_of(part)
             nc.vector.quantize_mx(out=dz_codes[1, 1][:, slots].bitcast(E5M2), scales=dz_scales[1, 1][:, slots], in_=late_bf[part][:])
@@ -267,15 +260,15 @@ def tile_attend_gex_tnh_x_kernel(tc, dyT, hT, ts, wm, offs, out):
         for i in range(len(PIECES)):
             load_w(i)
         interleave_second()
-        interleave_w(0, 1, 1, nc.scalar.copy, 50)
-        interleave_w(0, 0, 1, nc.scalar.copy, 52)
+        interleave_w(0, 1, 1, nc.scalar.copy, 98)
+        interleave_w(0, 0, 1, nc.scalar.copy, 104)
         finish_late(0)
         quantize_dz(1, 0)
         quantize_w(0, 1, 1, 68)
         multiply(0, 1)
         drain(0, 1, nc.scalar.copy, 80)
         on_scalar((0, 1))
-        interleave_w(1, 0, 2, nc.vector.tensor_copy, 54)
+        interleave_w(1, 0, 2, nc.vector.tensor_copy, 98)
         quantize_w(0, 0, 1, 69)
         multiply(0, 0)
         quantize_w(1, 0, 2, 66)
@@ -286,12 +279,12 @@ def tile_attend_gex_tnh_x_kernel(tc, dyT, hT, ts, wm, offs, out):
         drain(0, 0, nc.scalar.copy, 66)
         drain(0, 2, nc.scalar.copy, 82)
         on_scalar((0, 0), (0, 2))
-        interleave_w(2, 0, 2, nc.vector.tensor_copy, 58)
+        interleave_w(2, 0, 2, nc.vector.tensor_copy, 100)
         quantize_late(1)
         quantize_w(2, 0, 2, 84)
         multiply(1, 1)
         multiply(1, 0)
-        interleave_w(3, 0, 2, nc.vector.tensor_copy, 52)
+        interleave_w(3, 0, 2, nc.vector.tensor_copy, 104)
         quantize_w(3, 0, 2, 70)
         multiply(1, 2)
         multiply(1, 3)

@@ -29,7 +29,11 @@ BLOCKS = SLOTS // P
 D_TILES = D_IN // P
 HALF = SLOTS // 2
 KIB = 1024
-LOAD_PLACES = 6
+LOAD_KIB = {
+    "h0": 8, "h1": 16, "h2": 24, "dy0": 32, "h3": 40, "dy1": 48, "h4": 56, "dy2": 0,
+    "h5": 8, "dy3": 16, "h6": 24, "dy4": 40, "h7": 56, "dy5": 8, "dy6": 28, "dy7": 20,
+    "stage0": 36, "stage1": 44, "stage2": 4, "stage3": 12,
+}
 RUN = 4
 LEAD = 2
 TS_ROW = P - 1
@@ -59,14 +63,11 @@ def tile_attend_gex_tnh_x_kernel(tc, dyT, hT, ts, wm, offs, out):
         def half(e):
             return slice(e * SLOTS, (e + 1) * SLOTS)
 
-        loads = []
-
         def placed(shape, dtype, name, kib):
-            return big.tile(shape, dtype, name=name, align_bytes=64, offset=kib * KIB)
+            return big.tile(shape, dtype, name=name, align_bytes=64, offset=(kib + 16) * KIB)
 
         def loaded(shape, name):
-            loads.append(name)
-            return placed(shape, F32, name, 8 * ((len(loads) - 1) % LOAD_PLACES))
+            return big.tile(shape, F32, name=name, align_bytes=64, offset=LOAD_KIB[name] * KIB)
 
         def in_runs(planes):
             return planes.rearrange("p t (c i) -> p c t i", i=RUN)
@@ -92,12 +93,12 @@ def tile_attend_gex_tnh_x_kernel(tc, dyT, hT, ts, wm, offs, out):
         nc.vector.tensor_copy(ts_listed[:, half(0)], ts_all[:].indirect(slots_of(0)))
         nc.scalar.activation(ts_listed[:, half(1)], ts_all[:].indirect(slots_of(1)), COPY)
         for e in range(EXPERTS):
-            bank = psum.tile([P, BLOCKS, P], F32, name="turned", tag="bank", bufs=6)
+            bank = psum.tile([P, BLOCKS, P], F32, name="turned", tag="bank", bufs=8)
             for b in range(BLOCKS):
                 c = e * SLOTS + b * P
                 nc.tensor.transpose(bank[:, b, :], ts_listed[:, c : c + P], identity[:])
             nc.vector.tensor_scalar(minus_ts_col[:, e * BLOCKS : (e + 1) * BLOCKS], bank[:, :, TS_ROW], -1.0, None, MULT)
-            spread = psum.tile([P, SLOTS], F32, name="minus_ts%d" % e)
+            spread = psum.tile([P, SLOTS], F32, name="minus_ts%d" % e, tag="bank", bufs=8)
             for b in range(BLOCKS):
                 c = e * BLOCKS + b
                 nc.tensor.transpose(spread[:, b * P : (b + 1) * P], minus_ts_col[:, c : c + 1].to_broadcast([P, P]), identity[:])
@@ -192,7 +193,7 @@ def tile_attend_gex_tnh_x_kernel(tc, dyT, hT, ts, wm, offs, out):
 
         def load_w(i):
             e, n = PIECES[i]
-            stage[i] = placed([P, PASSES, PACK, W_COLS], F32, "stage%d" % i, 8 * (loads.index("dy%d" % (PACK + i)) % LOAD_PLACES))
+            stage[i] = loaded([P, PASSES, PACK, W_COLS], "stage%d" % i)
             for g in range(PASSES):
                 rows = wm[e][g * K_PASS : (g + 1) * K_PASS, n * W_COLS : (n + 1) * W_COLS]
                 nc.sync.dma_start(stage[i][:, g], rows.rearrange("(p t) d -> p t d", t=PACK))
@@ -218,15 +219,15 @@ def tile_attend_gex_tnh_x_kernel(tc, dyT, hT, ts, wm, offs, out):
         acc = {}
         dx = {}
 
-        def multiply(e, m):
-            acc[e, m] = psum.tile([P, SLOTS], F32, name="acc", tag="bank", bufs=6)
+        def multiply(e, m, slots=slice(0, SLOTS)):
+            acc[e, m] = psum.tile([P, slots.stop - slots.start], F32, name="acc", tag="bank", bufs=8)
             for g in range(PASSES):
                 nc.tensor.matmul_mx(
                     out=acc[e, m][:],
                     lhsT=w_codes[e, m, g].bitcast(E4M3),
                     lhsT_scale=w_scales[e, m, g],
-                    rhs=dz_codes[g, e][:].bitcast(E5M2),
-                    rhs_scale=dz_scales[g, e][:],
+                    rhs=dz_codes[g, e][:, slots].bitcast(E5M2),
+                    rhs_scale=dz_scales[g, e][:, slots],
                     start=(g == 0),
                     stop=(g == PASSES - 1),
                 )
@@ -265,8 +266,10 @@ def tile_attend_gex_tnh_x_kernel(tc, dyT, hT, ts, wm, offs, out):
         finish_late(0)
         quantize_dz(1, 0)
         quantize_w(0, 1, 1, 68)
-        multiply(0, 1)
-        drain(0, 1, nc.scalar.copy, 80)
+        dx[0, 1] = placed([P, SLOTS], F32, "dx01", 80)
+        for part in range(2):
+            multiply(0, 1, part_of(part))
+            nc.scalar.copy(dx[0, 1][:, part_of(part)], acc[0, 1][:])
         on_scalar((0, 1))
         interleave_w(1, 0, 2, nc.vector.tensor_copy, 98)
         quantize_w(0, 0, 1, 69)
@@ -285,10 +288,10 @@ def tile_attend_gex_tnh_x_kernel(tc, dyT, hT, ts, wm, offs, out):
         multiply(1, 1)
         multiply(1, 0)
         interleave_w(3, 0, 2, nc.vector.tensor_copy, 104)
+        drain(1, 1, nc.vector.tensor_copy, 60)
         quantize_w(3, 0, 2, 70)
         multiply(1, 2)
         multiply(1, 3)
-        drain(1, 1, nc.vector.tensor_copy, 84)
         drain(1, 0, nc.vector.tensor_copy, 62)
         drain(1, 2, nc.vector.tensor_copy, 64)
         for m in (1, 0, 2):

@@ -64,7 +64,7 @@ def tile_attend_gex_tnh_x_kernel(tc, dyT, hT, ts, wm, offs, out):
             return slice(e * SLOTS, (e + 1) * SLOTS)
 
         def placed(shape, dtype, name, kib):
-            return big.tile(shape, dtype, name=name, align_bytes=64, offset=(kib + 16) * KIB)
+            return big.tile(shape, dtype, name=name, align_bytes=64, offset=int((kib + 16) * KIB))
 
         def loaded(shape, name):
             return big.tile(shape, F32, name=name, align_bytes=64, offset=LOAD_KIB[name] * KIB)
@@ -174,14 +174,14 @@ def tile_attend_gex_tnh_x_kernel(tc, dyT, hT, ts, wm, offs, out):
         late_bf = {}
 
         def finish_late(part):
-            late_bf[part] = placed([P, HALF * PACK], BF16, "late_bf%d" % part, (96, 104)[part])
+            late_bf[part] = placed([P, HALF * PACK], BF16, "late_bf%d" % part, (95.5, 99.5)[part])
             nc.vector.tensor_tensor(
                 woven(late_bf[part][:]), in_runs(late_dy[:, :, part_of(part)]), in_runs(late_factor[:, :, part_of(part)]), MULT
             )
 
         def quantize_late(part):
             if part == 0:
-                dz_codes[1, 1] = placed([P, SLOTS], U32, "dz_codes11", 98)
+                dz_codes[1, 1] = placed([P, SLOTS], U32, "dz_codes11", 104)
                 dz_scales[1, 1] = keep.tile([P, SLOTS], U8, name="dz_scales11", align_bytes=64)
             slots = part_of(part)
             nc.vector.quantize_mx(out=dz_codes[1, 1][:, slots].bitcast(E5M2), scales=dz_scales[1, 1][:, slots], in_=late_bf[part][:])
@@ -261,7 +261,7 @@ def tile_attend_gex_tnh_x_kernel(tc, dyT, hT, ts, wm, offs, out):
         for i in range(len(PIECES)):
             load_w(i)
         interleave_second()
-        interleave_w(0, 1, 1, nc.scalar.copy, 98)
+        interleave_w(0, 1, 1, nc.scalar.copy, 98.5)
         interleave_w(0, 0, 1, nc.scalar.copy, 104)
         finish_late(0)
         quantize_dz(1, 0)
@@ -271,23 +271,25 @@ def tile_attend_gex_tnh_x_kernel(tc, dyT, hT, ts, wm, offs, out):
             multiply(0, 1, part_of(part))
             nc.scalar.copy(dx[0, 1][:, part_of(part)], acc[0, 1][:])
         on_scalar((0, 1))
-        interleave_w(1, 0, 2, nc.vector.tensor_copy, 98)
+        finish_late(1)
+        interleave_w(1, 0, 1, nc.vector.tensor_copy, 97.5)
         quantize_w(0, 0, 1, 69)
         multiply(0, 0)
-        quantize_w(1, 0, 2, 66)
-        multiply(0, 3)
+        quantize_w(1, 0, 1, 66)
         multiply(0, 2)
-        finish_late(1)
         quantize_late(0)
-        drain(0, 0, nc.scalar.copy, 66)
+        quantize_late(1)
+        drain(0, 0, nc.scalar.copy, 65)
         drain(0, 2, nc.scalar.copy, 82)
         on_scalar((0, 0), (0, 2))
-        interleave_w(2, 0, 2, nc.vector.tensor_copy, 100)
-        quantize_late(1)
+        interleave_w(1, 1, 1, nc.vector.tensor_copy, 95.5)
+        interleave_w(2, 0, 2, nc.vector.tensor_copy, 99.5)
+        quantize_w(1, 1, 1, 67)
+        multiply(0, 3)
         quantize_w(2, 0, 2, 84)
         multiply(1, 1)
         multiply(1, 0)
-        interleave_w(3, 0, 2, nc.vector.tensor_copy, 104)
+        interleave_w(3, 0, 2, nc.vector.tensor_copy, 93.5)
         drain(1, 1, nc.vector.tensor_copy, 60)
         quantize_w(3, 0, 2, 70)
         multiply(1, 2)

@@ -181,7 +181,7 @@ def tile_attend_gex_tnh_x_kernel(tc, dyT, hT, ts, wm, offs, out):
 
         def quantize_late(part):
             if part == 0:
-                dz_codes[1, 1] = placed([P, SLOTS], U32, "dz_codes11", 104)
+                dz_codes[1, 1] = placed([P, SLOTS], U32, "dz_codes11", 110)
                 dz_scales[1, 1] = keep.tile([P, SLOTS], U8, name="dz_scales11", align_bytes=64)
             slots = part_of(part)
             nc.vector.quantize_mx(out=dz_codes[1, 1][:, slots].bitcast(E5M2), scales=dz_scales[1, 1][:, slots], in_=late_bf[part][:])
@@ -215,6 +215,24 @@ def tile_attend_gex_tnh_x_kernel(tc, dyT, hT, ts, wm, offs, out):
                     cols = slice((g * count + k) * P, (g * count + k + 1) * P)
                     w_codes[e, 2 * n + first + k, g] = codes[:, cols]
                     w_scales[e, 2 * n + first + k, g] = scales[:, cols]
+
+        def interleave_on_gpsimd(place, i, m):
+            for g in range(PASSES):
+                nc.gpsimd.tensor_copy(
+                    place[:, g * P * PACK : (g + 1) * P * PACK].rearrange("p (c t) -> p c t", t=PACK),
+                    stage[i][:, g, :, m * P : (m + 1) * P].rearrange("p t c -> p c t"),
+                )
+
+        def quantize_tiles(rounded, units, kib):
+            name = "".join("%d%d" % unit for unit in units)
+            codes = placed([P, len(units) * PASSES * P], U32, "w_codes_" + name, kib)
+            scales = keep.tile([P, len(units) * PASSES * P], U8, name="w_scales_" + name, align_bytes=64)
+            nc.vector.quantize_mx(out=codes[:].bitcast(E4M3), scales=scales[:], in_=rounded[:])
+            for k, (e, m) in enumerate(units):
+                for g in range(PASSES):
+                    cols = slice((k * PASSES + g) * P, (k * PASSES + g + 1) * P)
+                    w_codes[e, m, g] = codes[:, cols]
+                    w_scales[e, m, g] = scales[:, cols]
 
         acc = {}
         dx = {}
@@ -262,7 +280,7 @@ def tile_attend_gex_tnh_x_kernel(tc, dyT, hT, ts, wm, offs, out):
             load_w(i)
         interleave_second()
         interleave_w(0, 1, 1, nc.scalar.copy, 98.5)
-        interleave_w(0, 0, 1, nc.scalar.copy, 104)
+        interleave_w(0, 0, 1, nc.scalar.copy, 110)
         finish_late(0)
         quantize_dz(1, 0)
         quantize_w(0, 1, 1, 68)
@@ -279,28 +297,37 @@ def tile_attend_gex_tnh_x_kernel(tc, dyT, hT, ts, wm, offs, out):
         multiply(0, 2)
         quantize_late(0)
         quantize_late(1)
-        drain(0, 0, nc.scalar.copy, 65)
-        drain(0, 2, nc.scalar.copy, 82)
-        on_scalar((0, 0), (0, 2))
-        interleave_w(1, 1, 1, nc.vector.tensor_copy, 95.5)
-        interleave_w(2, 0, 2, nc.vector.tensor_copy, 99.5)
-        quantize_w(1, 1, 1, 67)
-        multiply(0, 3)
-        quantize_w(2, 0, 2, 84)
+        interleave_w(2, 1, 1, nc.vector.tensor_copy, 95.5)
+        interleave_w(2, 0, 1, nc.vector.tensor_copy, 99.5)
+        quantize_w(2, 1, 1, 84)
         multiply(1, 1)
+        quantize_w(2, 0, 1, 85)
         multiply(1, 0)
-        interleave_w(3, 0, 2, nc.vector.tensor_copy, 93.5)
-        drain(1, 1, nc.vector.tensor_copy, 60)
-        quantize_w(3, 0, 2, 70)
-        multiply(1, 2)
-        multiply(1, 3)
-        drain(1, 0, nc.vector.tensor_copy, 62)
-        drain(1, 2, nc.vector.tensor_copy, 64)
-        for m in (1, 0, 2):
-            on_vector(1, m)
-            store(m)
+        drain(0, 0, nc.vector.tensor_copy, 94.5)
+        drain(0, 2, nc.scalar.copy, 98)
+        on_scalar((0, 0), (0, 2))
         last = D_TILES - 1
-        both = placed([P, LISTED], F32, "dx_last", 68)
+        tile_words = PASSES * P * PACK
+        for_scalar = placed([P, 2 * tile_words], BF16, "w_bf_last", 100.5)
+        interleave_on_gpsimd(for_scalar[:, 0:tile_words], 1, 1)
+        interleave_on_gpsimd(for_scalar[:, tile_words : 2 * tile_words], 3, 1)
+        for_vector = placed([P, tile_words], BF16, "w_bf_third", 85)
+        interleave_on_gpsimd(for_vector[:], 3, 0)
+        drain(1, 1, nc.vector.tensor_copy, 60)
+        on_vector(1, 1)
+        store(1)
+        quantize_tiles(for_scalar, ((0, last), (1, last)), 70)
+        multiply(0, last)
+        multiply(1, last)
+        drain(1, 0, nc.vector.tensor_copy, -4)
+        quantize_tiles(for_vector, ((1, 2),), 67)
+        multiply(1, 2)
+        on_vector(1, 0)
+        store(0)
+        drain(1, 2, nc.vector.tensor_copy, 62)
+        on_vector(1, 2)
+        store(2)
+        both = placed([P, LISTED], F32, "dx_last", 100.5)
         for e in range(EXPERTS):
             nc.scalar.copy(both[:, half(e)], acc[e, last][:])
         for start, stop in ((0, 384), (384, 768), (768, LISTED)):

@@ -24,21 +24,53 @@ K_PASS = P * PACK
 PASSES = D_OUT // K_PASS
 PLANES = PASSES * PACK
 LISTED = EXPERTS * SLOTS
-LIST_COLS = SLOTS // 16
 BLOCKS = SLOTS // P
 D_TILES = D_IN // P
+LAST_TILE = D_TILES - 1
 HALF = SLOTS // 2
-KIB = 1024
-LOAD_KIB = {
-    "h0": 8, "h1": 16, "h2": 24, "dy0": 32, "h3": 40, "dy1": 48, "h4": 56, "dy2": 0,
-    "h5": 8, "dy3": 16, "h6": 24, "dy4": 40, "h7": 56, "dy5": 8, "dy6": 28, "dy7": 20,
-    "stage0": 36, "stage1": 44, "stage2": 4, "stage3": 12,
-}
+BANKS = 8
 RUN = 4
 LEAD = 2
+H_ON_VECTOR = 1
 TS_ROW = P - 1
-W_COLS = 2 * P
-PIECES = ((0, 0), (0, 1), (1, 0), (1, 1))
+PIECE_TILES = 2
+TILE_WORDS = PASSES * P
+LONG_SCATTER = 384
+KIB = 1024
+
+LOAD_KIB = {
+    "h0": 8, "h1": 16, "h2": 24, "dy0": 32, "h3": 40, "dy1": 48, "h4": 56, "dy2": 0,
+    "h5": 8, "dy3": 16, "h6": 24, "dy4": 40, "h7": 56, "dy5": 8,
+    "dy6": 28, "dy7": 20,
+    "w00": 36, "w01": 44,
+    "w10": 4, "w11": 12,
+}
+DISTANCE_KIB = 67
+TS_LISTED_KIB = 66
+TS_ALL_KIB = 96
+SQUARES_KIB = (100, 68, 72)
+DZ_CODES_KIB = {(0, 0): 88, (0, 1): 90, (1, 0): 92, (1, 1): 126}
+DZ_SECOND_KIB = 120
+LATE_WOVEN_KIB = (20, 26)
+W_WOVEN_KIB = {
+    (0, 1): 25,
+    (0, 0): 126,
+    (0, 2): 24,
+    (1, 1): LATE_WOVEN_KIB[0],
+    (1, 0): LATE_WOVEN_KIB[1],
+    (0, LAST_TILE): 27,
+    (1, 2): 101,
+}
+W_CODES_KIB = {(0, 2): 82, (1, 2): 83, (0, 1): 84, (0, 0): 85, (0, LAST_TILE): 86, (1, 1): 100, (1, 0): 101}
+SUMS_KIB = {
+    (0, 1): 96,
+    (0, 0): 21,
+    (0, 2): 24.5,
+    (1, 1): 76,
+    (1, 0): LOAD_KIB["w11"],
+    (1, 2): 78,
+    (0, LAST_TILE): W_WOVEN_KIB[0, LAST_TILE],
+}
 
 
 def tile_attend_gex_tnh_x_kernel(tc, dyT, hT, ts, wm, offs, out):
@@ -46,188 +78,192 @@ def tile_attend_gex_tnh_x_kernel(tc, dyT, hT, ts, wm, offs, out):
 
     with ExitStack() as ctx:
         keep = ctx.enter_context(tc.tile_pool(name="keep", bufs=1))
-        ring = ctx.enter_context(tc.tile_pool(name="ring", bufs=1))
         big = ctx.enter_context(tc.tile_pool(name="big", bufs=1))
         psum = ctx.enter_context(tc.psum_pool(name="psum", bufs=1))
 
         offsets = keep.tile([P, LISTED // 16], U16, name="offsets")
         nc.sync.dma_start(offsets[:], offs)
 
-        def slots_of(e, start=0, stop=SLOTS):
-            return offsets[:, (e * SLOTS + start) // 16 : (e * SLOTS + stop) // 16]
+        def entries(start, stop):
+            return offsets[:, start // 16 : stop // 16]
 
-        def plane_rows(x, j):
-            g, t = divmod(j, PACK)
-            return x[g * K_PASS : (g + 1) * K_PASS, :].rearrange("(p t) c -> p t c", t=PACK)[:, t, :]
+        def slots_of(e, slots=slice(0, SLOTS)):
+            return entries(e * SLOTS + slots.start, e * SLOTS + slots.stop)
 
-        def half(e):
+        def expert(e):
             return slice(e * SLOTS, (e + 1) * SLOTS)
 
-        def placed(shape, dtype, name, kib):
-            return big.tile(shape, dtype, name=name, align_bytes=64, offset=int((kib + 16) * KIB))
+        def half(part):
+            return slice(part * HALF, (part + 1) * HALF)
 
-        def loaded(shape, name):
-            return big.tile(shape, F32, name=name, align_bytes=64, offset=LOAD_KIB[name] * KIB)
+        def placed(shape, dtype, name, kib):
+            return big.tile(shape, dtype, name=name, align_bytes=64, offset=int(kib * KIB))
+
+        def bank(shape, name):
+            return psum.tile(shape, F32, name=name, tag="bank", bufs=BANKS)
+
+        def load_plane(x, name, j):
+            g, t = divmod(j, PACK)
+            plane = placed([P, TOKENS], F32, name, LOAD_KIB[name])
+            nc.sync.dma_start(plane[:], x[g * K_PASS : (g + 1) * K_PASS, :].rearrange("(p t) c -> p t c", t=PACK)[:, t, :])
+            return plane
 
         def in_runs(planes):
             return planes.rearrange("p t (c i) -> p c t i", i=RUN)
 
-        def woven(tile):
-            return tile.rearrange("p (c i t) -> p c t i", i=RUN, t=PACK)
+        def woven(words):
+            return words.rearrange("p (c i t) -> p c t i", i=RUN, t=PACK)
 
         identity = keep.tile([P, P], F32, name="identity")
-        distance = placed([P, P], F32, "distance", 51)
+        distance = placed([P, P], F32, "distance", DISTANCE_KIB)
         nc.gpsimd.iota(distance[:], [[-1, P]], base=0, channel_multiplier=1, allow_small_or_imprecise_dtypes=True)
         nc.scalar.activation(distance[:], distance[:], SQUARE)
         nc.scalar.activation(identity[:], distance[:], RELU, bias=1.0, scale=-1.0)
-        ts_all = placed([P, TOKENS], F32, "ts_all", 80)
+
+        ts_all = placed([P, TOKENS], F32, "ts_all", TS_ALL_KIB)
         nc.sync.dma_start(ts_all[TS_ROW : TS_ROW + 1, :], ts[TS_ROW : TS_ROW + 1, :])
         nc.vector.memset(ts_all[0:TS_ROW, 0 : TOKENS - 1], 0.0)
         nc.vector.memset(ts_all[0:TS_ROW, TOKENS - 1 : TOKENS], 0.0)
         windows = [keep.tile([P, TOKENS], F32, name="out%d" % m) for m in range(D_TILES)]
         for window in windows:
             nc.gpsimd.memset(window[:], 0.0)
-        ts_listed = placed([P, LISTED], F32, "ts_listed", 50)
+        ts_listed = placed([P, LISTED], F32, "ts_listed", TS_LISTED_KIB)
         minus_ts_col = keep.tile([P, EXPERTS * BLOCKS], F32, name="minus_ts_col")
+        nc.vector.tensor_copy(ts_listed[:, expert(0)], ts_all[:].indirect(slots_of(0)))
+        nc.scalar.activation(ts_listed[:, expert(1)], ts_all[:].indirect(slots_of(1)), COPY)
+
         minus_ts = []
-        nc.vector.tensor_copy(ts_listed[:, half(0)], ts_all[:].indirect(slots_of(0)))
-        nc.scalar.activation(ts_listed[:, half(1)], ts_all[:].indirect(slots_of(1)), COPY)
         for e in range(EXPERTS):
-            bank = psum.tile([P, BLOCKS, P], F32, name="turned", tag="bank", bufs=8)
+            turned = bank([P, BLOCKS, P], "turned")
             for b in range(BLOCKS):
                 c = e * SLOTS + b * P
-                nc.tensor.transpose(bank[:, b, :], ts_listed[:, c : c + P], identity[:])
-            nc.vector.tensor_scalar(minus_ts_col[:, e * BLOCKS : (e + 1) * BLOCKS], bank[:, :, TS_ROW], -1.0, None, MULT)
-            spread = psum.tile([P, SLOTS], F32, name="minus_ts%d" % e, tag="bank", bufs=8)
+                nc.tensor.transpose(turned[:, b, :], ts_listed[:, c : c + P], identity[:])
+            nc.vector.tensor_scalar(minus_ts_col[:, e * BLOCKS : (e + 1) * BLOCKS], turned[:, :, TS_ROW], -1.0, None, MULT)
+            spread = bank([P, SLOTS], "minus_ts%d" % e)
             for b in range(BLOCKS):
                 c = e * BLOCKS + b
                 nc.tensor.transpose(spread[:, b * P : (b + 1) * P], minus_ts_col[:, c : c + 1].to_broadcast([P, P]), identity[:])
             minus_ts.append(spread)
 
-        late_factor = keep.tile([P, PACK, SLOTS], F32, name="late_factor")
+        factors = keep.tile([P, PACK * LISTED], F32, name="factors")
+        late_factor = factors[:].rearrange("p (t s) -> p t s", t=PACK)[:, :, expert(1)]
         late_dy = keep.tile([P, PACK, SLOTS], F32, name="late_dy")
-        factor = {}
 
-        def part_of(part):
-            return slice(part * HALF, (part + 1) * HALF)
+        def factor_of(j, e):
+            g, t = divmod(j, PACK)
+            if e == 1:
+                start = (t if g == 1 else t % 2) * LISTED + SLOTS
+            elif j % 2 == 0:
+                start = 0
+            else:
+                start = (PACK - 1) * LISTED + (0 if j == PLANES - 1 else HALF)
+            return factors[:, start : start + SLOTS]
+
+        squared = {}
+
+        def square(j):
+            h = load_plane(hT, "h%d" % j, j)
+            squares = placed([P, LISTED], F32, "squares%d" % j, SQUARES_KIB[j % len(SQUARES_KIB)])
+            for e in range(EXPERTS):
+                if j == H_ON_VECTOR:
+                    nc.vector.tensor_copy(squares[:, expert(e)], h[:].indirect(slots_of(e)))
+                else:
+                    nc.scalar.activation(squares[:, expert(e)], h[:].indirect(slots_of(e)), COPY)
+            for e in range(EXPERTS):
+                nc.scalar.activation(squares[:, expert(e)], squares[:, expert(e)], SQUARE)
+            squared[j] = squares
 
         def weigh(j):
-            g, t = divmod(j, PACK)
-            h = loaded([P, TOKENS], "h%d" % j)
-            nc.sync.dma_start(h[:], plane_rows(hT, j))
-            squares = placed([P, LISTED], F32, "squares%d" % j, (84, 52, 56)[j % 3])
             for e in range(EXPERTS):
-                if j == 1:
-                    nc.vector.tensor_copy(squares[:, half(e)], h[:].indirect(slots_of(e)))
-                else:
-                    nc.scalar.activation(squares[:, half(e)], h[:].indirect(slots_of(e)), COPY)
-            for e in range(EXPERTS):
-                nc.scalar.activation(squares[:, half(e)], squares[:, half(e)], SQUARE)
-            if j == PLANES - 1:
-                whole = placed([P, SLOTS], F32, "factor_last", 97)
-            else:
-                whole = ring.tile([P, LISTED], F32, name="factor%d" % j, tag="factor", bufs=3)
-            factor[j] = whole
-            for e in range(EXPERTS):
-                place = late_factor[:, t, :] if (g, e) == (1, 1) else whole[:, half(e)]
-                nc.vector.scalar_tensor_tensor(place, squares[:, half(e)], -1.0, minus_ts[e][:], ADD, MULT)
+                nc.vector.scalar_tensor_tensor(factor_of(j, e), squared[j][:, expert(e)], -1.0, minus_ts[e][:], ADD, MULT)
 
         dz_first = keep.tile([P, PACK, LISTED], F32, name="dz_first")
-        dz_second = placed([P, PACK, SLOTS], F32, "dz_second", 104)
-        dy = {}
+        dz_second = placed([P, PACK, SLOTS], F32, "dz_second", DZ_SECOND_KIB)
 
         def gather_dy(j):
             g, t = divmod(j, PACK)
-            dy[j] = loaded([P, TOKENS], "dy%d" % j)
-            nc.sync.dma_start(dy[j][:], plane_rows(dyT, j))
-            if g == 0:
-                nc.vector.tensor_tensor(dz_first[:, t, :], dy[j][:].indirect(offsets[:]), factor[j][:], MULT)
+            dy = load_plane(dyT, "dy%d" % j, j)
+            if g == 0 and j % 2 == 0:
+                nc.vector.tensor_tensor(dz_first[:, t, :], dy[:].indirect(offsets[:]), factors[:, 0:LISTED], MULT)
+            elif g == 0:
+                for e in range(EXPERTS):
+                    nc.vector.tensor_tensor(dz_first[:, t, expert(e)], dy[:].indirect(slots_of(e)), factor_of(j, e), MULT)
             else:
-                runs = [part_of(0), part_of(1)] if j == PLANES - 1 else [half(0)]
+                runs = [half(0), half(1)] if j == PLANES - 1 else [expert(0)]
                 for slots in runs:
-                    nc.vector.tensor_tensor(
-                        dz_second[:, t, slots], dy[j][:].indirect(slots_of(0, slots.start, slots.stop)), factor[j][:, slots], MULT
-                    )
-                nc.scalar.activation(late_dy[:, t, :], dy[j][:].indirect(slots_of(1)), COPY)
+                    nc.vector.tensor_tensor(dz_second[:, t, slots], dy[:].indirect(slots_of(0, slots)), factor_of(j, 0)[:, slots], MULT)
+                nc.scalar.activation(late_dy[:, t, :], dy[:].indirect(slots_of(1)), COPY)
 
-        dz_bf = {}
+        dz_woven = {}
         dz_codes = {}
         dz_scales = {}
+        late_woven = {}
 
-        def words_of(tile, part):
-            return woven(tile[:, part * HALF * PACK : (part + 1) * HALF * PACK])
+        def weave_first(e):
+            dz_woven[0, e] = keep.tile([P, SLOTS * PACK], BF16, name="dz_woven0%d" % e, align_bytes=64)
+            nc.vector.tensor_copy(woven(dz_woven[0, e][:]), in_runs(dz_first[:, :, expert(e)]))
 
-        def interleave_first(e):
-            dz_bf[0, e] = keep.tile([P, SLOTS * PACK], BF16, name="dz_bf0%d" % e, align_bytes=64)
-            nc.vector.tensor_copy(woven(dz_bf[0, e][:]), in_runs(dz_first[:, :, half(e)]))
+        def weave_second():
+            dz_woven[1, 0] = keep.tile([P, SLOTS * PACK], BF16, name="dz_woven10", align_bytes=64)
+            for part, copy in enumerate((nc.scalar.copy, nc.vector.tensor_copy)):
+                words = dz_woven[1, 0][:, part * HALF * PACK : (part + 1) * HALF * PACK]
+                copy(woven(words), in_runs(dz_second[:, :, half(part)]))
 
-        def interleave_second():
-            dz_bf[1, 0] = keep.tile([P, SLOTS * PACK], BF16, name="dz_bf10", align_bytes=64)
-            nc.scalar.copy(words_of(dz_bf[1, 0], 0), in_runs(dz_second[:, :, part_of(0)]))
-            nc.vector.tensor_copy(words_of(dz_bf[1, 0], 1), in_runs(dz_second[:, :, part_of(1)]))
-
-        def quantize_dz(g, e):
-            dz_codes[g, e] = placed([P, SLOTS], U32, "dz_codes%d%d" % (g, e), 72 + 4 * g + 2 * e)
-            dz_scales[g, e] = keep.tile([P, SLOTS], U8, name="dz_scales%d%d" % (g, e), align_bytes=64)
-            nc.vector.quantize_mx(out=dz_codes[g, e][:].bitcast(E5M2), scales=dz_scales[g, e][:], in_=dz_bf[g, e][:])
-
-        late_bf = {}
-
-        def finish_late(part):
-            late_bf[part] = placed([P, HALF * PACK], BF16, "late_bf%d" % part, (95.5, 99.5)[part])
+        def weave_late(part):
+            late_woven[part] = placed([P, HALF * PACK], BF16, "late_woven%d" % part, LATE_WOVEN_KIB[part])
             nc.vector.tensor_tensor(
-                woven(late_bf[part][:]), in_runs(late_dy[:, :, part_of(part)]), in_runs(late_factor[:, :, part_of(part)]), MULT
+                woven(late_woven[part][:]), in_runs(late_dy[:, :, half(part)]), in_runs(late_factor[:, :, half(part)]), MULT
             )
 
-        def quantize_late(part):
-            if part == 0:
-                dz_codes[1, 1] = placed([P, SLOTS], U32, "dz_codes11", 110)
-                dz_scales[1, 1] = keep.tile([P, SLOTS], U8, name="dz_scales11", align_bytes=64)
-            slots = part_of(part)
-            nc.vector.quantize_mx(out=dz_codes[1, 1][:, slots].bitcast(E5M2), scales=dz_scales[1, 1][:, slots], in_=late_bf[part][:])
+        def quantize_dz(g, e, pieces):
+            dz_codes[g, e] = placed([P, SLOTS], U32, "dz_codes%d%d" % (g, e), DZ_CODES_KIB[g, e])
+            dz_scales[g, e] = keep.tile([P, SLOTS], U8, name="dz_scales%d%d" % (g, e), align_bytes=64)
+            for slots, tile in pieces:
+                nc.vector.quantize_mx(out=dz_codes[g, e][:, slots].bitcast(E5M2), scales=dz_scales[g, e][:, slots], in_=tile[:])
+
+        def quantize_whole(g, e):
+            quantize_dz(g, e, [(slice(0, SLOTS), dz_woven[g, e])])
 
         stage = {}
-        w_bf = {}
+        w_woven = {}
         w_codes = {}
         w_scales = {}
 
-        def load_w(i):
-            e, n = PIECES[i]
-            stage[i] = loaded([P, PASSES, PACK, W_COLS], "stage%d" % i)
+        def load_w(e, piece):
+            name = "w%d%d" % (e, piece)
+            stage[e, piece] = placed([P, PASSES, PACK, PIECE_TILES * P], F32, name, LOAD_KIB[name])
             for g in range(PASSES):
-                rows = wm[e][g * K_PASS : (g + 1) * K_PASS, n * W_COLS : (n + 1) * W_COLS]
-                nc.sync.dma_start(stage[i][:, g], rows.rearrange("(p t) d -> p t d", t=PACK))
+                rows = wm[e][g * K_PASS : (g + 1) * K_PASS, piece * PIECE_TILES * P : (piece + 1) * PIECE_TILES * P]
+                nc.sync.dma_start(stage[e, piece][:, g], rows.rearrange("(p t) d -> p t d", t=PACK))
 
-        def interleave_w(i, first, count, copy, kib):
-            w_bf[i, first] = placed([P, PASSES * count * P * PACK], BF16, "w_bf%d%d" % (i, first), kib)
+        def staged(e, m):
+            piece, k = divmod(m, PIECE_TILES)
+            return stage[e, piece][:, :, :, k * P : (k + 1) * P]
+
+        def woven_tile(units):
+            w_woven[units] = placed([P, len(units) * TILE_WORDS * PACK], BF16, "w_woven%d%d" % units[0], W_WOVEN_KIB[units[0]])
+            return w_woven[units]
+
+        def weave_w(unit, copy):
             copy(
-                w_bf[i, first][:].rearrange("p (g c i t) -> p g c t i", g=PASSES, i=RUN, t=PACK),
-                stage[i][:, :, :, first * P : (first + count) * P].rearrange("p g t (c i) -> p g c t i", i=RUN),
+                woven_tile((unit,))[:].rearrange("p (g c i t) -> p g c t i", g=PASSES, i=RUN, t=PACK),
+                staged(*unit).rearrange("p g t (c i) -> p g c t i", i=RUN),
             )
 
-        def quantize_w(i, first, count, kib):
-            e, n = PIECES[i]
-            codes = placed([P, PASSES * count * P], U32, "w_codes%d%d" % (i, first), kib)
-            scales = keep.tile([P, PASSES * count * P], U8, name="w_scales%d%d" % (i, first), align_bytes=64)
-            nc.vector.quantize_mx(out=codes[:].bitcast(E4M3), scales=scales[:], in_=w_bf[i, first][:])
-            for g in range(PASSES):
-                for k in range(count):
-                    cols = slice((g * count + k) * P, (g * count + k + 1) * P)
-                    w_codes[e, 2 * n + first + k, g] = codes[:, cols]
-                    w_scales[e, 2 * n + first + k, g] = scales[:, cols]
+        def weave_on_gpsimd(*units):
+            tile = woven_tile(units)
+            for k, unit in enumerate(units):
+                for g in range(PASSES):
+                    start = (k * PASSES + g) * P * PACK
+                    nc.gpsimd.tensor_copy(
+                        tile[:, start : start + P * PACK].rearrange("p (c t) -> p c t", t=PACK),
+                        staged(*unit)[:, g].rearrange("p t c -> p c t"),
+                    )
 
-        def interleave_on_gpsimd(place, i, m):
-            for g in range(PASSES):
-                nc.gpsimd.tensor_copy(
-                    place[:, g * P * PACK : (g + 1) * P * PACK].rearrange("p (c t) -> p c t", t=PACK),
-                    stage[i][:, g, :, m * P : (m + 1) * P].rearrange("p t c -> p c t"),
-                )
-
-        def quantize_tiles(rounded, units, kib):
-            name = "".join("%d%d" % unit for unit in units)
-            codes = placed([P, len(units) * PASSES * P], U32, "w_codes_" + name, kib)
-            scales = keep.tile([P, len(units) * PASSES * P], U8, name="w_scales_" + name, align_bytes=64)
-            nc.vector.quantize_mx(out=codes[:].bitcast(E4M3), scales=scales[:], in_=rounded[:])
+        def quantize_w(*units):
+            codes = placed([P, len(units) * TILE_WORDS], U32, "w_codes%d%d" % units[0], W_CODES_KIB[units[0]])
+            scales = keep.tile([P, len(units) * TILE_WORDS], U8, name="w_scales%d%d" % units[0], align_bytes=64)
+            nc.vector.quantize_mx(out=codes[:].bitcast(E4M3), scales=scales[:], in_=w_woven[units][:])
             for k, (e, m) in enumerate(units):
                 for g in range(PASSES):
                     cols = slice((k * PASSES + g) * P, (k * PASSES + g + 1) * P)
@@ -235,10 +271,10 @@ def tile_attend_gex_tnh_x_kernel(tc, dyT, hT, ts, wm, offs, out):
                     w_scales[e, m, g] = scales[:, cols]
 
         acc = {}
-        dx = {}
+        sums = {}
 
         def multiply(e, m, slots=slice(0, SLOTS)):
-            acc[e, m] = psum.tile([P, slots.stop - slots.start], F32, name="acc", tag="bank", bufs=8)
+            acc[e, m] = bank([P, slots.stop - slots.start], "acc")
             for g in range(PASSES):
                 nc.tensor.matmul_mx(
                     out=acc[e, m][:],
@@ -250,86 +286,85 @@ def tile_attend_gex_tnh_x_kernel(tc, dyT, hT, ts, wm, offs, out):
                     stop=(g == PASSES - 1),
                 )
 
-        def on_vector(e, m):
-            nc.vector.tensor_copy(windows[m][:].indirect(slots_of(e)), dx[e, m][:])
+        def drain(e, m, copy):
+            sums[e, m] = placed([P, SLOTS], F32, "sums%d%d" % (e, m), SUMS_KIB[e, m])
+            copy(sums[e, m][:], acc[e, m][:])
 
-        def drain(e, m, copy, kib):
-            dx[e, m] = placed([P, SLOTS], F32, "dx%d%d" % (e, m), kib)
-            copy(dx[e, m][:], acc[e, m][:])
-
-        def on_scalar(*units):
+        def scatter_on_scalar(*units):
             for part in range(2):
-                slots = part_of(part)
                 for e, m in units:
-                    nc.scalar.activation(windows[m][:].indirect(slots_of(e, slots.start, slots.stop)), dx[e, m][:, slots], COPY)
+                    nc.scalar.activation(windows[m][:].indirect(slots_of(e, half(part))), sums[e, m][:, half(part)], COPY)
 
         def store(m):
             nc.sync.dma_start(out[m * P : (m + 1) * P, :], windows[m][:])
 
+        def finish_on_vector(m):
+            nc.vector.tensor_copy(windows[m][:].indirect(slots_of(1)), sums[1, m][:])
+            store(m)
+
         for j in range(LEAD):
+            square(j)
             weigh(j)
         for j in range(PLANES):
             if j + LEAD < PLANES:
-                weigh(j + LEAD)
+                square(j + LEAD)
             gather_dy(j)
-            if j in (PACK, PACK + 1):
-                interleave_first(j - PACK)
-            if j in (PACK + 1, PACK + 2):
-                quantize_dz(0, j - PACK - 1)
-        for i in range(len(PIECES)):
-            load_w(i)
-        interleave_second()
-        interleave_w(0, 1, 1, nc.scalar.copy, 98.5)
-        interleave_w(0, 0, 1, nc.scalar.copy, 110)
-        finish_late(0)
-        quantize_dz(1, 0)
-        quantize_w(0, 1, 1, 68)
-        dx[0, 1] = placed([P, SLOTS], F32, "dx01", 80)
-        for part in range(2):
-            multiply(0, 1, part_of(part))
-            nc.scalar.copy(dx[0, 1][:, part_of(part)], acc[0, 1][:])
-        on_scalar((0, 1))
-        finish_late(1)
-        interleave_w(1, 0, 1, nc.vector.tensor_copy, 97.5)
-        quantize_w(0, 0, 1, 69)
-        multiply(0, 0)
-        quantize_w(1, 0, 1, 66)
-        multiply(0, 2)
-        quantize_late(0)
-        quantize_late(1)
-        interleave_w(2, 1, 1, nc.vector.tensor_copy, 95.5)
-        interleave_w(2, 0, 1, nc.vector.tensor_copy, 99.5)
-        quantize_w(2, 1, 1, 84)
-        multiply(1, 1)
-        quantize_w(2, 0, 1, 85)
-        multiply(1, 0)
-        drain(0, 0, nc.vector.tensor_copy, 94.5)
-        drain(0, 2, nc.scalar.copy, 98)
-        on_scalar((0, 0), (0, 2))
-        last = D_TILES - 1
-        tile_words = PASSES * P * PACK
-        for_scalar = placed([P, 2 * tile_words], BF16, "w_bf_last", 100.5)
-        interleave_on_gpsimd(for_scalar[:, 0:tile_words], 1, 1)
-        interleave_on_gpsimd(for_scalar[:, tile_words : 2 * tile_words], 3, 1)
-        for_vector = placed([P, tile_words], BF16, "w_bf_third", 85)
-        interleave_on_gpsimd(for_vector[:], 3, 0)
-        drain(1, 1, nc.vector.tensor_copy, 60)
-        on_vector(1, 1)
-        store(1)
-        quantize_tiles(for_scalar, ((0, last), (1, last)), 70)
-        multiply(0, last)
-        multiply(1, last)
-        drain(1, 0, nc.vector.tensor_copy, -4)
-        quantize_tiles(for_vector, ((1, 2),), 67)
-        multiply(1, 2)
-        on_vector(1, 0)
-        store(0)
-        drain(1, 2, nc.vector.tensor_copy, 62)
-        on_vector(1, 2)
-        store(2)
-        both = placed([P, LISTED], F32, "dx_last", 100.5)
+            if j + LEAD < PLANES:
+                weigh(j + LEAD)
+            if PACK <= j < PACK + EXPERTS:
+                weave_first(j - PACK)
+            if PACK < j <= PACK + EXPERTS:
+                quantize_whole(0, j - PACK - 1)
         for e in range(EXPERTS):
-            nc.scalar.copy(both[:, half(e)], acc[e, last][:])
-        for start, stop in ((0, 384), (384, 768), (768, LISTED)):
-            nc.scalar.activation(windows[last][:].indirect(offsets[:, start // 16 : stop // 16]), both[:, start:stop], COPY)
-        store(last)
+            for piece in range(D_TILES // PIECE_TILES):
+                load_w(e, piece)
+
+        weave_second()
+        weave_w((0, 1), nc.scalar.copy)
+        weave_w((0, 0), nc.scalar.copy)
+        weave_late(0)
+        quantize_whole(1, 0)
+        quantize_w((0, 1))
+        sums[0, 1] = placed([P, SLOTS], F32, "sums01", SUMS_KIB[0, 1])
+        for part in range(2):
+            multiply(0, 1, half(part))
+            nc.scalar.copy(sums[0, 1][:, half(part)], acc[0, 1][:])
+        scatter_on_scalar((0, 1))
+
+        weave_late(1)
+        weave_w((0, 2), nc.vector.tensor_copy)
+        for m in (0, 2):
+            quantize_w((0, m))
+            multiply(0, m)
+        quantize_dz(1, 1, [(half(part), late_woven[part]) for part in range(2)])
+        for m in (1, 0):
+            weave_w((1, m), nc.vector.tensor_copy)
+        for m in (1, 0):
+            quantize_w((1, m))
+            multiply(1, m)
+        drain(0, 0, nc.vector.tensor_copy)
+        drain(0, 2, nc.scalar.copy)
+        scatter_on_scalar((0, 0), (0, 2))
+
+        last_units = tuple((e, LAST_TILE) for e in range(EXPERTS))
+        weave_on_gpsimd(*last_units)
+        weave_on_gpsimd((1, 2))
+        drain(1, 1, nc.vector.tensor_copy)
+        finish_on_vector(1)
+        quantize_w(*last_units)
+        for unit in last_units:
+            multiply(*unit)
+        drain(1, 0, nc.vector.tensor_copy)
+        quantize_w((1, 2))
+        multiply(1, 2)
+        finish_on_vector(0)
+        drain(1, 2, nc.vector.tensor_copy)
+        finish_on_vector(2)
+
+        both = placed([P, LISTED], F32, "sums_last", SUMS_KIB[0, LAST_TILE])
+        for e in range(EXPERTS):
+            nc.scalar.copy(both[:, expert(e)], acc[e, LAST_TILE][:])
+        for start in range(0, LISTED, LONG_SCATTER):
+            stop = min(start + LONG_SCATTER, LISTED)
+            nc.scalar.activation(windows[LAST_TILE][:].indirect(entries(start, stop)), both[:, start:stop], COPY)
+        store(LAST_TILE)

@@ -31,7 +31,7 @@ HALF = SLOTS // 2
 BANKS = 8
 RUN = 4
 LEAD = 2
-H_ON_VECTOR = 1
+H_SHARED = 2
 TS_ROW = P - 1
 PIECE_TILES = 2
 TILE_WORDS = PASSES * P
@@ -46,8 +46,9 @@ LOAD_KIB = {
     "w10": 4, "w11": 12,
 }
 DISTANCE_KIB = 67
-TS_LISTED_KIB = 66
+TS_LISTED_KIB = (68, 66)
 TS_ALL_KIB = 96
+MINUS_ONE_KIB = 71
 SQUARES_KIB = (100, 68, 72)
 DZ_CODES_KIB = {(0, 0): 88, (0, 1): 90, (1, 0): 92, (1, 1): 126}
 DZ_SECOND_KIB = 120
@@ -59,9 +60,9 @@ W_WOVEN_KIB = {
     (1, 1): LATE_WOVEN_KIB[0],
     (1, 0): LATE_WOVEN_KIB[1],
     (0, LAST_TILE): 27,
-    (1, 2): 101,
+    (1, LAST_TILE): 101,
 }
-W_CODES_KIB = {(0, 2): 82, (1, 2): 83, (0, 1): 84, (0, 0): 85, (0, LAST_TILE): 86, (1, 1): 100, (1, 0): 101}
+W_CODES_KIB = {(0, 2): 82, (1, LAST_TILE): 83, (0, 1): 84, (0, 0): 85, (0, LAST_TILE): 86, (1, 1): 100, (1, 0): 101}
 SUMS_KIB = {
     (0, 1): 96,
     (0, 0): 21,
@@ -127,18 +128,19 @@ def tile_attend_gex_tnh_x_kernel(tc, dyT, hT, ts, wm, offs, out):
         windows = [keep.tile([P, TOKENS], F32, name="out%d" % m) for m in range(D_TILES)]
         for window in windows:
             nc.gpsimd.memset(window[:], 0.0)
-        ts_listed = placed([P, LISTED], F32, "ts_listed", TS_LISTED_KIB)
+        ts_listed = [placed([P, SLOTS], F32, "ts_listed%d" % e, TS_LISTED_KIB[e]) for e in range(EXPERTS)]
         minus_ts_col = keep.tile([P, EXPERTS * BLOCKS], F32, name="minus_ts_col")
-        nc.vector.tensor_copy(ts_listed[:, expert(0)], ts_all[:].indirect(slots_of(0)))
-        nc.scalar.activation(ts_listed[:, expert(1)], ts_all[:].indirect(slots_of(1)), COPY)
+        nc.vector.tensor_copy(ts_listed[0][:], ts_all[:].indirect(slots_of(0)))
+        nc.scalar.activation(ts_listed[1][:], ts_all[:].indirect(slots_of(1)), COPY)
 
+        minus_one = placed([P, 1], F32, "minus_one", MINUS_ONE_KIB)
+        nc.vector.memset(minus_one[:], -1.0)
         minus_ts = []
         for e in range(EXPERTS):
             turned = bank([P, BLOCKS, P], "turned")
             for b in range(BLOCKS):
-                c = e * SLOTS + b * P
-                nc.tensor.transpose(turned[:, b, :], ts_listed[:, c : c + P], identity[:])
-            nc.vector.tensor_scalar(minus_ts_col[:, e * BLOCKS : (e + 1) * BLOCKS], turned[:, :, TS_ROW], -1.0, None, MULT)
+                nc.tensor.transpose(turned[:, b, :], ts_listed[e][:, b * P : (b + 1) * P], identity[:])
+            nc.vector.tensor_scalar(minus_ts_col[:, e * BLOCKS : (e + 1) * BLOCKS], turned[:, :, TS_ROW], minus_one[:], None, MULT)
             spread = bank([P, SLOTS], "minus_ts%d" % e)
             for b in range(BLOCKS):
                 c = e * BLOCKS + b
@@ -165,7 +167,7 @@ def tile_attend_gex_tnh_x_kernel(tc, dyT, hT, ts, wm, offs, out):
             h = load_plane(hT, "h%d" % j, j)
             squares = placed([P, LISTED], F32, "squares%d" % j, SQUARES_KIB[j % len(SQUARES_KIB)])
             for e in range(EXPERTS):
-                if j == H_ON_VECTOR:
+                if j < H_SHARED and e == 1:
                     nc.vector.tensor_copy(squares[:, expert(e)], h[:].indirect(slots_of(e)))
                 else:
                     nc.scalar.activation(squares[:, expert(e)], h[:].indirect(slots_of(e)), COPY)
@@ -295,8 +297,8 @@ def tile_attend_gex_tnh_x_kernel(tc, dyT, hT, ts, wm, offs, out):
                 for e, m in units:
                     nc.scalar.activation(windows[m][:].indirect(slots_of(e, half(part))), sums[e, m][:, half(part)], COPY)
 
-        def store(m):
-            nc.sync.dma_start(out[m * P : (m + 1) * P, :], windows[m][:])
+        def store(m, queue=nc.sync):
+            queue.dma_start(out[m * P : (m + 1) * P, :], windows[m][:])
 
         def finish_on_vector(m):
             nc.vector.tensor_copy(windows[m][:].indirect(slots_of(1)), sums[1, m][:])
@@ -346,25 +348,30 @@ def tile_attend_gex_tnh_x_kernel(tc, dyT, hT, ts, wm, offs, out):
         drain(0, 2, nc.scalar.copy)
         scatter_on_scalar((0, 0), (0, 2))
 
-        last_units = tuple((e, LAST_TILE) for e in range(EXPERTS))
-        weave_on_gpsimd(*last_units)
-        weave_on_gpsimd((1, 2))
+        weave_on_gpsimd((0, LAST_TILE), (1, 2))
+        weave_on_gpsimd((1, LAST_TILE))
         drain(1, 1, nc.vector.tensor_copy)
         finish_on_vector(1)
-        quantize_w(*last_units)
-        for unit in last_units:
-            multiply(*unit)
+        quantize_w((0, LAST_TILE), (1, 2))
+        multiply(0, LAST_TILE)
+        halves = []
+        for part in range(2):
+            multiply(1, 2, half(part))
+            halves.append(acc[1, 2])
         drain(1, 0, nc.vector.tensor_copy)
-        quantize_w((1, 2))
-        multiply(1, 2)
+        quantize_w((1, LAST_TILE))
+        multiply(1, LAST_TILE)
         finish_on_vector(0)
-        drain(1, 2, nc.vector.tensor_copy)
+        first = placed([P, SLOTS], F32, "sums12", SUMS_KIB[1, 2])
+        sums[1, 2] = first
+        nc.scalar.copy(first[:, half(0)], halves[0][:])
+        nc.vector.tensor_copy(first[:, half(1)], halves[1][:])
         finish_on_vector(2)
 
         both = placed([P, LISTED], F32, "sums_last", SUMS_KIB[0, LAST_TILE])
         for e in range(EXPERTS):
-            nc.scalar.copy(both[:, expert(e)], acc[e, LAST_TILE][:])
-        for start in range(0, LISTED, LONG_SCATTER):
-            stop = min(start + LONG_SCATTER, LISTED)
+            for part in range(2):
+                nc.scalar.copy(both[:, expert(e)][:, half(part)], acc[e, LAST_TILE][:, half(part)])
+        for start, stop in ((0, HALF), (HALF, HALF + LONG_SCATTER), (HALF + LONG_SCATTER, LISTED)):
             nc.scalar.activation(windows[LAST_TILE][:].indirect(entries(start, stop)), both[:, start:stop], COPY)
-        store(LAST_TILE)
+        store(LAST_TILE, nc.scalar)

from contextlib import ExitStack

import concourse.mybir as mybir

EXPERTS, SLOTS, TOKENS, D_IN, D_OUT = 2, 512, 2048, 512, 1024
FLOPS = 2 * EXPERTS * SLOTS * D_IN * D_OUT

F32 = mybir.dt.float32
BF16 = mybir.dt.bfloat16
U32 = mybir.dt.uint32
U16 = mybir.dt.uint16
U8 = mybir.dt.uint8
E4M3 = mybir.dt.float8_e4m3fn_x4
E5M2 = mybir.dt.float8_e5m2_x4
MULT = mybir.AluOpType.mult
ADD = mybir.AluOpType.add
COPY = mybir.ActivationFunctionType.Copy
RELU = mybir.ActivationFunctionType.Relu
SQUARE = mybir.ActivationFunctionType.Square

P = 128
PACK = 4
K_PASS = P * PACK
PASSES = D_OUT // K_PASS
PLANES = PASSES * PACK
LISTED = EXPERTS * SLOTS
BLOCKS = SLOTS // P
D_TILES = D_IN // P
LAST_TILE = D_TILES - 1
HALF = SLOTS // 2
BANKS = 8
RUN = 4
LEAD = 2
H_SHARED = 2
TS_ROW = P - 1
PIECE_TILES = 2
TILE_WORDS = PASSES * P
LONG_SCATTER = 384
KIB = 1024

LOAD_KIB = {
    "h0": 8, "h1": 16, "h2": 24, "dy0": 32, "h3": 40, "dy1": 48, "h4": 56, "dy2": 0,
    "h5": 8, "dy3": 16, "h6": 24, "dy4": 40, "h7": 56, "dy5": 8,
    "dy6": 28, "dy7": 20,
    "w00": 36, "w01": 44,
    "w10": 4, "w11": 12,
}
DISTANCE_KIB = 67
TS_LISTED_KIB = (68, 66)
TS_ALL_KIB = 96
MINUS_ONE_KIB = 71
SQUARES_KIB = (100, 68, 72)
DZ_CODES_KIB = {(0, 0): 88, (0, 1): 90, (1, 0): 92, (1, 1): 126}
DZ_SECOND_KIB = 120
LATE_WOVEN_KIB = (20, 26)
W_WOVEN_KIB = {
    (0, 1): 25,
    (0, 0): 126,
    (0, 2): 24,
    (1, 1): LATE_WOVEN_KIB[0],
    (1, 0): LATE_WOVEN_KIB[1],
    (0, LAST_TILE): 27,
    (1, LAST_TILE): 101,
}
W_CODES_KIB = {(0, 2): 82, (1, LAST_TILE): 83, (0, 1): 84, (0, 0): 85, (0, LAST_TILE): 86, (1, 1): 100, (1, 0): 101}
SUMS_KIB = {
    (0, 1): 96,
    (0, 0): 21,
    (0, 2): 24.5,
    (1, 1): 76,
    (1, 0): LOAD_KIB["w11"],
    (1, 2): 78,
    (0, LAST_TILE): W_WOVEN_KIB[0, LAST_TILE],
}


def tile_attend_gex_tnh_x_kernel(tc, dyT, hT, ts, wm, offs, out):
    nc = tc.nc

    with ExitStack() as ctx:
        keep = ctx.enter_context(tc.tile_pool(name="keep", bufs=1))
        big = ctx.enter_context(tc.tile_pool(name="big", bufs=1))
        psum = ctx.enter_context(tc.psum_pool(name="psum", bufs=1))

        offsets = keep.tile([P, LISTED // 16], U16, name="offsets")
        nc.sync.dma_start(offsets[:], offs)

        def entries(start, stop):
            return offsets[:, start // 16 : stop // 16]

        def slots_of(e, slots=slice(0, SLOTS)):
            return entries(e * SLOTS + slots.start, e * SLOTS + slots.stop)

        def expert(e):
            return slice(e * SLOTS, (e + 1) * SLOTS)

        def half(part):
            return slice(part * HALF, (part + 1) * HALF)

        def placed(shape, dtype, name, kib):
            return big.tile(shape, dtype, name=name, align_bytes=64, offset=int(kib * KIB))

        def bank(shape, name):
            return psum.tile(shape, F32, name=name, tag="bank", bufs=BANKS)

        def load_plane(x, name, j):
            g, t = divmod(j, PACK)
            plane = placed([P, TOKENS], F32, name, LOAD_KIB[name])
            nc.sync.dma_start(plane[:], x[g * K_PASS : (g + 1) * K_PASS, :].rearrange("(p t) c -> p t c", t=PACK)[:, t, :])
            return plane

        def in_runs(planes):
            return planes.rearrange("p t (c i) -> p c t i", i=RUN)

        def woven(words):
            return words.rearrange("p (c i t) -> p c t i", i=RUN, t=PACK)

        identity = keep.tile([P, P], F32, name="identity")
        distance = placed([P, P], F32, "distance", DISTANCE_KIB)
        nc.gpsimd.iota(distance[:], [[-1, P]], base=0, channel_multiplier=1, allow_small_or_imprecise_dtypes=True)
        nc.scalar.activation(distance[:], distance[:], SQUARE)
        nc.scalar.activation(identity[:], distance[:], RELU, bias=1.0, scale=-1.0)

        ts_all = placed([P, TOKENS], F32, "ts_all", TS_ALL_KIB)
        nc.sync.dma_start(ts_all[TS_ROW : TS_ROW + 1, :], ts[TS_ROW : TS_ROW + 1, :])
        nc.vector.memset(ts_all[0:TS_ROW, 0 : TOKENS - 1], 0.0)
        nc.vector.memset(ts_all[0:TS_ROW, TOKENS - 1 : TOKENS], 0.0)
        windows = [keep.tile([P, TOKENS], F32, name="out%d" % m) for m in range(D_TILES)]
        for window in windows:
            nc.gpsimd.memset(window[:], 0.0)
        ts_listed = [placed([P, SLOTS], F32, "ts_listed%d" % e, TS_LISTED_KIB[e]) for e in range(EXPERTS)]
        minus_ts_col = keep.tile([P, EXPERTS * BLOCKS], F32, name="minus_ts_col")
        nc.vector.tensor_copy(ts_listed[0][:], ts_all[:].indirect(slots_of(0)))
        nc.scalar.activation(ts_listed[1][:], ts_all[:].indirect(slots_of(1)), COPY)

        minus_one = placed([P, 1], F32, "minus_one", MINUS_ONE_KIB)
        nc.vector.memset(minus_one[:], -1.0)
        minus_ts = []
        for e in range(EXPERTS):
            turned = bank([P, BLOCKS, P], "turned")
            for b in range(BLOCKS):
                nc.tensor.transpose(turned[:, b, :], ts_listed[e][:, b * P : (b + 1) * P], identity[:])
            nc.vector.tensor_scalar(minus_ts_col[:, e * BLOCKS : (e + 1) * BLOCKS], turned[:, :, TS_ROW], minus_one[:], None, MULT)
            spread = bank([P, SLOTS], "minus_ts%d" % e)
            for b in range(BLOCKS):
                c = e * BLOCKS + b
                nc.tensor.transpose(spread[:, b * P : (b + 1) * P], minus_ts_col[:, c : c + 1].to_broadcast([P, P]), identity[:])
            minus_ts.append(spread)

        factors = keep.tile([P, PACK * LISTED], F32, name="factors")
        late_factor = factors[:].rearrange("p (t s) -> p t s", t=PACK)[:, :, expert(1)]
        late_dy = keep.tile([P, PACK, SLOTS], F32, name="late_dy")

        def factor_of(j, e):
            g, t = divmod(j, PACK)
            if e == 1:
                start = (t if g == 1 else t % 2) * LISTED + SLOTS
            elif j % 2 == 0:
                start = 0
            else:
                start = (PACK - 1) * LISTED + (0 if j == PLANES - 1 else HALF)
            return factors[:, start : start + SLOTS]

        squared = {}

        def square(j):
            h = load_plane(hT, "h%d" % j, j)
            squares = placed([P, LISTED], F32, "squares%d" % j, SQUARES_KIB[j % len(SQUARES_KIB)])
            for e in range(EXPERTS):
                if j < H_SHARED and e == 1:
                    nc.vector.tensor_copy(squares[:, expert(e)], h[:].indirect(slots_of(e)))
                else:
                    nc.scalar.activation(squares[:, expert(e)], h[:].indirect(slots_of(e)), COPY)
            for e in range(EXPERTS):
                nc.scalar.activation(squares[:, expert(e)], squares[:, expert(e)], SQUARE)
            squared[j] = squares

        def weigh(j):
            for e in range(EXPERTS):
                nc.vector.scalar_tensor_tensor(factor_of(j, e), squared[j][:, expert(e)], -1.0, minus_ts[e][:], ADD, MULT)

        dz_first = keep.tile([P, PACK, LISTED], F32, name="dz_first")
        dz_second = placed([P, PACK, SLOTS], F32, "dz_second", DZ_SECOND_KIB)

        def gather_dy(j):
            g, t = divmod(j, PACK)
            dy = load_plane(dyT, "dy%d" % j, j)
            if g == 0 and j % 2 == 0:
                nc.vector.tensor_tensor(dz_first[:, t, :], dy[:].indirect(offsets[:]), factors[:, 0:LISTED], MULT)
            elif g == 0:
                for e in range(EXPERTS):
                    nc.vector.tensor_tensor(dz_first[:, t, expert(e)], dy[:].indirect(slots_of(e)), factor_of(j, e), MULT)
            else:
                runs = [half(0), half(1)] if j == PLANES - 1 else [expert(0)]
                for slots in runs:
                    nc.vector.tensor_tensor(dz_second[:, t, slots], dy[:].indirect(slots_of(0, slots)), factor_of(j, 0)[:, slots], MULT)
                nc.scalar.activation(late_dy[:, t, :], dy[:].indirect(slots_of(1)), COPY)

        dz_woven = {}
        dz_codes = {}
        dz_scales = {}
        late_woven = {}

        def weave_first(e):
            dz_woven[0, e] = keep.tile([P, SLOTS * PACK], BF16, name="dz_woven0%d" % e, align_bytes=64)
            nc.vector.tensor_copy(woven(dz_woven[0, e][:]), in_runs(dz_first[:, :, expert(e)]))

        def weave_second():
            dz_woven[1, 0] = keep.tile([P, SLOTS * PACK], BF16, name="dz_woven10", align_bytes=64)
            for part, copy in enumerate((nc.scalar.copy, nc.vector.tensor_copy)):
                words = dz_woven[1, 0][:, part * HALF * PACK : (part + 1) * HALF * PACK]
                copy(woven(words), in_runs(dz_second[:, :, half(part)]))

        def weave_late(part):
            late_woven[part] = placed([P, HALF * PACK], BF16, "late_woven%d" % part, LATE_WOVEN_KIB[part])
            nc.vector.tensor_tensor(
                woven(late_woven[part][:]), in_runs(late_dy[:, :, half(part)]), in_runs(late_factor[:, :, half(part)]), MULT
            )

        def quantize_dz(g, e, pieces):
            dz_codes[g, e] = placed([P, SLOTS], U32, "dz_codes%d%d" % (g, e), DZ_CODES_KIB[g, e])
            dz_scales[g, e] = keep.tile([P, SLOTS], U8, name="dz_scales%d%d" % (g, e), align_bytes=64)
            for slots, tile in pieces:
                nc.vector.quantize_mx(out=dz_codes[g, e][:, slots].bitcast(E5M2), scales=dz_scales[g, e][:, slots], in_=tile[:])

        def quantize_whole(g, e):
            quantize_dz(g, e, [(slice(0, SLOTS), dz_woven[g, e])])

        stage = {}
        w_woven = {}
        w_codes = {}
        w_scales = {}

        def load_w(e, piece):
            name = "w%d%d" % (e, piece)
            stage[e, piece] = placed([P, PASSES, PACK, PIECE_TILES * P], F32, name, LOAD_KIB[name])
            for g in range(PASSES):
                rows = wm[e][g * K_PASS : (g + 1) * K_PASS, piece * PIECE_TILES * P : (piece + 1) * PIECE_TILES * P]
                nc.sync.dma_start(stage[e, piece][:, g], rows.rearrange("(p t) d -> p t d", t=PACK))

        def staged(e, m):
            piece, k = divmod(m, PIECE_TILES)
            return stage[e, piece][:, :, :, k * P : (k + 1) * P]

        def woven_tile(units):
            w_woven[units] = placed([P, len(units) * TILE_WORDS * PACK], BF16, "w_woven%d%d" % units[0], W_WOVEN_KIB[units[0]])
            return w_woven[units]

        def weave_w(unit, copy):
            copy(
                woven_tile((unit,))[:].rearrange("p (g c i t) -> p g c t i", g=PASSES, i=RUN, t=PACK),
                staged(*unit).rearrange("p g t (c i) -> p g c t i", i=RUN),
            )

        def weave_on_gpsimd(*units):
            tile = woven_tile(units)
            for k, unit in enumerate(units):
                for g in range(PASSES):
                    start = (k * PASSES + g) * P * PACK
                    nc.gpsimd.tensor_copy(
                        tile[:, start : start + P * PACK].rearrange("p (c t) -> p c t", t=PACK),
                        staged(*unit)[:, g].rearrange("p t c -> p c t"),
                    )

        def quantize_w(*units):
            codes = placed([P, len(units) * TILE_WORDS], U32, "w_codes%d%d" % units[0], W_CODES_KIB[units[0]])
            scales = keep.tile([P, len(units) * TILE_WORDS], U8, name="w_scales%d%d" % units[0], align_bytes=64)
            nc.vector.quantize_mx(out=codes[:].bitcast(E4M3), scales=scales[:], in_=w_woven[units][:])
            for k, (e, m) in enumerate(units):
                for g in range(PASSES):
                    cols = slice((k * PASSES + g) * P, (k * PASSES + g + 1) * P)
                    w_codes[e, m, g] = codes[:, cols]
                    w_scales[e, m, g] = scales[:, cols]

        acc = {}
        sums = {}

        def multiply(e, m, slots=slice(0, SLOTS)):
            acc[e, m] = bank([P, slots.stop - slots.start], "acc")
            for g in range(PASSES):
                nc.tensor.matmul_mx(
                    out=acc[e, m][:],
                    lhsT=w_codes[e, m, g].bitcast(E4M3),
                    lhsT_scale=w_scales[e, m, g],
                    rhs=dz_codes[g, e][:, slots].bitcast(E5M2),
                    rhs_scale=dz_scales[g, e][:, slots],
                    start=(g == 0),
                    stop=(g == PASSES - 1),
                )

        def drain(e, m, copy):
            sums[e, m] = placed([P, SLOTS], F32, "sums%d%d" % (e, m), SUMS_KIB[e, m])
            copy(sums[e, m][:], acc[e, m][:])

        def scatter_on_scalar(*units):
            for part in range(2):
                for e, m in units:
                    nc.scalar.activation(windows[m][:].indirect(slots_of(e, half(part))), sums[e, m][:, half(part)], COPY)

        def store(m, queue=nc.sync):
            queue.dma_start(out[m * P : (m + 1) * P, :], windows[m][:])

        def finish_on_vector(m):
            nc.vector.tensor_copy(windows[m][:].indirect(slots_of(1)), sums[1, m][:])
            store(m)

        for j in range(LEAD):
            square(j)
            weigh(j)
        for j in range(PLANES):
            if j + LEAD < PLANES:
                square(j + LEAD)
            gather_dy(j)
            if j + LEAD < PLANES:
                weigh(j + LEAD)
            if PACK <= j < PACK + EXPERTS:
                weave_first(j - PACK)
            if PACK < j <= PACK + EXPERTS:
                quantize_whole(0, j - PACK - 1)
        for e in range(EXPERTS):
            for piece in range(D_TILES // PIECE_TILES):
                load_w(e, piece)

        weave_second()
        weave_w((0, 1), nc.scalar.copy)
        weave_w((0, 0), nc.scalar.copy)
        weave_late(0)
        quantize_whole(1, 0)
        quantize_w((0, 1))
        sums[0, 1] = placed([P, SLOTS], F32, "sums01", SUMS_KIB[0, 1])
        for part in range(2):
            multiply(0, 1, half(part))
            nc.scalar.copy(sums[0, 1][:, half(part)], acc[0, 1][:])
        scatter_on_scalar((0, 1))

        weave_late(1)
        weave_w((0, 2), nc.vector.tensor_copy)
        for m in (0, 2):
            quantize_w((0, m))
            multiply(0, m)
        quantize_dz(1, 1, [(half(part), late_woven[part]) for part in range(2)])
        for m in (1, 0):
            weave_w((1, m), nc.vector.tensor_copy)
        for m in (1, 0):
            quantize_w((1, m))
            multiply(1, m)
        drain(0, 0, nc.vector.tensor_copy)
        drain(0, 2, nc.scalar.copy)
        scatter_on_scalar((0, 0), (0, 2))

        weave_on_gpsimd((0, LAST_TILE), (1, 2))
        weave_on_gpsimd((1, LAST_TILE))
        drain(1, 1, nc.vector.tensor_copy)
        finish_on_vector(1)
        quantize_w((0, LAST_TILE), (1, 2))
        multiply(0, LAST_TILE)
        halves = []
        for part in range(2):
            multiply(1, 2, half(part))
            halves.append(acc[1, 2])
        drain(1, 0, nc.vector.tensor_copy)
        quantize_w((1, LAST_TILE))
        multiply(1, LAST_TILE)
        finish_on_vector(0)
        first = placed([P, SLOTS], F32, "sums12", SUMS_KIB[1, 2])
        sums[1, 2] = first
        nc.scalar.copy(first[:, half(0)], halves[0][:])
        nc.vector.tensor_copy(first[:, half(1)], halves[1][:])
        finish_on_vector(2)

        both = placed([P, LISTED], F32, "sums_last", SUMS_KIB[0, LAST_TILE])
        for e in range(EXPERTS):
            for part in range(2):
                nc.scalar.copy(both[:, expert(e)][:, half(part)], acc[e, LAST_TILE][:, half(part)])
        for start, stop in ((0, HALF), (HALF, HALF + LONG_SCATTER), (HALF + LONG_SCATTER, LISTED)):
            nc.scalar.activation(windows[LAST_TILE][:].indirect(entries(start, stop)), both[:, start:stop], COPY)
        store(LAST_TILE, nc.scalar)
